import numpy as np
import ml_dtypes


def mxq(x, axis, fmt="e4m3"):
    dtype, down = {"e4m3": (ml_dtypes.float8_e4m3fn, 7), "e5m2": (ml_dtypes.float8_e5m2, 14)}[fmt]
    v = np.moveaxis(np.asarray(x, np.float32).astype(ml_dtypes.bfloat16).astype(np.float64), axis, -1)
    blocks = v.reshape(v.shape[:-1] + (-1, 32))
    amax = np.abs(blocks).max(-1, keepdims=True)
    byte = np.maximum(np.where(amax > 0, np.frexp(amax)[1] - 1 + 127, 0) - down, 1)
    scale = np.exp2(byte - 127.0)
    codes = (blocks / scale).astype(np.float32).astype(dtype).astype(np.float64)
    return np.moveaxis((codes * scale).reshape(v.shape), -1, axis)


WIDE = False


def mx_kscale(k):
    if not WIDE:
        return np.ones(k)
    levels = np.array([18, -18])
    if k % 512:
        return np.exp2(np.random.permutation(np.resize(levels, k // 32))).repeat(32)
    a = np.empty((k // 512, 16))
    for p in range(k // 512):
        a[p, :8] = np.random.permutation(np.resize(levels, 8))
        for g in range(8):
            far = levels[np.abs(levels - a[p, g]) >= 10]
            a[p, g + 8] = far[np.random.randint(len(far))]
    return np.exp2(a.ravel()).repeat(32)


def f64(x):
    return np.asarray(x).astype(np.float64)


def striped(idx):
    return np.tile(np.asarray(idx).reshape(-1, 16).T, (8, 1)).astype(np.uint16)


def unstriped(offs):
    return offs[:16].T.reshape(-1).astype(np.int64)

def planes(y):
    n, m = y.shape
    v = y.astype(np.float32).astype(ml_dtypes.bfloat16).astype(np.float64).reshape(n // 32, 32, m)
    top = np.abs(v).max(1)
    byte = np.clip(np.where(top > 0, np.frexp(top)[1] - 1 + 127 - 7, 1), 1, 254)
    codes = (v * np.exp2(127.0 - byte)[:, None, :]).reshape(n, m).astype(np.float32).astype(ml_dtypes.float8_e4m3fn).view(np.uint8)
    words = codes.reshape(n // 512, 128, 4, m).transpose(0, 1, 3, 2)
    return np.ascontiguousarray(words), np.ascontiguousarray(byte.astype(np.uint8).reshape(n // 512, 16, m))


def setup_inputs():
    n = np.random.standard_normal
    uni = np.random.uniform
    idx = np.random.permutation(1024)[:512]
    f_d = mx_kscale(512)
    f_k = mx_kscale(512)
    return {
        "dyT": (n((512, 1024)) * f_d[:, None]).astype(np.float32),
        "R": (n((512, 512)) / np.sqrt(512) / f_d[:, None]).astype(np.float32),
        "W": (n((512, 512)) / np.sqrt(512) * f_d[:, None] * f_k[None, :]).astype(np.float32),
        "ck": (uni(0.75, 1.3, (512, 1)) / f_k[:, None]).astype(np.float32),
        "offs": striped(idx),
    }


def reference(dyT, R, W, ck, offs):
    idx = unstriped(offs)
    dy = f64(dyT)[:, idx]
    u = mxq(f64(R), 0, "e4m3").T @ mxq(dy, 0, "e5m2")
    s = f64(ck) * u
    v = mxq(f64(W), 1, "e4m3") @ mxq(s, 0, "e5m2")
    nd = dy + v
    out_0 = f64(dyT)
    out_0[:, idx] = nd
    return (out_0,) + planes(out_0)

@@ -1,0 +1,184 @@
+from contextlib import ExitStack
+
+import concourse.mybir as mybir
+from concourse.masks import make_identity
+
+F32 = mybir.dt.float32
+BF16 = mybir.dt.bfloat16
+I32 = mybir.dt.int32
+U32 = mybir.dt.uint32
+U16 = mybir.dt.uint16
+U8 = mybir.dt.uint8
+E4M3 = mybir.dt.float8_e4m3fn_x4
+E5M2 = mybir.dt.float8_e5m2_x4
+COPY = mybir.ActivationFunctionType.Copy
+ADD = mybir.AluOpType.add
+MULT = mybir.AluOpType.mult
+
+P = 128
+LANES = 4
+D = 512
+K = 512
+SLOTS = 512
+TOKENS = 1024
+PER_COL = 16
+
+FLOPS = 2 * 2 * D * K * SLOTS
+
+
+def tile_attend_greft_pl_kernel(tc, dyT, R, W, ck, offs, out_0, out_1, out_2):
+    nc = tc.nc
+    with ExitStack() as ctx:
+        keep = ctx.enter_context(tc.tile_pool(name="keep", bufs=1))
+        psum = ctx.enter_context(tc.psum_pool(name="psum", bufs=1))
+
+        offsets = keep.tile([P, SLOTS // PER_COL], U16, name="offsets")
+        nc.sync.dma_start(offsets[:], offs)
+
+        dy_planes = dyT.rearrange("(p t) c -> p t c", t=LANES)
+        out_planes = out_0.rearrange("(p t) c -> p t c", t=LANES)
+        w_planes = W.rearrange("(m t) k -> m t k", t=LANES)
+        r_rows = R.rearrange("(p j) k -> p j k", j=LANES)
+        order = (2, 0, 1, 3)
+
+        source = [keep.tile([P, TOKENS], F32, name="source%d" % t) for t in range(LANES)]
+        for t in range(LANES):
+            nc.sync.dma_start(source[t][:], dy_planes[:, t, :])
+        r_raw = [keep.tile([P, LANES, K // 2], F32, name="r_raw%d" % h) for h in range(2)]
+        for h in range(2):
+            nc.sync.dma_start(r_raw[h][:], r_rows[:, :, h * K // 2:(h + 1) * K // 2])
+        ck_sb = keep.tile([P, LANES], F32, name="ck_sb")
+        nc.sync.dma_start(ck_sb[:], ck.rearrange("(p t) o -> p (t o)", t=LANES))
+        w_raw = [keep.tile([P, K], F32, name="w_raw%d" % t) for t in range(LANES)]
+        for t in order:
+            nc.sync.dma_start(w_raw[t][:], w_planes[:, t, :])
+        window = [keep.tile([P, TOKENS], F32, name="window%d" % t) for t in range(LANES)]
+        for t in order:
+            nc.sync.dma_start(window[t][:], dy_planes[:, t, :])
+
+        ident = keep.tile([P, P], F32, name="ident")
+        make_identity(nc, ident[:])
+
+        def slot_offsets(a, b):
+            return offsets[:, a // PER_COL:b // PER_COL]
+
+        def weave(copy, dst, src, a, b):
+            copy(out=dst[:, a:b, :].rearrange("p (c i) t -> p c t i", i=4),
+                 in_=src[:, :, a:b].rearrange("p t (c i) -> p c t i", i=4))
+
+        picked = keep.tile([P, LANES, SLOTS], F32, name="picked")
+        dy_grouped = keep.tile([P, SLOTS, LANES], BF16, name="dy_grouped", align_bytes=64)
+        dy_codes = keep.tile([P, SLOTS], U32, name="dy_codes", align_bytes=64)
+        dy_scales = keep.tile([P, SLOTS], U8, name="dy_scales", align_bytes=64)
+        r_grouped = keep.tile([P, LANES, P, LANES], BF16, name="r_grouped", align_bytes=64)
+        r_codes = keep.tile([P, LANES, P], U32, name="r_codes", align_bytes=64)
+        r_scales = keep.tile([P, LANES, P], U8, name="r_scales", align_bytes=64)
+
+        def deal_r(copy, a, b):
+            h, base = divmod(a, P // 2)
+            copy(out=r_grouped[:, :, a:b, :].rearrange("p t m j -> p m j t"),
+                 in_=r_raw[h][:].rearrange("p j (m t) -> p m j t", t=LANES)[:, base:base + b - a, :, :])
+
+        dy_split = 128
+        last = LANES - 1
+        for t in range(last):
+            nc.vector.tensor_copy(picked[:, t, :], source[t][:].indirect(offsets[:]))
+        nc.vector.tensor_copy(picked[:, last, 0:dy_split], source[last][:].indirect(slot_offsets(0, dy_split)))
+        weave(nc.scalar.copy, dy_grouped, picked, 0, dy_split)
+        nc.vector.tensor_copy(picked[:, last, dy_split:SLOTS], source[last][:].indirect(slot_offsets(dy_split, SLOTS)))
+        weave(nc.vector.tensor_copy, dy_grouped, picked, dy_split, SLOTS)
+        r_split = P - 24
+        deal_r(nc.scalar.copy, 0, P // 2)
+        deal_r(nc.scalar.copy, P // 2, r_split)
+        deal_r(nc.vector.tensor_copy, r_split, P)
+        nc.vector.quantize_mx(out=dy_codes[:].bitcast(E5M2), scales=dy_scales[:],
+                              in_=dy_grouped[:].rearrange("p c t -> p (c t)"))
+
+        u_bank = [psum.tile([P, SLOTS], F32, name="u_bank%d" % t, tag="bank%d" % t) for t in range(LANES)]
+        for t in range(LANES):
+            nc.vector.quantize_mx(out=r_codes[:, t, :].bitcast(E4M3), scales=r_scales[:, t, :],
+                                  in_=r_grouped[:, t, :, :].rearrange("p m j -> p (m j)"))
+            nc.tensor.matmul_mx(out=u_bank[t][:], lhsT=r_codes[:, t, :].bitcast(E4M3), lhsT_scale=r_scales[:, t, :],
+                                rhs=dy_codes[:].bitcast(E5M2), rhs_scale=dy_scales[:], start=True, stop=True)
+
+        s_planes = keep.tile([P, LANES, SLOTS], BF16, name="s_planes", align_bytes=64)
+        for t in range(LANES):
+            if t % 2 == 0:
+                nc.scalar.activation(out=s_planes[:, t, :], in_=u_bank[t][:], func=COPY, scale=ck_sb[:, t:t + 1])
+            else:
+                nc.vector.tensor_scalar(out=s_planes[:, t, :], in0=u_bank[t][:], scalar1=ck_sb[:, t:t + 1],
+                                        scalar2=None, op0=MULT)
+
+        w_sorted = keep.tile([P, LANES, K], BF16, name="w_sorted", align_bytes=64)
+        w_grouped = keep.tile([P, LANES, P * LANES], BF16, name="w_grouped", align_bytes=64)
+        w_codes = keep.tile([P, LANES, P], U32, name="w_codes", align_bytes=64)
+        w_scales = keep.tile([P, LANES, P], U8, name="w_scales", align_bytes=64)
+        for n, t in enumerate(order):
+            nc.scalar.copy(out=w_sorted[:, n, :].rearrange("m (u p e) -> m p u e", u=2, e=2),
+                           in_=w_raw[t][:].rearrange("m (p u e) -> m p u e", u=2, e=2))
+
+        def turn_w(h):
+            turned = psum.tile([P, 2, 2, P], F32, name="turned%d" % h, tag="bank%d" % h)
+            for n in range(2):
+                words = w_sorted[:, 2 * h + n, :].bitcast(F32)
+                for u in range(2):
+                    nc.tensor.transpose(turned[:, n, u, :], words[:, u * P:(u + 1) * P], ident[:])
+            nc.scalar.copy(
+                out=w_grouped[:, 2 * h:2 * h + 2, :].rearrange("p n c -> p (n c)").bitcast(F32).rearrange("p (n m u) -> p n m u", n=2, u=2),
+                in_=turned[:].rearrange("p n u m -> p n m u"))
+
+        def quantize_w(h):
+            nc.vector.quantize_mx(out=w_codes[:, 2 * h:2 * h + 2, :].rearrange("p n m -> p (n m)").bitcast(E4M3),
+                                  scales=w_scales[:, 2 * h:2 * h + 2, :].rearrange("p n m -> p (n m)"),
+                                  in_=w_grouped[:, 2 * h:2 * h + 2, :].rearrange("p n c -> p (n c)"))
+
+        s_grouped = keep.tile([P, SLOTS, LANES], BF16, name="s_grouped", align_bytes=64)
+        s_codes = keep.tile([P, SLOTS], U32, name="s_codes", align_bytes=64)
+        s_scales = keep.tile([P, SLOTS], U8, name="s_scales", align_bytes=64)
+        s_split = 160
+        turn_w(0)
+        weave(nc.scalar.copy, s_grouped, s_planes, 0, s_split)
+        weave(nc.vector.tensor_copy, s_grouped, s_planes, s_split, SLOTS)
+        quantize_w(0)
+        nc.vector.quantize_mx(out=s_codes[:].bitcast(E5M2), scales=s_scales[:],
+                              in_=s_grouped[:].rearrange("p c t -> p (c t)"))
+
+        turn_w(1)
+        quantize_w(1)
+
+        half = SLOTS // 2
+        v_sb = keep.tile([P, LANES, SLOTS], F32, name="v_sb")
+        for n, t in enumerate(order):
+            v_bank = psum.tile([P, SLOTS], F32, name="v_bank%d" % n, tag="bank%d" % (LANES + n))
+            nc.tensor.matmul_mx(out=v_bank[:], lhsT=w_codes[:, n, :].bitcast(E4M3), lhsT_scale=w_scales[:, n, :],
+                                rhs=s_codes[:].bitcast(E5M2), rhs_scale=s_scales[:], start=True, stop=True)
+            for a, b in (((0, half), (half, SLOTS)) if n == 0 else ((0, SLOTS),)):
+                nc.scalar.copy(out=v_sb[:, t, a:b], in_=v_bank[:, a:b])
+
+        y_grouped = keep.tile([P, TOKENS, LANES], BF16, name="y_grouped", align_bytes=64)
+        y_codes = keep.tile([P, TOKENS], U32, name="y_codes", align_bytes=64)
+        y_scales = keep.tile([P, TOKENS], U8, name="y_scales", align_bytes=64)
+        for n, t in enumerate(order):
+            for a, b in (((0, half), (half, SLOTS)) if n == 0 else ((0, SLOTS),)):
+                nc.vector.tensor_tensor(window[t][:].indirect(slot_offsets(a, b)), picked[:, t, a:b], v_sb[:, t, a:b], ADD)
+            nc.sync.dma_start(out_planes[:, t, :], window[t][:])
+            if n == 0:
+
+                nc.scalar.copy(out=y_grouped[:, 0:512, 2:4],
+                               in_=window[t][:, 0:512].rearrange("p (c o) -> p c o", o=1).to_broadcast([P, 512, 2]))
+                nc.scalar.copy(out=y_grouped[:, 512:1024, t], in_=window[t][:, 512:1024])
+            elif n < LANES - 1:
+                nc.scalar.copy(out=y_grouped[:, :, t], in_=window[t][:])
+            else:
+                for a in (512, 768):
+                    nc.scalar.copy(out=y_grouped[:, a:a + 256, t], in_=window[t][:, a:a + 256])
+                for a in (0, 256):
+                    nc.vector.tensor_copy(out=y_grouped[:, a:a + 256, t], in_=window[t][:, a:a + 256])
+        words_out = out_1[0].rearrange("p c l -> p (c l)").bitcast(I32)
+        for a in range(0, TOKENS, 256):
+            nc.vector.quantize_mx(out=y_codes[:, a:a + 256].bitcast(E4M3), scales=y_scales[:, a:a + 256],
+                                  in_=y_grouped[:, a:a + 256, :].rearrange("p c t -> p (c t)"))
+            nc.sync.dma_start(words_out[:, a:a + 256], y_codes[:, a:a + 256].bitcast(I32))
+        for q in range(4):
+            queue = nc.sync if q == 0 else nc.scalar
+            queue.dma_start(out_2[0, 4 * q:4 * q + 4, :].bitcast(I32), y_scales[32 * q:32 * q + 4, :].bitcast(I32))

@@ -95,58 +95,67 @@ def tile_attend_greft_pl_kernel(tc, dyT, R, W, ck, offs, out_0, out_1, out_2):
                               in_=dy_grouped[:].rearrange("p c t -> p (c t)"))
 
         u_bank = [psum.tile([P, SLOTS], F32, name="u_bank%d" % t, tag="bank%d" % t) for t in range(LANES)]
-        for t in range(LANES):
+        for t in (0, 2, 1, 3):
             nc.vector.quantize_mx(out=r_codes[:, t, :].bitcast(E4M3), scales=r_scales[:, t, :],
                                   in_=r_grouped[:, t, :, :].rearrange("p m j -> p (m j)"))
             nc.tensor.matmul_mx(out=u_bank[t][:], lhsT=r_codes[:, t, :].bitcast(E4M3), lhsT_scale=r_scales[:, t, :],
                                 rhs=dy_codes[:].bitcast(E5M2), rhs_scale=dy_scales[:], start=True, stop=True)
 
-        s_planes = keep.tile([P, LANES, SLOTS], BF16, name="s_planes", align_bytes=64)
-        for t in range(LANES):
-            if t % 2 == 0:
-                nc.scalar.activation(out=s_planes[:, t, :], in_=u_bank[t][:], func=COPY, scale=ck_sb[:, t:t + 1])
-            else:
-                nc.vector.tensor_scalar(out=s_planes[:, t, :], in0=u_bank[t][:], scalar1=ck_sb[:, t:t + 1],
-                                        scalar2=None, op0=MULT)
+        mid = SLOTS // 2
+        s_pairs = [keep.tile([P, 2, mid, 2], BF16, name="s_pairs%d" % g, align_bytes=64) for g in range(2)]
+        for t in (0, 2, 1, 3):
+            for g in range(2):
+                dst = s_pairs[g][:, t // 2, :, t % 2]
+                src = u_bank[t][:, g * mid:(g + 1) * mid]
+                if t < 2:
+                    nc.scalar.activation(out=dst, in_=src, func=COPY, scale=ck_sb[:, t:t + 1])
+                else:
+                    nc.vector.tensor_scalar(out=dst, in0=src, scalar1=ck_sb[:, t:t + 1], scalar2=None, op0=MULT)
 
-        w_sorted = keep.tile([P, LANES, K], BF16, name="w_sorted", align_bytes=64)
-        w_grouped = keep.tile([P, LANES, P * LANES], BF16, name="w_grouped", align_bytes=64)
         w_codes = keep.tile([P, LANES, P], U32, name="w_codes", align_bytes=64)
         w_scales = keep.tile([P, LANES, P], U8, name="w_scales", align_bytes=64)
+        w_sorted = [keep.tile([P, K], BF16, name="w_sorted%d" % n, align_bytes=64) for n in range(LANES)]
         for n, t in enumerate(order):
-            nc.scalar.copy(out=w_sorted[:, n, :].rearrange("m (u p e) -> m p u e", u=2, e=2),
-                           in_=w_raw[t][:].rearrange("m (p u e) -> m p u e", u=2, e=2))
+            copy = nc.vector.tensor_copy if n in (2, 3,) else nc.scalar.copy
+            copy(out=w_sorted[n][:].rearrange("m (u p e) -> m p u e", u=2, e=2),
+                 in_=w_raw[t][:].rearrange("m (p u e) -> m p u e", u=2, e=2))
 
-        def turn_w(h):
-            turned = psum.tile([P, 2, 2, P], F32, name="turned%d" % h, tag="bank%d" % h)
-            for n in range(2):
-                words = w_sorted[:, 2 * h + n, :].bitcast(F32)
+        def turn_w(first, count, bank):
+            turned = psum.tile([P, count, 2, P], F32, name="turned%d" % first, tag="bank%d" % bank)
+            for n in range(count):
+                words = w_sorted[first + n][:].bitcast(F32)
                 for u in range(2):
                     nc.tensor.transpose(turned[:, n, u, :], words[:, u * P:(u + 1) * P], ident[:])
-            nc.scalar.copy(
-                out=w_grouped[:, 2 * h:2 * h + 2, :].rearrange("p n c -> p (n c)").bitcast(F32).rearrange("p (n m u) -> p n m u", n=2, u=2),
-                in_=turned[:].rearrange("p n u m -> p n m u"))
+            grouped = keep.tile([P, count * P * LANES], BF16, name="w_grouped%d" % first, align_bytes=64)
+            nc.scalar.copy(out=grouped[:].bitcast(F32).rearrange("p (n m u) -> p n m u", n=count, u=2),
+                           in_=turned[:].rearrange("p n u m -> p n m u"))
+            return grouped
 
-        def quantize_w(h):
-            nc.vector.quantize_mx(out=w_codes[:, 2 * h:2 * h + 2, :].rearrange("p n m -> p (n m)").bitcast(E4M3),
-                                  scales=w_scales[:, 2 * h:2 * h + 2, :].rearrange("p n m -> p (n m)"),
-                                  in_=w_grouped[:, 2 * h:2 * h + 2, :].rearrange("p n c -> p (n c)"))
+        def quantize_w(first, count, grouped):
+            nc.vector.quantize_mx(out=w_codes[:, first:first + count, :].rearrange("p n m -> p (n m)").bitcast(E4M3),
+                                  scales=w_scales[:, first:first + count, :].rearrange("p n m -> p (n m)"),
+                                  in_=grouped[:])
 
-        s_grouped = keep.tile([P, SLOTS, LANES], BF16, name="s_grouped", align_bytes=64)
-        s_codes = keep.tile([P, SLOTS], U32, name="s_codes", align_bytes=64)
+        s_grouped = [keep.tile([P, mid * LANES], BF16, name="s_grouped%d" % g, align_bytes=64) for g in range(2)]
+        s_codes = keep.tile([P, SLOTS], U32, name="s_codes", tag="s_then_y", align_bytes=64)
         s_scales = keep.tile([P, SLOTS], U8, name="s_scales", align_bytes=64)
-        s_split = 160
-        turn_w(0)
-        weave(nc.scalar.copy, s_grouped, s_planes, 0, s_split)
-        weave(nc.vector.tensor_copy, s_grouped, s_planes, s_split, SLOTS)
-        quantize_w(0)
-        nc.vector.quantize_mx(out=s_codes[:].bitcast(E5M2), scales=s_scales[:],
-                              in_=s_grouped[:].rearrange("p c t -> p (c t)"))
 
-        turn_w(1)
-        quantize_w(1)
+        def join_pairs(copy, g):
+            copy(out=s_grouped[g][:].bitcast(F32).rearrange("p (c i h) -> p c h i", i=2, h=2),
+                 in_=s_pairs[g][:].rearrange("p h c e -> p (h c e)").bitcast(F32).rearrange("p (h c i) -> p c h i", h=2, i=2))
 
-        half = SLOTS // 2
+        w_first = turn_w(0, 1, 0)
+        join_pairs(nc.scalar.copy, 0)
+        quantize_w(0, 1, w_first)
+        join_pairs(nc.vector.tensor_copy, 1)
+        for g in range(2):
+            nc.vector.quantize_mx(out=s_codes[:, g * mid:(g + 1) * mid].bitcast(E5M2), scales=s_scales[:, g * mid:(g + 1) * mid],
+                                  in_=s_grouped[g][:])
+
+        quantize_w(1, 1, turn_w(1, 1, 2))
+        quantize_w(2, 2, turn_w(2, 2, 1))
+
+        half = 128
         v_sb = keep.tile([P, LANES, SLOTS], F32, name="v_sb")
         for n, t in enumerate(order):
             v_bank = psum.tile([P, SLOTS], F32, name="v_bank%d" % n, tag="bank%d" % (LANES + n))
@@ -155,7 +164,7 @@ def tile_attend_greft_pl_kernel(tc, dyT, R, W, ck, offs, out_0, out_1, out_2):
             for a, b in (((0, half), (half, SLOTS)) if n == 0 else ((0, SLOTS),)):
                 nc.scalar.copy(out=v_sb[:, t, a:b], in_=v_bank[:, a:b])
 
-        y_grouped = keep.tile([P, TOKENS, LANES], BF16, name="y_grouped", align_bytes=64)
+        y_grouped = keep.tile([P, TOKENS, LANES], BF16, name="y_grouped", tag="s_then_y", align_bytes=64)
         y_codes = keep.tile([P, TOKENS], U32, name="y_codes", align_bytes=64)
         y_scales = keep.tile([P, TOKENS], U8, name="y_scales", align_bytes=64)
         for n, t in enumerate(order):
@@ -164,16 +173,16 @@ def tile_attend_greft_pl_kernel(tc, dyT, R, W, ck, offs, out_0, out_1, out_2):
             nc.sync.dma_start(out_planes[:, t, :], window[t][:])
             if n == 0:
 
-                nc.scalar.copy(out=y_grouped[:, 0:512, 2:4],
-                               in_=window[t][:, 0:512].rearrange("p (c o) -> p c o", o=1).to_broadcast([P, 512, 2]))
-                nc.scalar.copy(out=y_grouped[:, 512:1024, t], in_=window[t][:, 512:1024])
+                nc.scalar.copy(out=y_grouped[:, 0:640, 2:4],
+                               in_=window[t][:, 0:640].rearrange("p (c o) -> p c o", o=1).to_broadcast([P, 640, 2]))
+                nc.scalar.copy(out=y_grouped[:, 640:1024, t], in_=window[t][:, 640:1024])
             elif n < LANES - 1:
                 nc.scalar.copy(out=y_grouped[:, :, t], in_=window[t][:])
             else:
-                for a in (512, 768):
-                    nc.scalar.copy(out=y_grouped[:, a:a + 256, t], in_=window[t][:, a:a + 256])
-                for a in (0, 256):
-                    nc.vector.tensor_copy(out=y_grouped[:, a:a + 256, t], in_=window[t][:, a:a + 256])
+                for a, b in ((640, 768), (768, 1024)):
+                    nc.scalar.copy(out=y_grouped[:, a:b, t], in_=window[t][:, a:b])
+                for a, b in ((0, 256), (256, 640)):
+                    nc.vector.tensor_copy(out=y_grouped[:, a:b, t], in_=window[t][:, a:b])
         words_out = out_1[0].rearrange("p c l -> p (c l)").bitcast(I32)
         for a in range(0, TOKENS, 256):
             nc.vector.quantize_mx(out=y_codes[:, a:a + 256].bitcast(E4M3), scales=y_scales[:, a:a + 256],

@@ -48,10 +48,11 @@ def tile_attend_greft_pl_kernel(tc, dyT, R, W, ck, offs, out_0, out_1, out_2):
         for h in range(2):
             nc.sync.dma_start(r_raw[h][:], r_rows[:, :, h * K // 2:(h + 1) * K // 2])
         ck_sb = keep.tile([P, LANES], F32, name="ck_sb")
-        nc.sync.dma_start(ck_sb[:], ck.rearrange("(p t) o -> p (t o)", t=LANES))
         w_raw = [keep.tile([P, K], F32, name="w_raw%d" % t) for t in range(LANES)]
         for t in order:
             nc.sync.dma_start(w_raw[t][:], w_planes[:, t, :])
+            if t == order[0]:
+                nc.sync.dma_start(ck_sb[:], ck.rearrange("(p t) o -> p (t o)", t=LANES))
         window = [keep.tile([P, TOKENS], F32, name="window%d" % t) for t in range(LANES)]
         for t in order:
             nc.sync.dma_start(window[t][:], dy_planes[:, t, :])
@@ -61,10 +62,6 @@ def tile_attend_greft_pl_kernel(tc, dyT, R, W, ck, offs, out_0, out_1, out_2):
 
         def slot_offsets(a, b):
             return offsets[:, a // PER_COL:b // PER_COL]
-
-        def weave(copy, dst, src, a, b):
-            copy(out=dst[:, a:b, :].rearrange("p (c i) t -> p c t i", i=4),
-                 in_=src[:, :, a:b].rearrange("p t (c i) -> p c t i", i=4))
 
         picked = keep.tile([P, LANES, SLOTS], F32, name="picked")
         dy_grouped = keep.tile([P, SLOTS, LANES], BF16, name="dy_grouped", align_bytes=64)
@@ -79,20 +76,26 @@ def tile_attend_greft_pl_kernel(tc, dyT, R, W, ck, offs, out_0, out_1, out_2):
             copy(out=r_grouped[:, :, a:b, :].rearrange("p t m j -> p m j t"),
                  in_=r_raw[h][:].rearrange("p j (m t) -> p m j t", t=LANES)[:, base:base + b - a, :, :])
 
-        dy_split = 128
+        def weave_pair(copy, h, a, b):
+            copy(out=dy_grouped[:, a:b, 2 * h:2 * h + 2].rearrange("p (c i) t -> p c t i", i=4),
+                 in_=picked[:, 2 * h:2 * h + 2, a:b].rearrange("p t (c i) -> p c t i", i=4))
+
         last = LANES - 1
         for t in range(last):
             nc.vector.tensor_copy(picked[:, t, :], source[t][:].indirect(offsets[:]))
-        nc.vector.tensor_copy(picked[:, last, 0:dy_split], source[last][:].indirect(slot_offsets(0, dy_split)))
-        weave(nc.scalar.copy, dy_grouped, picked, 0, dy_split)
-        nc.vector.tensor_copy(picked[:, last, dy_split:SLOTS], source[last][:].indirect(slot_offsets(dy_split, SLOTS)))
-        weave(nc.vector.tensor_copy, dy_grouped, picked, dy_split, SLOTS)
-        r_split = P - 24
+            if t == 1:
+                weave_pair(nc.scalar.copy, 0, 0, SLOTS)
+        for a in (0, SLOTS // 2):
+            nc.vector.tensor_copy(picked[:, last, a:a + SLOTS // 2], source[last][:].indirect(slot_offsets(a, a + SLOTS // 2)))
+        for a in (0, SLOTS // 2):
+            weave_pair(nc.vector.tensor_copy, 1, a, a + SLOTS // 2)
+        for a in (0, SLOTS // 2):
+            nc.vector.quantize_mx(out=dy_codes[:, a:a + SLOTS // 2].bitcast(E5M2), scales=dy_scales[:, a:a + SLOTS // 2],
+                                  in_=dy_grouped[:, a:a + SLOTS // 2, :].rearrange("p c t -> p (c t)"))
+        r_split = P - 36
         deal_r(nc.scalar.copy, 0, P // 2)
         deal_r(nc.scalar.copy, P // 2, r_split)
         deal_r(nc.vector.tensor_copy, r_split, P)
-        nc.vector.quantize_mx(out=dy_codes[:].bitcast(E5M2), scales=dy_scales[:],
-                              in_=dy_grouped[:].rearrange("p c t -> p (c t)"))
 
         u_bank = [psum.tile([P, SLOTS], F32, name="u_bank%d" % t, tag="bank%d" % t) for t in range(LANES)]
         for t in (0, 2, 1, 3):
@@ -112,29 +115,32 @@ def tile_attend_greft_pl_kernel(tc, dyT, R, W, ck, offs, out_0, out_1, out_2):
                 else:
                     nc.vector.tensor_scalar(out=dst, in0=src, scalar1=ck_sb[:, t:t + 1], scalar2=None, op0=MULT)
 
-        w_codes = keep.tile([P, LANES, P], U32, name="w_codes", align_bytes=64)
-        w_scales = keep.tile([P, LANES, P], U8, name="w_scales", align_bytes=64)
+        w_codes = []
+        w_scales = []
         w_sorted = [keep.tile([P, K], BF16, name="w_sorted%d" % n, align_bytes=64) for n in range(LANES)]
         for n, t in enumerate(order):
             copy = nc.vector.tensor_copy if n in (2, 3,) else nc.scalar.copy
             copy(out=w_sorted[n][:].rearrange("m (u p e) -> m p u e", u=2, e=2),
                  in_=w_raw[t][:].rearrange("m (p u e) -> m p u e", u=2, e=2))
 
-        def turn_w(first, count, bank):
+        def turn_w(first, count, bank, copy):
             turned = psum.tile([P, count, 2, P], F32, name="turned%d" % first, tag="bank%d" % bank)
             for n in range(count):
                 words = w_sorted[first + n][:].bitcast(F32)
                 for u in range(2):
                     nc.tensor.transpose(turned[:, n, u, :], words[:, u * P:(u + 1) * P], ident[:])
             grouped = keep.tile([P, count * P * LANES], BF16, name="w_grouped%d" % first, align_bytes=64)
-            nc.scalar.copy(out=grouped[:].bitcast(F32).rearrange("p (n m u) -> p n m u", n=count, u=2),
-                           in_=turned[:].rearrange("p n u m -> p n m u"))
+            copy(out=grouped[:].bitcast(F32).rearrange("p (n m u) -> p n m u", n=count, u=2),
+                 in_=turned[:].rearrange("p n u m -> p n m u"))
             return grouped
 
         def quantize_w(first, count, grouped):
-            nc.vector.quantize_mx(out=w_codes[:, first:first + count, :].rearrange("p n m -> p (n m)").bitcast(E4M3),
-                                  scales=w_scales[:, first:first + count, :].rearrange("p n m -> p (n m)"),
-                                  in_=grouped[:])
+            codes = keep.tile([P, count * P], U32, name="w_codes%d" % first, align_bytes=64)
+            scales = keep.tile([P, count * P], U8, name="w_scales%d" % first, align_bytes=64)
+            nc.vector.quantize_mx(out=codes[:].bitcast(E4M3), scales=scales[:], in_=grouped[:])
+            for n in range(count):
+                w_codes.append(codes[:, n * P:(n + 1) * P])
+                w_scales.append(scales[:, n * P:(n + 1) * P])
 
         s_grouped = [keep.tile([P, mid * LANES], BF16, name="s_grouped%d" % g, align_bytes=64) for g in range(2)]
         s_codes = keep.tile([P, SLOTS], U32, name="s_codes", tag="s_then_y", align_bytes=64)
@@ -144,22 +150,22 @@ def tile_attend_greft_pl_kernel(tc, dyT, R, W, ck, offs, out_0, out_1, out_2):
             copy(out=s_grouped[g][:].bitcast(F32).rearrange("p (c i h) -> p c h i", i=2, h=2),
                  in_=s_pairs[g][:].rearrange("p h c e -> p (h c e)").bitcast(F32).rearrange("p (h c i) -> p c h i", h=2, i=2))
 
-        w_first = turn_w(0, 1, 0)
+        w_first = turn_w(0, 1, 0, nc.vector.tensor_copy)
         join_pairs(nc.scalar.copy, 0)
-        quantize_w(0, 1, w_first)
         join_pairs(nc.vector.tensor_copy, 1)
+        quantize_w(0, 1, w_first)
         for g in range(2):
             nc.vector.quantize_mx(out=s_codes[:, g * mid:(g + 1) * mid].bitcast(E5M2), scales=s_scales[:, g * mid:(g + 1) * mid],
                                   in_=s_grouped[g][:])
 
-        quantize_w(1, 1, turn_w(1, 1, 2))
-        quantize_w(2, 2, turn_w(2, 2, 1))
+        quantize_w(1, 1, turn_w(1, 1, 2, nc.scalar.copy))
+        quantize_w(2, 2, turn_w(2, 2, 1, nc.scalar.copy))
 
         half = 128
         v_sb = keep.tile([P, LANES, SLOTS], F32, name="v_sb")
         for n, t in enumerate(order):
             v_bank = psum.tile([P, SLOTS], F32, name="v_bank%d" % n, tag="bank%d" % (LANES + n))
-            nc.tensor.matmul_mx(out=v_bank[:], lhsT=w_codes[:, n, :].bitcast(E4M3), lhsT_scale=w_scales[:, n, :],
+            nc.tensor.matmul_mx(out=v_bank[:], lhsT=w_codes[n].bitcast(E4M3), lhsT_scale=w_scales[n],
                                 rhs=s_codes[:].bitcast(E5M2), rhs_scale=s_scales[:], start=True, stop=True)
             for a, b in (((0, half), (half, SLOTS)) if n == 0 else ((0, SLOTS),)):
                 nc.scalar.copy(out=v_sb[:, t, a:b], in_=v_bank[:, a:b])

@@ -13,7 +13,6 @@ E4M3 = mybir.dt.float8_e4m3fn_x4
 E5M2 = mybir.dt.float8_e5m2_x4
 COPY = mybir.ActivationFunctionType.Copy
 ADD = mybir.AluOpType.add
-MULT = mybir.AluOpType.mult
 
 P = 128
 LANES = 4
@@ -22,6 +21,13 @@ K = 512
 SLOTS = 512
 TOKENS = 1024
 PER_COL = 16
+HALF = SLOTS // 2
+DY_SPLIT = 192
+R_SPLIT = 44
+S_SPLIT = 384
+V_HEAD = 64
+Y_SPLIT = 576
+Y_PIECE = 256
 
 FLOPS = 2 * 2 * D * K * SLOTS
 
@@ -32,27 +38,26 @@ def tile_attend_greft_pl_kernel(tc, dyT, R, W, ck, offs, out_0, out_1, out_2):
         keep = ctx.enter_context(tc.tile_pool(name="keep", bufs=1))
         psum = ctx.enter_context(tc.psum_pool(name="psum", bufs=1))
 
-        offsets = keep.tile([P, SLOTS // PER_COL], U16, name="offsets")
-        nc.sync.dma_start(offsets[:], offs)
-
         dy_planes = dyT.rearrange("(p t) c -> p t c", t=LANES)
         out_planes = out_0.rearrange("(p t) c -> p t c", t=LANES)
         w_planes = W.rearrange("(m t) k -> m t k", t=LANES)
-        r_rows = R.rearrange("(p j) k -> p j k", j=LANES)
-        order = (2, 0, 1, 3)
+        order = (0, 2, 3, 1)
 
+        offsets = keep.tile([P, SLOTS // PER_COL], U16, name="offsets")
+        nc.sync.dma_start(offsets[:], offs)
         source = [keep.tile([P, TOKENS], F32, name="source%d" % t) for t in range(LANES)]
         for t in range(LANES):
             nc.sync.dma_start(source[t][:], dy_planes[:, t, :])
-        r_raw = [keep.tile([P, LANES, K // 2], F32, name="r_raw%d" % h) for h in range(2)]
-        for h in range(2):
-            nc.sync.dma_start(r_raw[h][:], r_rows[:, :, h * K // 2:(h + 1) * K // 2])
+        r_rows = R.rearrange("(p j) k -> p j k", j=LANES)
+        r_raw = [keep.tile([P, LANES, K // 2], F32, name="r_raw%d" % g) for g in range(2)]
+        for g in range(2):
+            nc.sync.dma_start(r_raw[g][:], r_rows[:, :, g * K // 2:(g + 1) * K // 2])
         ck_sb = keep.tile([P, LANES], F32, name="ck_sb")
-        w_raw = [keep.tile([P, K], F32, name="w_raw%d" % t) for t in range(LANES)]
-        for t in order:
-            nc.sync.dma_start(w_raw[t][:], w_planes[:, t, :])
-            if t == order[0]:
-                nc.sync.dma_start(ck_sb[:], ck.rearrange("(p t) o -> p (t o)", t=LANES))
+        nc.sync.dma_start(ck_sb[:], ck.rearrange("(p t) o -> p (t o)", t=LANES))
+        w_first = keep.tile([P, K], F32, name="w_first")
+        nc.sync.dma_start(w_first[:], w_planes[:, 0, :])
+        w_rest = keep.tile([P, LANES - 1, K], F32, name="w_rest")
+        nc.sync.dma_start(w_rest[:], w_planes[:, 1:LANES, :])
         window = [keep.tile([P, TOKENS], F32, name="window%d" % t) for t in range(LANES)]
         for t in order:
             nc.sync.dma_start(window[t][:], dy_planes[:, t, :])
@@ -63,137 +68,124 @@ def tile_attend_greft_pl_kernel(tc, dyT, R, W, ck, offs, out_0, out_1, out_2):
         def slot_offsets(a, b):
             return offsets[:, a // PER_COL:b // PER_COL]
 
+        def weave(copy, lanes, planes):
+            copy(out=lanes.rearrange("p (c i) t -> p c t i", i=4), in_=planes.rearrange("p t (c i) -> p c t i", i=4))
+
+        def quantize(codes, scales, grouped, fmt):
+            nc.vector.quantize_mx(out=codes.bitcast(fmt), scales=scales, in_=grouped.rearrange("p c t -> p (c t)"))
+
         picked = keep.tile([P, LANES, SLOTS], F32, name="picked")
         dy_grouped = keep.tile([P, SLOTS, LANES], BF16, name="dy_grouped", align_bytes=64)
         dy_codes = keep.tile([P, SLOTS], U32, name="dy_codes", align_bytes=64)
         dy_scales = keep.tile([P, SLOTS], U8, name="dy_scales", align_bytes=64)
-        r_grouped = keep.tile([P, LANES, P, LANES], BF16, name="r_grouped", align_bytes=64)
-        r_codes = keep.tile([P, LANES, P], U32, name="r_codes", align_bytes=64)
-        r_scales = keep.tile([P, LANES, P], U8, name="r_scales", align_bytes=64)
-
-        def deal_r(copy, a, b):
-            h, base = divmod(a, P // 2)
-            copy(out=r_grouped[:, :, a:b, :].rearrange("p t m j -> p m j t"),
-                 in_=r_raw[h][:].rearrange("p j (m t) -> p m j t", t=LANES)[:, base:base + b - a, :, :])
-
-        def weave_pair(copy, h, a, b):
-            copy(out=dy_grouped[:, a:b, 2 * h:2 * h + 2].rearrange("p (c i) t -> p c t i", i=4),
-                 in_=picked[:, 2 * h:2 * h + 2, a:b].rearrange("p t (c i) -> p c t i", i=4))
-
         last = LANES - 1
         for t in range(last):
             nc.vector.tensor_copy(picked[:, t, :], source[t][:].indirect(offsets[:]))
             if t == 1:
-                weave_pair(nc.scalar.copy, 0, 0, SLOTS)
-        for a in (0, SLOTS // 2):
-            nc.vector.tensor_copy(picked[:, last, a:a + SLOTS // 2], source[last][:].indirect(slot_offsets(a, a + SLOTS // 2)))
-        for a in (0, SLOTS // 2):
-            weave_pair(nc.vector.tensor_copy, 1, a, a + SLOTS // 2)
-        for a in (0, SLOTS // 2):
-            nc.vector.quantize_mx(out=dy_codes[:, a:a + SLOTS // 2].bitcast(E5M2), scales=dy_scales[:, a:a + SLOTS // 2],
-                                  in_=dy_grouped[:, a:a + SLOTS // 2, :].rearrange("p c t -> p (c t)"))
-        r_split = P - 36
-        deal_r(nc.scalar.copy, 0, P // 2)
-        deal_r(nc.scalar.copy, P // 2, r_split)
-        deal_r(nc.vector.tensor_copy, r_split, P)
+                weave(nc.scalar.copy, dy_grouped[:, DY_SPLIT:SLOTS, 0:2], picked[:, 0:2, DY_SPLIT:SLOTS])
+        for a, b in ((0, DY_SPLIT), (DY_SPLIT, SLOTS)):
+            nc.vector.tensor_copy(picked[:, last, a:b], source[last][:].indirect(slot_offsets(a, b)))
+        weave(nc.scalar.copy, dy_grouped[:, 0:DY_SPLIT, :], picked[:, :, 0:DY_SPLIT])
+        weave(nc.vector.tensor_copy, dy_grouped[:, DY_SPLIT:SLOTS, 2:4], picked[:, 2:4, DY_SPLIT:SLOTS])
+        for a in (0, HALF):
+            quantize(dy_codes[:, a:a + HALF], dy_scales[:, a:a + HALF], dy_grouped[:, a:a + HALF, :], E5M2)
 
+        r_codes = keep.tile([P, LANES, P], U32, name="r_codes", align_bytes=64)
+        r_scales = keep.tile([P, LANES, P], U8, name="r_scales", align_bytes=64)
+        r_columns = [r_raw[g][:].rearrange("p j (m t) -> p m j t", t=LANES) for g in range(2)]
         u_bank = [psum.tile([P, SLOTS], F32, name="u_bank%d" % t, tag="bank%d" % t) for t in range(LANES)]
-        for t in (0, 2, 1, 3):
-            nc.vector.quantize_mx(out=r_codes[:, t, :].bitcast(E4M3), scales=r_scales[:, t, :],
-                                  in_=r_grouped[:, t, :, :].rearrange("p m j -> p (m j)"))
-            nc.tensor.matmul_mx(out=u_bank[t][:], lhsT=r_codes[:, t, :].bitcast(E4M3), lhsT_scale=r_scales[:, t, :],
-                                rhs=dy_codes[:].bitcast(E5M2), rhs_scale=dy_scales[:], start=True, stop=True)
+        for h in range(2):
+            r_grouped = keep.tile([P, 2, P, LANES], BF16, name="r_grouped%d" % h, tag="r_then_w", align_bytes=64)
+            if h == 0:
+                shares = ((0, 0, 64, nc.scalar.copy), (1, 0, 64, nc.scalar.copy))
+            else:
+                shares = ((0, 0, R_SPLIT, nc.scalar.copy), (1, 0, 64, nc.vector.tensor_copy), (0, R_SPLIT, 64, nc.vector.tensor_copy))
+            for g, a, b, copy in shares:
+                copy(out=r_grouped[:, :, 64 * g + a:64 * g + b, :].rearrange("p e m j -> p m j e"),
+                     in_=r_columns[g][:, a:b, :, 2 * h:2 * h + 2])
+            for e in range(2):
+                t = 2 * h + e
+                quantize(r_codes[:, t, :], r_scales[:, t, :], r_grouped[:, e, :, :], E4M3)
+                nc.tensor.matmul_mx(out=u_bank[t][:], lhsT=r_codes[:, t, :].bitcast(E4M3), lhsT_scale=r_scales[:, t, :],
+                                    rhs=dy_codes[:].bitcast(E5M2), rhs_scale=dy_scales[:], start=True, stop=True)
 
-        mid = SLOTS // 2
-        s_pairs = [keep.tile([P, 2, mid, 2], BF16, name="s_pairs%d" % g, align_bytes=64) for g in range(2)]
-        for t in (0, 2, 1, 3):
-            for g in range(2):
-                dst = s_pairs[g][:, t // 2, :, t % 2]
-                src = u_bank[t][:, g * mid:(g + 1) * mid]
-                if t < 2:
-                    nc.scalar.activation(out=dst, in_=src, func=COPY, scale=ck_sb[:, t:t + 1])
-                else:
-                    nc.vector.tensor_scalar(out=dst, in0=src, scalar1=ck_sb[:, t:t + 1], scalar2=None, op0=MULT)
+        w_sorted = [keep.tile([P, K], BF16, name="w_sorted%d" % t, tag="r_then_w" if t == order[1] else "w_sorted%d" % t, align_bytes=64)
+                    for t in range(LANES)]
+        for t in order:
+            w_plane = w_first[:] if t == 0 else w_rest[:, t - 1, :]
+            copy = nc.scalar.copy if t == 0 else nc.vector.tensor_copy
+            copy(out=w_sorted[t][:].rearrange("m (u p e) -> m u p e", u=2, e=2),
+                 in_=w_plane.rearrange("m (p u e) -> m u p e", u=2, e=2))
 
-        w_codes = []
-        w_scales = []
-        w_sorted = [keep.tile([P, K], BF16, name="w_sorted%d" % n, align_bytes=64) for n in range(LANES)]
-        for n, t in enumerate(order):
-            copy = nc.vector.tensor_copy if n in (2, 3,) else nc.scalar.copy
-            copy(out=w_sorted[n][:].rearrange("m (u p e) -> m p u e", u=2, e=2),
-                 in_=w_raw[t][:].rearrange("m (p u e) -> m p u e", u=2, e=2))
+        s_planes = keep.tile([P, LANES, SLOTS], BF16, name="s_planes", align_bytes=64)
+        s_pieces = ((0, 128), (128, 256), (256, SLOTS))
+        for t in range(LANES):
+            for a, b in (s_pieces if t == last else ((0, SLOTS),)):
+                nc.scalar.activation(out=s_planes[:, t, a:b], in_=u_bank[t][:, a:b], func=COPY, scale=ck_sb[:, t:t + 1])
 
-        def turn_w(first, count, bank, copy):
-            turned = psum.tile([P, count, 2, P], F32, name="turned%d" % first, tag="bank%d" % bank)
+        w_codes = keep.tile([P, LANES * P], U32, name="w_codes", align_bytes=64)
+        w_scales = keep.tile([P, LANES * P], U8, name="w_scales", align_bytes=64)
+
+        def turn_w(first, count, bank, grouped):
+            turned = psum.tile([P, count, 2, P], F32, name="turned%d" % first, tag=bank)
             for n in range(count):
-                words = w_sorted[first + n][:].bitcast(F32)
+                words = w_sorted[order[first + n]][:].bitcast(F32)
                 for u in range(2):
                     nc.tensor.transpose(turned[:, n, u, :], words[:, u * P:(u + 1) * P], ident[:])
-            grouped = keep.tile([P, count * P * LANES], BF16, name="w_grouped%d" % first, align_bytes=64)
-            copy(out=grouped[:].bitcast(F32).rearrange("p (n m u) -> p n m u", n=count, u=2),
-                 in_=turned[:].rearrange("p n u m -> p n m u"))
-            return grouped
+            nc.scalar.copy(out=grouped.rearrange("p m t -> p (m t)").bitcast(F32).rearrange("p (n m u) -> p n m u", n=count, u=2),
+                           in_=turned[:].rearrange("p n u m -> p n m u"))
 
-        def quantize_w(first, count, grouped):
-            codes = keep.tile([P, count * P], U32, name="w_codes%d" % first, align_bytes=64)
-            scales = keep.tile([P, count * P], U8, name="w_scales%d" % first, align_bytes=64)
-            nc.vector.quantize_mx(out=codes[:].bitcast(E4M3), scales=scales[:], in_=grouped[:])
-            for n in range(count):
-                w_codes.append(codes[:, n * P:(n + 1) * P])
-                w_scales.append(scales[:, n * P:(n + 1) * P])
-
-        s_grouped = [keep.tile([P, mid * LANES], BF16, name="s_grouped%d" % g, align_bytes=64) for g in range(2)]
+        s_grouped = keep.tile([P, SLOTS, LANES], BF16, name="s_grouped", align_bytes=64)
         s_codes = keep.tile([P, SLOTS], U32, name="s_codes", tag="s_then_y", align_bytes=64)
         s_scales = keep.tile([P, SLOTS], U8, name="s_scales", align_bytes=64)
+        w_head = keep.tile([P, P, LANES], BF16, name="w_head", align_bytes=64)
+        turn_w(0, 1, "bank1", w_head[:])
+        for a in range(0, S_SPLIT, 128):
+            weave(nc.vector.tensor_copy, s_grouped[:, a:a + 128, :], s_planes[:, :, a:a + 128])
+        weave(nc.scalar.copy, s_grouped[:, S_SPLIT:SLOTS, :], s_planes[:, :, S_SPLIT:SLOTS])
+        quantize(w_codes[:, 0:P], w_scales[:, 0:P], w_head[:], E4M3)
+        for a in (0, HALF):
+            quantize(s_codes[:, a:a + HALF], s_scales[:, a:a + HALF], s_grouped[:, a:a + HALF, :], E5M2)
+        w_late = keep.tile([P, 3 * P, LANES], BF16, name="w_late", tag="s_planes", align_bytes=64)
+        turn_w(1, 2, "bank5", w_late[:, 0:2 * P, :])
+        turn_w(3, 1, "bank7", w_late[:, 2 * P:3 * P, :])
+        quantize(w_codes[:, P:3 * P], w_scales[:, P:3 * P], w_late[:, 0:2 * P, :], E4M3)
+        quantize(w_codes[:, 3 * P:4 * P], w_scales[:, 3 * P:4 * P], w_late[:, 2 * P:3 * P, :], E4M3)
 
-        def join_pairs(copy, g):
-            copy(out=s_grouped[g][:].bitcast(F32).rearrange("p (c i h) -> p c h i", i=2, h=2),
-                 in_=s_pairs[g][:].rearrange("p h c e -> p (h c e)").bitcast(F32).rearrange("p (h c i) -> p c h i", h=2, i=2))
-
-        w_first = turn_w(0, 1, 0, nc.vector.tensor_copy)
-        join_pairs(nc.scalar.copy, 0)
-        join_pairs(nc.vector.tensor_copy, 1)
-        quantize_w(0, 1, w_first)
-        for g in range(2):
-            nc.vector.quantize_mx(out=s_codes[:, g * mid:(g + 1) * mid].bitcast(E5M2), scales=s_scales[:, g * mid:(g + 1) * mid],
-                                  in_=s_grouped[g][:])
-
-        quantize_w(1, 1, turn_w(1, 1, 2, nc.scalar.copy))
-        quantize_w(2, 2, turn_w(2, 2, 1, nc.scalar.copy))
-
-        half = 128
         v_sb = keep.tile([P, LANES, SLOTS], F32, name="v_sb")
         for n, t in enumerate(order):
             v_bank = psum.tile([P, SLOTS], F32, name="v_bank%d" % n, tag="bank%d" % (LANES + n))
-            nc.tensor.matmul_mx(out=v_bank[:], lhsT=w_codes[n].bitcast(E4M3), lhsT_scale=w_scales[n],
+            nc.tensor.matmul_mx(out=v_bank[:], lhsT=w_codes[:, n * P:(n + 1) * P].bitcast(E4M3),
+                                lhsT_scale=w_scales[:, n * P:(n + 1) * P],
                                 rhs=s_codes[:].bitcast(E5M2), rhs_scale=s_scales[:], start=True, stop=True)
-            for a, b in (((0, half), (half, SLOTS)) if n == 0 else ((0, SLOTS),)):
+            for a, b in (((0, V_HEAD), (V_HEAD, SLOTS)) if n == 0 else ((0, SLOTS),)):
                 nc.scalar.copy(out=v_sb[:, t, a:b], in_=v_bank[:, a:b])
 
         y_grouped = keep.tile([P, TOKENS, LANES], BF16, name="y_grouped", tag="s_then_y", align_bytes=64)
-        y_codes = keep.tile([P, TOKENS], U32, name="y_codes", align_bytes=64)
         y_scales = keep.tile([P, TOKENS], U8, name="y_scales", align_bytes=64)
         for n, t in enumerate(order):
-            for a, b in (((0, half), (half, SLOTS)) if n == 0 else ((0, SLOTS),)):
+            for a, b in (((0, V_HEAD), (V_HEAD, SLOTS)) if n == 0 else ((0, SLOTS),)):
                 nc.vector.tensor_tensor(window[t][:].indirect(slot_offsets(a, b)), picked[:, t, a:b], v_sb[:, t, a:b], ADD)
             nc.sync.dma_start(out_planes[:, t, :], window[t][:])
             if n == 0:
-
-                nc.scalar.copy(out=y_grouped[:, 0:640, 2:4],
-                               in_=window[t][:, 0:640].rearrange("p (c o) -> p c o", o=1).to_broadcast([P, 640, 2]))
-                nc.scalar.copy(out=y_grouped[:, 640:1024, t], in_=window[t][:, 640:1024])
-            elif n < LANES - 1:
+                nc.scalar.copy(out=y_grouped[:, :, t], in_=window[t][:])
+                a, b = Y_PIECE - 4, Y_PIECE + 4
+                nc.scalar.copy(out=y_grouped[:, a:b, 0:2],
+                               in_=window[t][:, a:b].rearrange("p (c o) -> p c o", o=1).to_broadcast([P, b - a, 2]))
+            elif n < last:
                 nc.scalar.copy(out=y_grouped[:, :, t], in_=window[t][:])
             else:
-                for a, b in ((640, 768), (768, 1024)):
+                for a, b in ((Y_SPLIT, 768), (768, 896), (896, TOKENS)):
                     nc.scalar.copy(out=y_grouped[:, a:b, t], in_=window[t][:, a:b])
-                for a, b in ((0, 256), (256, 640)):
+                for a, b in ((0, Y_PIECE), (Y_PIECE, Y_SPLIT)):
                     nc.vector.tensor_copy(out=y_grouped[:, a:b, t], in_=window[t][:, a:b])
         words_out = out_1[0].rearrange("p c l -> p (c l)").bitcast(I32)
-        for a in range(0, TOKENS, 256):
-            nc.vector.quantize_mx(out=y_codes[:, a:a + 256].bitcast(E4M3), scales=y_scales[:, a:a + 256],
-                                  in_=y_grouped[:, a:a + 256, :].rearrange("p c t -> p (c t)"))
-            nc.sync.dma_start(words_out[:, a:a + 256], y_codes[:, a:a + 256].bitcast(I32))
+        for pieces in (((0, 256), (256, 512)), ((512, 768), (768, 896)), ((896, TOKENS),)):
+            first, end = pieces[0][0], pieces[-1][1]
+            y_codes = keep.tile([P, end - first], U32, name="y_codes%d" % first, align_bytes=64)
+            for a, b in pieces:
+                quantize(y_codes[:, a - first:b - first], y_scales[:, a:b], y_grouped[:, a:b, :], E4M3)
+            nc.sync.dma_start(words_out[:, first:end], y_codes[:].bitcast(I32))
         for q in range(4):
-            queue = nc.sync if q == 0 else nc.scalar
+            queue = nc.sync if q < 2 else nc.scalar
             queue.dma_start(out_2[0, 4 * q:4 * q + 4, :].bitcast(I32), y_scales[32 * q:32 * q + 4, :].bitcast(I32))

@@ -22,8 +22,7 @@ SLOTS = 512
 TOKENS = 1024
 PER_COL = 16
 HALF = SLOTS // 2
-DY_SPLIT = 192
-R_SPLIT = 44
+DY_SPLIT = 128
 S_SPLIT = 384
 V_HEAD = 64
 Y_SPLIT = 576
@@ -94,22 +93,17 @@ def tile_attend_greft_pl_kernel(tc, dyT, R, W, ck, offs, out_0, out_1, out_2):
         r_scales = keep.tile([P, LANES, P], U8, name="r_scales", align_bytes=64)
         r_columns = [r_raw[g][:].rearrange("p j (m t) -> p m j t", t=LANES) for g in range(2)]
         u_bank = [psum.tile([P, SLOTS], F32, name="u_bank%d" % t, tag="bank%d" % t) for t in range(LANES)]
-        for h in range(2):
-            r_grouped = keep.tile([P, 2, P, LANES], BF16, name="r_grouped%d" % h, tag="r_then_w", align_bytes=64)
-            if h == 0:
-                shares = ((0, 0, 64, nc.scalar.copy), (1, 0, 64, nc.scalar.copy))
-            else:
-                shares = ((0, 0, R_SPLIT, nc.scalar.copy), (1, 0, 64, nc.vector.tensor_copy), (0, R_SPLIT, 64, nc.vector.tensor_copy))
-            for g, a, b, copy in shares:
-                copy(out=r_grouped[:, :, 64 * g + a:64 * g + b, :].rearrange("p e m j -> p m j e"),
-                     in_=r_columns[g][:, a:b, :, 2 * h:2 * h + 2])
-            for e in range(2):
-                t = 2 * h + e
-                quantize(r_codes[:, t, :], r_scales[:, t, :], r_grouped[:, e, :, :], E4M3)
-                nc.tensor.matmul_mx(out=u_bank[t][:], lhsT=r_codes[:, t, :].bitcast(E4M3), lhsT_scale=r_scales[:, t, :],
-                                    rhs=dy_codes[:].bitcast(E5M2), rhs_scale=dy_scales[:], start=True, stop=True)
+        r_grouped = [keep.tile([P, 2, P, LANES], BF16, name="r_grouped%d" % h, align_bytes=64) for h in range(2)]
+        for g in range(2):
+            for h in range(2):
+                nc.scalar.copy(out=r_grouped[h][:, :, 64 * g:64 * g + 64, :].rearrange("p e m j -> p m j e"),
+                               in_=r_columns[g][:, :, :, 2 * h:2 * h + 2])
+        for t in range(LANES):
+            quantize(r_codes[:, t, :], r_scales[:, t, :], r_grouped[t // 2][:, t % 2, :, :], E4M3)
+            nc.tensor.matmul_mx(out=u_bank[t][:], lhsT=r_codes[:, t, :].bitcast(E4M3), lhsT_scale=r_scales[:, t, :],
+                                rhs=dy_codes[:].bitcast(E5M2), rhs_scale=dy_scales[:], start=True, stop=True)
 
-        w_sorted = [keep.tile([P, K], BF16, name="w_sorted%d" % t, tag="r_then_w" if t == order[1] else "w_sorted%d" % t, align_bytes=64)
+        w_sorted = [keep.tile([P, K], BF16, name="w_sorted%d" % t, tag="r_grouped1" if t == order[1] else "w_sorted%d" % t, align_bytes=64)
                     for t in range(LANES)]
         for t in order:
             w_plane = w_first[:] if t == 0 else w_rest[:, t - 1, :]
@@ -162,6 +156,7 @@ def tile_attend_greft_pl_kernel(tc, dyT, R, W, ck, offs, out_0, out_1, out_2):
                 nc.scalar.copy(out=v_sb[:, t, a:b], in_=v_bank[:, a:b])
 
         y_grouped = keep.tile([P, TOKENS, LANES], BF16, name="y_grouped", tag="s_then_y", align_bytes=64)
+        y_codes = keep.tile([P, TOKENS], U32, name="y_codes", align_bytes=64)
         y_scales = keep.tile([P, TOKENS], U8, name="y_scales", align_bytes=64)
         for n, t in enumerate(order):
             for a, b in (((0, V_HEAD), (V_HEAD, SLOTS)) if n == 0 else ((0, SLOTS),)):
@@ -175,17 +170,14 @@ def tile_attend_greft_pl_kernel(tc, dyT, R, W, ck, offs, out_0, out_1, out_2):
             elif n < last:
                 nc.scalar.copy(out=y_grouped[:, :, t], in_=window[t][:])
             else:
-                for a, b in ((Y_SPLIT, 768), (768, 896), (896, TOKENS)):
+                for a, b in ((Y_SPLIT, TOKENS - Y_PIECE), (TOKENS - Y_PIECE, TOKENS)):
                     nc.scalar.copy(out=y_grouped[:, a:b, t], in_=window[t][:, a:b])
                 for a, b in ((0, Y_PIECE), (Y_PIECE, Y_SPLIT)):
                     nc.vector.tensor_copy(out=y_grouped[:, a:b, t], in_=window[t][:, a:b])
         words_out = out_1[0].rearrange("p c l -> p (c l)").bitcast(I32)
-        for pieces in (((0, 256), (256, 512)), ((512, 768), (768, 896)), ((896, TOKENS),)):
-            first, end = pieces[0][0], pieces[-1][1]
-            y_codes = keep.tile([P, end - first], U32, name="y_codes%d" % first, align_bytes=64)
-            for a, b in pieces:
-                quantize(y_codes[:, a - first:b - first], y_scales[:, a:b], y_grouped[:, a:b, :], E4M3)
-            nc.sync.dma_start(words_out[:, first:end], y_codes[:].bitcast(I32))
+        for a in range(0, TOKENS, Y_PIECE):
+            quantize(y_codes[:, a:a + Y_PIECE], y_scales[:, a:a + Y_PIECE], y_grouped[:, a:a + Y_PIECE, :], E4M3)
+            nc.sync.dma_start(words_out[:, a:a + Y_PIECE], y_codes[:, a:a + Y_PIECE].bitcast(I32))
         for q in range(4):
             queue = nc.sync if q < 2 else nc.scalar
             queue.dma_start(out_2[0, 4 * q:4 * q + 4, :].bitcast(I32), y_scales[32 * q:32 * q + 4, :].bitcast(I32))

@@ -13,6 +13,7 @@ E4M3 = mybir.dt.float8_e4m3fn_x4
 E5M2 = mybir.dt.float8_e5m2_x4
 COPY = mybir.ActivationFunctionType.Copy
 ADD = mybir.AluOpType.add
+MULT = mybir.AluOpType.mult
 
 P = 128
 LANES = 4
@@ -22,8 +23,10 @@ SLOTS = 512
 TOKENS = 1024
 PER_COL = 16
 HALF = SLOTS // 2
-DY_SPLIT = 128
+RUN = 8
+GROUP = 128
 S_SPLIT = 384
+S_FIRST = SLOTS - GROUP
 V_HEAD = 64
 Y_SPLIT = 576
 Y_PIECE = 256
@@ -47,22 +50,27 @@ def tile_attend_greft_pl_kernel(tc, dyT, R, W, ck, offs, out_0, out_1, out_2):
         source = [keep.tile([P, TOKENS], F32, name="source%d" % t) for t in range(LANES)]
         for t in range(LANES):
             nc.sync.dma_start(source[t][:], dy_planes[:, t, :])
-        r_rows = R.rearrange("(p j) k -> p j k", j=LANES)
-        r_raw = [keep.tile([P, LANES, K // 2], F32, name="r_raw%d" % g) for g in range(2)]
-        for g in range(2):
-            nc.sync.dma_start(r_raw[g][:], r_rows[:, :, g * K // 2:(g + 1) * K // 2])
-        ck_sb = keep.tile([P, LANES], F32, name="ck_sb")
-        nc.sync.dma_start(ck_sb[:], ck.rearrange("(p t) o -> p (t o)", t=LANES))
-        w_first = keep.tile([P, K], F32, name="w_first")
-        nc.sync.dma_start(w_first[:], w_planes[:, 0, :])
-        w_rest = keep.tile([P, LANES - 1, K], F32, name="w_rest")
-        nc.sync.dma_start(w_rest[:], w_planes[:, 1:LANES, :])
+        r_raw = keep.tile([P, LANES, K], F32, name="r_raw")
+        nc.sync.dma_start(r_raw[:], R.rearrange("(p j) k -> p j k", j=LANES))
+        ck_rows = keep.tile([P, P], F32, name="ck_rows")
+        nc.gpsimd.memset(ck_rows[:], 0.0)
+        nc.sync.dma_start(ck_rows[0:LANES, :].rearrange("t (b i) -> t b i", i=RUN),
+                          ck.rearrange("(b t i) o -> t b (i o)", t=LANES, i=RUN))
+        w_raw = [keep.tile([P, K], F32, name="w_raw%d" % t, tag="s_turns" if t == order[LANES - 1] else "w_raw%d" % t, align_bytes=64)
+                 for t in range(LANES)]
+        for t in order:
+            nc.sync.dma_start(w_raw[t][:], w_planes[:, t, :])
         window = [keep.tile([P, TOKENS], F32, name="window%d" % t) for t in range(LANES)]
         for t in order:
             nc.sync.dma_start(window[t][:], dy_planes[:, t, :])
 
         ident = keep.tile([P, P], F32, name="ident")
         make_identity(nc, ident[:])
+
+        ck_bank = psum.tile([P, P], F32, name="ck_bank", tag="bank7")
+        nc.tensor.transpose(ck_bank[:], ck_rows[:], ident[:])
+        ck_sb = keep.tile([P, LANES], F32, name="ck_sb")
+        nc.scalar.copy(out=ck_sb[:], in_=ck_bank[:, 0:LANES])
 
         def slot_offsets(a, b):
             return offsets[:, a // PER_COL:b // PER_COL]
@@ -75,47 +83,50 @@ def tile_attend_greft_pl_kernel(tc, dyT, R, W, ck, offs, out_0, out_1, out_2):
 
         picked = keep.tile([P, LANES, SLOTS], F32, name="picked")
         dy_grouped = keep.tile([P, SLOTS, LANES], BF16, name="dy_grouped", align_bytes=64)
-        dy_codes = keep.tile([P, SLOTS], U32, name="dy_codes", align_bytes=64)
-        dy_scales = keep.tile([P, SLOTS], U8, name="dy_scales", align_bytes=64)
+        codes = keep.tile([P, S_FIRST + SLOTS], U32, name="codes", tag="codes_then_y", align_bytes=64)
+        scales = keep.tile([P, S_FIRST + SLOTS], U8, name="scales", align_bytes=64)
         last = LANES - 1
+
+        def gather(t, a, b):
+            nc.vector.tensor_copy(picked[:, t, a:b], source[t][:].indirect(slot_offsets(a, b)))
+
         for t in range(last):
-            nc.vector.tensor_copy(picked[:, t, :], source[t][:].indirect(offsets[:]))
+            gather(t, 0, SLOTS)
             if t == 1:
-                weave(nc.scalar.copy, dy_grouped[:, DY_SPLIT:SLOTS, 0:2], picked[:, 0:2, DY_SPLIT:SLOTS])
-        for a, b in ((0, DY_SPLIT), (DY_SPLIT, SLOTS)):
-            nc.vector.tensor_copy(picked[:, last, a:b], source[last][:].indirect(slot_offsets(a, b)))
-        weave(nc.scalar.copy, dy_grouped[:, 0:DY_SPLIT, :], picked[:, :, 0:DY_SPLIT])
-        weave(nc.vector.tensor_copy, dy_grouped[:, DY_SPLIT:SLOTS, 2:4], picked[:, 2:4, DY_SPLIT:SLOTS])
-        for a in (0, HALF):
-            quantize(dy_codes[:, a:a + HALF], dy_scales[:, a:a + HALF], dy_grouped[:, a:a + HALF, :], E5M2)
+                weave(nc.scalar.copy, dy_grouped[:, GROUP:SLOTS, 0:2], picked[:, 0:2, GROUP:SLOTS])
+        for a, b in ((0, GROUP), (GROUP, HALF), (HALF, SLOTS)):
+            gather(last, a, b)
+        weave(nc.scalar.copy, dy_grouped[:, 0:GROUP, :], picked[:, :, 0:GROUP])
+        weave(nc.scalar.copy, dy_grouped[:, GROUP:HALF, 2:4], picked[:, 2:4, GROUP:HALF])
+        weave(nc.vector.tensor_copy, dy_grouped[:, HALF:SLOTS, 2:4], picked[:, 2:4, HALF:SLOTS])
+        for a, b in ((0, GROUP), (GROUP, HALF), (HALF, SLOTS)):
+            quantize(codes[:, a:b], scales[:, a:b], dy_grouped[:, a:b, :], E5M2)
 
         r_codes = keep.tile([P, LANES, P], U32, name="r_codes", align_bytes=64)
         r_scales = keep.tile([P, LANES, P], U8, name="r_scales", align_bytes=64)
-        r_columns = [r_raw[g][:].rearrange("p j (m t) -> p m j t", t=LANES) for g in range(2)]
+        r_columns = r_raw[:].rearrange("p j (b t h i) -> p t b h j i", t=LANES, h=2, i=4)
         u_bank = [psum.tile([P, SLOTS], F32, name="u_bank%d" % t, tag="bank%d" % t) for t in range(LANES)]
-        r_grouped = [keep.tile([P, 2, P, LANES], BF16, name="r_grouped%d" % h, align_bytes=64) for h in range(2)]
-        for g in range(2):
-            for h in range(2):
-                nc.scalar.copy(out=r_grouped[h][:, :, 64 * g:64 * g + 64, :].rearrange("p e m j -> p m j e"),
-                               in_=r_columns[g][:, :, :, 2 * h:2 * h + 2])
+        r_grouped = {}
+
+        def deal(copy, t, tag):
+            r_grouped[t] = keep.tile([P, P, LANES], BF16, name="r_grouped%d" % t, tag=tag, align_bytes=64)
+            copy(out=r_grouped[t][:].rearrange("p (b h i) j -> p b h j i", h=2, i=4), in_=r_columns[:, t])
+
+        deal(nc.scalar.copy, 0, "r_even")
+        deal(nc.scalar.copy, 1, "r_second")
+        deal(nc.scalar.copy, 3, "r_then_w")
         for t in range(LANES):
-            quantize(r_codes[:, t, :], r_scales[:, t, :], r_grouped[t // 2][:, t % 2, :, :], E4M3)
+            quantize(r_codes[:, t, :], r_scales[:, t, :], r_grouped[t][:], E4M3)
             nc.tensor.matmul_mx(out=u_bank[t][:], lhsT=r_codes[:, t, :].bitcast(E4M3), lhsT_scale=r_scales[:, t, :],
-                                rhs=dy_codes[:].bitcast(E5M2), rhs_scale=dy_scales[:], start=True, stop=True)
+                                rhs=codes[:, 0:SLOTS].bitcast(E5M2), rhs_scale=scales[:, 0:SLOTS], start=True, stop=True)
+            if t == 0:
+                deal(nc.vector.tensor_copy, 2, "r_even")
 
-        w_sorted = [keep.tile([P, K], BF16, name="w_sorted%d" % t, tag="r_grouped1" if t == order[1] else "w_sorted%d" % t, align_bytes=64)
-                    for t in range(LANES)]
-        for t in order:
-            w_plane = w_first[:] if t == 0 else w_rest[:, t - 1, :]
-            copy = nc.scalar.copy if t == 0 else nc.vector.tensor_copy
-            copy(out=w_sorted[t][:].rearrange("m (u p e) -> m u p e", u=2, e=2),
-                 in_=w_plane.rearrange("m (p u e) -> m u p e", u=2, e=2))
-
-        s_planes = keep.tile([P, LANES, SLOTS], BF16, name="s_planes", align_bytes=64)
-        s_pieces = ((0, 128), (128, 256), (256, SLOTS))
-        for t in range(LANES):
-            for a, b in (s_pieces if t == last else ((0, SLOTS),)):
-                nc.scalar.activation(out=s_planes[:, t, a:b], in_=u_bank[t][:, a:b], func=COPY, scale=ck_sb[:, t:t + 1])
+        w_sorted = [keep.tile([P, K], BF16, name="w_sorted%d" % n, tag="r_then_w" if n == 0 else "w_sorted%d" % n, align_bytes=64)
+                    for n in range(LANES)]
+        for n, t in enumerate(order):
+            nc.vector.tensor_copy(out=w_sorted[n][:].rearrange("m (u b i e) -> m u b i e", u=2, i=RUN, e=2),
+                                  in_=w_raw[t][:].rearrange("m (b u e i) -> m u b i e", u=2, i=RUN, e=2))
 
         w_codes = keep.tile([P, LANES * P], U32, name="w_codes", align_bytes=64)
         w_scales = keep.tile([P, LANES * P], U8, name="w_scales", align_bytes=64)
@@ -123,43 +134,70 @@ def tile_attend_greft_pl_kernel(tc, dyT, R, W, ck, offs, out_0, out_1, out_2):
         def turn_w(first, count, bank, grouped):
             turned = psum.tile([P, count, 2, P], F32, name="turned%d" % first, tag=bank)
             for n in range(count):
-                words = w_sorted[order[first + n]][:].bitcast(F32)
+                words = w_sorted[first + n][:].bitcast(F32)
                 for u in range(2):
                     nc.tensor.transpose(turned[:, n, u, :], words[:, u * P:(u + 1) * P], ident[:])
             nc.scalar.copy(out=grouped.rearrange("p m t -> p (m t)").bitcast(F32).rearrange("p (n m u) -> p n m u", n=count, u=2),
                            in_=turned[:].rearrange("p n u m -> p n m u"))
 
-        s_grouped = keep.tile([P, SLOTS, LANES], BF16, name="s_grouped", align_bytes=64)
-        s_codes = keep.tile([P, SLOTS], U32, name="s_codes", tag="s_then_y", align_bytes=64)
-        s_scales = keep.tile([P, SLOTS], U8, name="s_scales", align_bytes=64)
-        w_head = keep.tile([P, P, LANES], BF16, name="w_head", align_bytes=64)
-        turn_w(0, 1, "bank1", w_head[:])
-        for a in range(0, S_SPLIT, 128):
-            weave(nc.vector.tensor_copy, s_grouped[:, a:a + 128, :], s_planes[:, :, a:a + 128])
-        weave(nc.scalar.copy, s_grouped[:, S_SPLIT:SLOTS, :], s_planes[:, :, S_SPLIT:SLOTS])
-        quantize(w_codes[:, 0:P], w_scales[:, 0:P], w_head[:], E4M3)
-        for a in (0, HALF):
-            quantize(s_codes[:, a:a + HALF], s_scales[:, a:a + HALF], s_grouped[:, a:a + HALF, :], E5M2)
+        s_planes = keep.tile([P, LANES, SLOTS], BF16, name="s_planes", align_bytes=64)
+        s_grouped = keep.tile([P, HALF + GROUP, LANES], BF16, name="s_grouped", tag="s_turns", align_bytes=64)
+        s_first = s_grouped[:, 0:GROUP, :]
+        s_second = s_grouped[:, HALF:HALF + GROUP, :]
+        s_rest = s_grouped[:, 0:HALF, :]
+        w_head = s_grouped[:, GROUP:HALF, :]
+
+        def scale_u(t, a, b):
+            if t == 2:
+                nc.vector.tensor_scalar(s_planes[:, t, a:b], u_bank[t][:, a:b], ck_sb[:, t:t + 1], None, MULT)
+            else:
+                nc.scalar.activation(out=s_planes[:, t, a:b], in_=u_bank[t][:, a:b], func=COPY, scale=ck_sb[:, t:t + 1])
+
+        def quantize_s(a, b, grouped):
+            quantize(codes[:, S_FIRST + a:S_FIRST + b], scales[:, S_FIRST + a:S_FIRST + b], grouped, E5M2)
+
+        def second_product(bank, n, a):
+            nc.tensor.matmul_mx(out=bank[:], lhsT=w_codes[:, n * P:(n + 1) * P].bitcast(E4M3),
+                                lhsT_scale=w_scales[:, n * P:(n + 1) * P],
+                                rhs=codes[:, a:a + SLOTS].bitcast(E5M2), rhs_scale=scales[:, a:a + SLOTS], start=True, stop=True)
+
+        for t in range(last):
+            scale_u(t, 0, SLOTS)
+        scale_u(last, 0, GROUP)
+        turn_w(0, 1, "bank4", w_head)
+        scale_u(last, GROUP, HALF)
+        scale_u(last, HALF, SLOTS)
+        weave(nc.vector.tensor_copy, s_first, s_planes[:, :, 0:GROUP])
+        weave(nc.vector.tensor_copy, s_second, s_planes[:, :, GROUP:HALF])
+        quantize(w_codes[:, 0:P], w_scales[:, 0:P], w_head, E4M3)
+        quantize_s(0, GROUP, s_first)
+        v_sb = keep.tile([P, LANES, SLOTS], F32, name="v_sb")
+        early_bank = psum.tile([P, SLOTS], F32, name="early_bank", tag="bank7")
+        second_product(early_bank, 0, 0)
+        weave(nc.vector.tensor_copy, s_rest[:, 0:S_SPLIT - HALF, :], s_planes[:, :, HALF:S_SPLIT])
+        weave(nc.scalar.copy, s_rest[:, S_SPLIT - HALF:HALF, :], s_planes[:, :, S_SPLIT:SLOTS])
+        quantize_s(GROUP, HALF, s_second)
+        quantize_s(HALF, SLOTS, s_rest)
         w_late = keep.tile([P, 3 * P, LANES], BF16, name="w_late", tag="s_planes", align_bytes=64)
-        turn_w(1, 2, "bank5", w_late[:, 0:2 * P, :])
-        turn_w(3, 1, "bank7", w_late[:, 2 * P:3 * P, :])
+        turn_w(1, 2, "bank1", w_late[:, 0:2 * P, :])
+        nc.scalar.copy(out=v_sb[:, order[0], 0:GROUP], in_=early_bank[:, S_FIRST:SLOTS])
+        turn_w(3, 1, "bank0", w_late[:, 2 * P:3 * P, :])
         quantize(w_codes[:, P:3 * P], w_scales[:, P:3 * P], w_late[:, 0:2 * P, :], E4M3)
+        nc.vector.tensor_tensor(window[order[0]][:].indirect(slot_offsets(0, GROUP)), picked[:, order[0], 0:GROUP], v_sb[:, order[0], 0:GROUP], ADD)
         quantize(w_codes[:, 3 * P:4 * P], w_scales[:, 3 * P:4 * P], w_late[:, 2 * P:3 * P, :], E4M3)
 
-        v_sb = keep.tile([P, LANES, SLOTS], F32, name="v_sb")
+        first_pieces = ((GROUP, SLOTS),)
         for n, t in enumerate(order):
-            v_bank = psum.tile([P, SLOTS], F32, name="v_bank%d" % n, tag="bank%d" % (LANES + n))
-            nc.tensor.matmul_mx(out=v_bank[:], lhsT=w_codes[:, n * P:(n + 1) * P].bitcast(E4M3),
-                                lhsT_scale=w_scales[:, n * P:(n + 1) * P],
-                                rhs=s_codes[:].bitcast(E5M2), rhs_scale=s_scales[:], start=True, stop=True)
-            for a, b in (((0, V_HEAD), (V_HEAD, SLOTS)) if n == 0 else ((0, SLOTS),)):
+            v_bank = psum.tile([P, SLOTS], F32, name="v_bank%d" % n, tag="bank%d" % (5, 6, 2, 3)[n])
+            second_product(v_bank, n, S_FIRST)
+            for a, b in (first_pieces if n == 0 else ((0, SLOTS),)):
                 nc.scalar.copy(out=v_sb[:, t, a:b], in_=v_bank[:, a:b])
 
-        y_grouped = keep.tile([P, TOKENS, LANES], BF16, name="y_grouped", tag="s_then_y", align_bytes=64)
+        y_grouped = keep.tile([P, TOKENS, LANES], BF16, name="y_grouped", tag="codes_then_y", align_bytes=64)
         y_codes = keep.tile([P, TOKENS], U32, name="y_codes", align_bytes=64)
         y_scales = keep.tile([P, TOKENS], U8, name="y_scales", align_bytes=64)
         for n, t in enumerate(order):
-            for a, b in (((0, V_HEAD), (V_HEAD, SLOTS)) if n == 0 else ((0, SLOTS),)):
+            for a, b in (first_pieces if n == 0 else ((0, SLOTS),)):
                 nc.vector.tensor_tensor(window[t][:].indirect(slot_offsets(a, b)), picked[:, t, a:b], v_sb[:, t, a:b], ADD)
             nc.sync.dma_start(out_planes[:, t, :], window[t][:])
             if n == 0:

@@ -53,9 +53,9 @@ def tile_attend_greft_pl_kernel(tc, dyT, R, W, ck, offs, out_0, out_1, out_2):
         r_raw = keep.tile([P, LANES, K], F32, name="r_raw")
         nc.sync.dma_start(r_raw[:], R.rearrange("(p j) k -> p j k", j=LANES))
         ck_rows = keep.tile([P, P], F32, name="ck_rows")
-        nc.gpsimd.memset(ck_rows[:], 0.0)
-        nc.sync.dma_start(ck_rows[0:LANES, :].rearrange("t (b i) -> t b i", i=RUN),
-                          ck.rearrange("(b t i) o -> t b (i o)", t=LANES, i=RUN))
+        nc.vector.memset(ck_rows[:], 0.0)
+        nc.scalar.dma_start(ck_rows[0:LANES, :].rearrange("t (b i) -> t b i", i=RUN),
+                            ck.rearrange("(b t i) o -> t b (i o)", t=LANES, i=RUN))
         w_raw = [keep.tile([P, K], F32, name="w_raw%d" % t, tag="s_turns" if t == order[LANES - 1] else "w_raw%d" % t, align_bytes=64)
                  for t in range(LANES)]
         for t in order:

@@ -25,6 +25,7 @@ PER_COL = 16
 HALF = SLOTS // 2
 RUN = 8
 GROUP = 128
+LAP = 8
 S_SPLIT = 384
 S_FIRST = SLOTS - GROUP
 V_HEAD = 64
@@ -81,6 +82,12 @@ def tile_attend_greft_pl_kernel(tc, dyT, R, W, ck, offs, out_0, out_1, out_2):
         def quantize(codes, scales, grouped, fmt):
             nc.vector.quantize_mx(out=codes.bitcast(fmt), scales=scales, in_=grouped.rearrange("p c t -> p (c t)"))
 
+        warm_values = keep.tile([P, SLOTS, LANES], BF16, name="warm_values", align_bytes=64)
+        warm_codes = keep.tile([P, SLOTS], U32, name="warm_codes", align_bytes=64)
+        warm_scales = keep.tile([P, SLOTS], U8, name="warm_scales", align_bytes=64)
+        nc.vector.memset(warm_values[:].rearrange("p c t -> p (c t)").bitcast(F32), 1.0)
+        quantize(warm_codes[:], warm_scales[:], warm_values[:], E4M3)
+
         picked = keep.tile([P, LANES, SLOTS], F32, name="picked")
         dy_grouped = keep.tile([P, SLOTS, LANES], BF16, name="dy_grouped", align_bytes=64)
         codes = keep.tile([P, S_FIRST + SLOTS], U32, name="codes", tag="codes_then_y", align_bytes=64)
@@ -93,14 +100,23 @@ def tile_attend_greft_pl_kernel(tc, dyT, R, W, ck, offs, out_0, out_1, out_2):
         for t in range(last):
             gather(t, 0, SLOTS)
             if t == 1:
-                weave(nc.scalar.copy, dy_grouped[:, GROUP:SLOTS, 0:2], picked[:, 0:2, GROUP:SLOTS])
-        for a, b in ((0, GROUP), (GROUP, HALF), (HALF, SLOTS)):
+                for a, b in ((0, GROUP), (HALF + LAP, SLOTS)):
+                    weave(nc.scalar.copy, dy_grouped[:, a:b, 0:2], picked[:, 0:2, a:b])
+        for a, b in ((GROUP, HALF + 2 * PER_COL), (0, GROUP), (HALF + 2 * PER_COL, SLOTS)):
             gather(last, a, b)
-        weave(nc.scalar.copy, dy_grouped[:, 0:GROUP, :], picked[:, :, 0:GROUP])
-        weave(nc.scalar.copy, dy_grouped[:, GROUP:HALF, 2:4], picked[:, 2:4, GROUP:HALF])
-        weave(nc.vector.tensor_copy, dy_grouped[:, HALF:SLOTS, 2:4], picked[:, 2:4, HALF:SLOTS])
-        for a, b in ((0, GROUP), (GROUP, HALF), (HALF, SLOTS)):
+
+        def quantize_dy(a, b):
             quantize(codes[:, a:b], scales[:, a:b], dy_grouped[:, a:b, :], E5M2)
+
+        weave(nc.scalar.copy, dy_grouped[:, GROUP:HALF + LAP, :], picked[:, :, GROUP:HALF + LAP])
+        weave(nc.scalar.copy, dy_grouped[:, 0:GROUP, 2:4], picked[:, 2:4, 0:GROUP])
+        quantize_dy(GROUP, HALF)
+        weave(nc.vector.tensor_copy, dy_grouped[:, HALF:SLOTS, 2:4], picked[:, 2:4, HALF:SLOTS])
+        quantize_dy(0, GROUP)
+        quantize_dy(HALF, SLOTS)
+        warm_bank = psum.tile([P, SLOTS], F32, name="warm_bank", tag="bank6")
+        nc.tensor.matmul_mx(out=warm_bank[:], lhsT=codes[:, 0:GROUP].bitcast(E5M2), lhsT_scale=scales[:, 0:GROUP],
+                            rhs=warm_codes[:].bitcast(E4M3), rhs_scale=warm_scales[:], start=True, stop=True)
 
         r_codes = keep.tile([P, LANES, P], U32, name="r_codes", align_bytes=64)
         r_scales = keep.tile([P, LANES, P], U8, name="r_scales", align_bytes=64)

@@ -53,10 +53,8 @@ def tile_attend_greft_pl_kernel(tc, dyT, R, W, ck, offs, out_0, out_1, out_2):
             nc.sync.dma_start(source[t][:], dy_planes[:, t, :])
         r_raw = keep.tile([P, LANES, K], F32, name="r_raw")
         nc.sync.dma_start(r_raw[:], R.rearrange("(p j) k -> p j k", j=LANES))
-        ck_rows = keep.tile([P, P], F32, name="ck_rows")
-        nc.vector.memset(ck_rows[:], 0.0)
-        nc.scalar.dma_start(ck_rows[0:LANES, :].rearrange("t (b i) -> t b i", i=RUN),
-                            ck.rearrange("(b t i) o -> t b (i o)", t=LANES, i=RUN))
+        ck_line = keep.tile([1, K], F32, name="ck_line")
+        nc.scalar.dma_start(ck_line[:], ck.rearrange("k o -> o k"))
         w_raw = [keep.tile([P, K], F32, name="w_raw%d" % t, tag="s_turns" if t == order[LANES - 1] else "w_raw%d" % t, align_bytes=64)
                  for t in range(LANES)]
         for t in order:
@@ -68,10 +66,13 @@ def tile_attend_greft_pl_kernel(tc, dyT, R, W, ck, offs, out_0, out_1, out_2):
         ident = keep.tile([P, P], F32, name="ident")
         make_identity(nc, ident[:])
 
-        ck_bank = psum.tile([P, P], F32, name="ck_bank", tag="bank7")
-        nc.tensor.transpose(ck_bank[:], ck_rows[:], ident[:])
-        ck_sb = keep.tile([P, LANES], F32, name="ck_sb")
-        nc.scalar.copy(out=ck_sb[:], in_=ck_bank[:, 0:LANES])
+        ck_dealt = keep.tile([P, K], F32, name="ck_dealt")
+        nc.vector.memset(ck_dealt[:], 0.0)
+        nc.gpsimd.tensor_copy(out=ck_dealt[0:1, :].rearrange("o (t b i) -> o t b i", t=LANES, i=RUN),
+                              in_=ck_line[:].rearrange("o (b t i) -> o t b i", t=LANES, i=RUN))
+        ck_bank = psum.tile([P, LANES, P], F32, name="ck_bank", tag="bank7")
+        for t in range(LANES):
+            nc.tensor.transpose(ck_bank[:, t, :], ck_dealt[:, t * P:(t + 1) * P], ident[:])
 
         def slot_offsets(a, b):
             return offsets[:, a // PER_COL:b // PER_COL]
@@ -137,6 +138,9 @@ def tile_attend_greft_pl_kernel(tc, dyT, R, W, ck, offs, out_0, out_1, out_2):
                                 rhs=codes[:, 0:SLOTS].bitcast(E5M2), rhs_scale=scales[:, 0:SLOTS], start=True, stop=True)
             if t == 0:
                 deal(nc.vector.tensor_copy, 2, "r_even")
+
+        ck_sb = keep.tile([P, LANES], F32, name="ck_sb", tag="r_second", align_bytes=64)
+        nc.scalar.copy(out=ck_sb[:], in_=ck_bank[:, :, 0])
 
         w_sorted = [keep.tile([P, K], BF16, name="w_sorted%d" % n, tag="r_then_w" if n == 0 else "w_sorted%d" % n, align_bytes=64)
                     for n in range(LANES)]

@@ -68,8 +68,8 @@ def tile_attend_greft_pl_kernel(tc, dyT, R, W, ck, offs, out_0, out_1, out_2):
 
         ck_dealt = keep.tile([P, K], F32, name="ck_dealt")
         nc.vector.memset(ck_dealt[:], 0.0)
-        nc.gpsimd.tensor_copy(out=ck_dealt[0:1, :].rearrange("o (t b i) -> o t b i", t=LANES, i=RUN),
-                              in_=ck_line[:].rearrange("o (b t i) -> o t b i", t=LANES, i=RUN))
+        nc.gpsimd.tensor_scalar(ck_dealt[0:1, :].rearrange("o (t b i) -> o t b i", t=LANES, i=RUN),
+                                ck_line[:].rearrange("o (b t i) -> o t b i", t=LANES, i=RUN), 1.0, 0.0, MULT, ADD)
         ck_bank = psum.tile([P, LANES, P], F32, name="ck_bank", tag="bank7")
         for t in range(LANES):
             nc.tensor.transpose(ck_bank[:, t, :], ck_dealt[:, t * P:(t + 1) * P], ident[:])
@@ -83,11 +83,12 @@ def tile_attend_greft_pl_kernel(tc, dyT, R, W, ck, offs, out_0, out_1, out_2):
         def quantize(codes, scales, grouped, fmt):
             nc.vector.quantize_mx(out=codes.bitcast(fmt), scales=scales, in_=grouped.rearrange("p c t -> p (c t)"))
 
-        warm_values = keep.tile([P, SLOTS, LANES], BF16, name="warm_values", align_bytes=64)
+        warm_values = keep.tile([P, GROUP, LANES], BF16, name="warm_values", align_bytes=64)
         warm_codes = keep.tile([P, SLOTS], U32, name="warm_codes", align_bytes=64)
         warm_scales = keep.tile([P, SLOTS], U8, name="warm_scales", align_bytes=64)
         nc.vector.memset(warm_values[:].rearrange("p c t -> p (c t)").bitcast(F32), 1.0)
-        quantize(warm_codes[:], warm_scales[:], warm_values[:], E4M3)
+        for a in range(0, SLOTS, GROUP):
+            quantize(warm_codes[:, a:a + GROUP], warm_scales[:, a:a + GROUP], warm_values[:], E4M3)
 
         picked = keep.tile([P, LANES, SLOTS], F32, name="picked")
         dy_grouped = keep.tile([P, SLOTS, LANES], BF16, name="dy_grouped", align_bytes=64)

@@ -83,13 +83,6 @@ def tile_attend_greft_pl_kernel(tc, dyT, R, W, ck, offs, out_0, out_1, out_2):
         def quantize(codes, scales, grouped, fmt):
             nc.vector.quantize_mx(out=codes.bitcast(fmt), scales=scales, in_=grouped.rearrange("p c t -> p (c t)"))
 
-        warm_values = keep.tile([P, GROUP, LANES], BF16, name="warm_values", align_bytes=64)
-        warm_codes = keep.tile([P, SLOTS], U32, name="warm_codes", align_bytes=64)
-        warm_scales = keep.tile([P, SLOTS], U8, name="warm_scales", align_bytes=64)
-        nc.vector.memset(warm_values[:].rearrange("p c t -> p (c t)").bitcast(F32), 1.0)
-        for a in range(0, SLOTS, GROUP):
-            quantize(warm_codes[:, a:a + GROUP], warm_scales[:, a:a + GROUP], warm_values[:], E4M3)
-
         picked = keep.tile([P, LANES, SLOTS], F32, name="picked")
         dy_grouped = keep.tile([P, SLOTS, LANES], BF16, name="dy_grouped", align_bytes=64)
         codes = keep.tile([P, S_FIRST + SLOTS], U32, name="codes", tag="codes_then_y", align_bytes=64)
@@ -116,9 +109,6 @@ def tile_attend_greft_pl_kernel(tc, dyT, R, W, ck, offs, out_0, out_1, out_2):
         weave(nc.vector.tensor_copy, dy_grouped[:, HALF:SLOTS, 2:4], picked[:, 2:4, HALF:SLOTS])
         quantize_dy(0, GROUP)
         quantize_dy(HALF, SLOTS)
-        warm_bank = psum.tile([P, SLOTS], F32, name="warm_bank", tag="bank6")
-        nc.tensor.matmul_mx(out=warm_bank[:], lhsT=codes[:, 0:GROUP].bitcast(E5M2), lhsT_scale=scales[:, 0:GROUP],
-                            rhs=warm_codes[:].bitcast(E4M3), rhs_scale=warm_scales[:], start=True, stop=True)
 
         r_codes = keep.tile([P, LANES, P], U32, name="r_codes", align_bytes=64)
         r_scales = keep.tile([P, LANES, P], U8, name="r_scales", align_bytes=64)

@@ -25,12 +25,9 @@ PER_COL = 16
 HALF = SLOTS // 2
 RUN = 8
 GROUP = 128
-LAP = 8
-S_SPLIT = 384
-S_FIRST = SLOTS - GROUP
-V_HEAD = 64
-Y_SPLIT = 576
-Y_PIECE = 256
+GROUPS = SLOTS // GROUP
+PIECE = 256
+PIECES = TOKENS // PIECE
 
 FLOPS = 2 * 2 * D * K * SLOTS
 
@@ -44,7 +41,7 @@ def tile_attend_greft_pl_kernel(tc, dyT, R, W, ck, offs, out_0, out_1, out_2):
         dy_planes = dyT.rearrange("(p t) c -> p t c", t=LANES)
         out_planes = out_0.rearrange("(p t) c -> p t c", t=LANES)
         w_planes = W.rearrange("(m t) k -> m t k", t=LANES)
-        order = (0, 2, 3, 1)
+        last = LANES - 1
 
         offsets = keep.tile([P, SLOTS // PER_COL], U16, name="offsets")
         nc.sync.dma_start(offsets[:], offs)
@@ -55,13 +52,13 @@ def tile_attend_greft_pl_kernel(tc, dyT, R, W, ck, offs, out_0, out_1, out_2):
         nc.sync.dma_start(r_raw[:], R.rearrange("(p j) k -> p j k", j=LANES))
         ck_line = keep.tile([1, K], F32, name="ck_line")
         nc.scalar.dma_start(ck_line[:], ck.rearrange("k o -> o k"))
-        w_raw = [keep.tile([P, K], F32, name="w_raw%d" % t, tag="s_turns" if t == order[LANES - 1] else "w_raw%d" % t, align_bytes=64)
-                 for t in range(LANES)]
-        for t in order:
-            nc.sync.dma_start(w_raw[t][:], w_planes[:, t, :])
+        w_sets = ((0, 1), (1, 1), (2, 1), (3, 1))
+        w_raw = {}
+        for t, count in w_sets:
+            w_raw[t] = keep.tile([P, count, K], F32, name="w_raw%d" % t)
+            nc.sync.dma_start(w_raw[t][:], w_planes[:, t:t + count, :])
         window = [keep.tile([P, TOKENS], F32, name="window%d" % t) for t in range(LANES)]
-        for t in order:
-            nc.sync.dma_start(window[t][:], dy_planes[:, t, :])
+        nc.sync.dma_start(window[last][:], dy_planes[:, last, :])
 
         ident = keep.tile([P, P], F32, name="ident")
         make_identity(nc, ident[:])
@@ -83,150 +80,147 @@ def tile_attend_greft_pl_kernel(tc, dyT, R, W, ck, offs, out_0, out_1, out_2):
         def quantize(codes, scales, grouped, fmt):
             nc.vector.quantize_mx(out=codes.bitcast(fmt), scales=scales, in_=grouped.rearrange("p c t -> p (c t)"))
 
+        def group(g):
+            return slice(g * GROUP, (g + 1) * GROUP)
+
         picked = keep.tile([P, LANES, SLOTS], F32, name="picked")
         dy_grouped = keep.tile([P, SLOTS, LANES], BF16, name="dy_grouped", align_bytes=64)
-        codes = keep.tile([P, S_FIRST + SLOTS], U32, name="codes", tag="codes_then_y", align_bytes=64)
-        scales = keep.tile([P, S_FIRST + SLOTS], U8, name="scales", align_bytes=64)
-        last = LANES - 1
-
-        def gather(t, a, b):
-            nc.vector.tensor_copy(picked[:, t, a:b], source[t][:].indirect(slot_offsets(a, b)))
+        dy_codes = keep.tile([P, SLOTS], U32, name="dy_codes", align_bytes=64)
+        dy_scales = keep.tile([P, SLOTS], U8, name="dy_scales", align_bytes=64)
 
         for t in range(last):
-            gather(t, 0, SLOTS)
-            if t == 1:
-                for a, b in ((0, GROUP), (HALF + LAP, SLOTS)):
-                    weave(nc.scalar.copy, dy_grouped[:, a:b, 0:2], picked[:, 0:2, a:b])
-        for a, b in ((GROUP, HALF + 2 * PER_COL), (0, GROUP), (HALF + 2 * PER_COL, SLOTS)):
-            gather(last, a, b)
-
-        def quantize_dy(a, b):
-            quantize(codes[:, a:b], scales[:, a:b], dy_grouped[:, a:b, :], E5M2)
-
-        weave(nc.scalar.copy, dy_grouped[:, GROUP:HALF + LAP, :], picked[:, :, GROUP:HALF + LAP])
-        weave(nc.scalar.copy, dy_grouped[:, 0:GROUP, 2:4], picked[:, 2:4, 0:GROUP])
-        quantize_dy(GROUP, HALF)
-        weave(nc.vector.tensor_copy, dy_grouped[:, HALF:SLOTS, 2:4], picked[:, 2:4, HALF:SLOTS])
-        quantize_dy(0, GROUP)
-        quantize_dy(HALF, SLOTS)
+            nc.vector.tensor_copy(picked[:, t, :], source[t][:].indirect(offsets[:]))
+            nc.scalar.activation(out=window[t][:], in_=source[t][:], func=COPY)
+        for a in (0, GROUP):
+            nc.vector.tensor_copy(picked[:, last, a:a + GROUP], source[last][:].indirect(slot_offsets(a, a + GROUP)))
+        nc.scalar.activation(out=picked[:, last, HALF:SLOTS], in_=source[last][:].indirect(slot_offsets(HALF, SLOTS)), func=COPY)
+        for g in range(GROUPS):
+            weave(nc.vector.tensor_copy if g < 2 else nc.scalar.copy, dy_grouped[:, group(g), :], picked[:, :, group(g)])
+        for g in range(GROUPS):
+            quantize(dy_codes[:, group(g)], dy_scales[:, group(g)], dy_grouped[:, group(g), :], E5M2)
 
         r_codes = keep.tile([P, LANES, P], U32, name="r_codes", align_bytes=64)
         r_scales = keep.tile([P, LANES, P], U8, name="r_scales", align_bytes=64)
         r_columns = r_raw[:].rearrange("p j (b t h i) -> p t b h j i", t=LANES, h=2, i=4)
-        u_bank = [psum.tile([P, SLOTS], F32, name="u_bank%d" % t, tag="bank%d" % t) for t in range(LANES)]
-        r_grouped = {}
-
-        def deal(copy, t, tag):
-            r_grouped[t] = keep.tile([P, P, LANES], BF16, name="r_grouped%d" % t, tag=tag, align_bytes=64)
-            copy(out=r_grouped[t][:].rearrange("p (b h i) j -> p b h j i", h=2, i=4), in_=r_columns[:, t])
-
-        deal(nc.scalar.copy, 0, "r_even")
-        deal(nc.scalar.copy, 1, "r_second")
-        deal(nc.scalar.copy, 3, "r_then_w")
+        r_grouped = [keep.tile([P, P, LANES], BF16, name="r_grouped%d" % t, tag="r_grouped%d" % t, align_bytes=64) for t in range(LANES)]
         for t in range(LANES):
-            quantize(r_codes[:, t, :], r_scales[:, t, :], r_grouped[t][:], E4M3)
-            nc.tensor.matmul_mx(out=u_bank[t][:], lhsT=r_codes[:, t, :].bitcast(E4M3), lhsT_scale=r_scales[:, t, :],
-                                rhs=codes[:, 0:SLOTS].bitcast(E5M2), rhs_scale=scales[:, 0:SLOTS], start=True, stop=True)
-            if t == 0:
-                deal(nc.vector.tensor_copy, 2, "r_even")
+            copy = nc.vector.tensor_copy if t < last else nc.scalar.copy
+            copy(out=r_grouped[t][:].rearrange("p (b h i) j -> p b h j i", h=2, i=4), in_=r_columns[:, t])
+        u_bank = {}
 
-        ck_sb = keep.tile([P, LANES], F32, name="ck_sb", tag="r_second", align_bytes=64)
+        def first_product(g):
+            u_bank[g] = psum.tile([P, LANES, GROUP], F32, name="u_bank%d" % g, tag="bank%d" % (g % 2))
+            for t in range(LANES):
+                if g == 0:
+                    quantize(r_codes[:, t, :], r_scales[:, t, :], r_grouped[t][:], E4M3)
+                nc.tensor.matmul_mx(out=u_bank[g][:, t, :], lhsT=r_codes[:, t, :].bitcast(E4M3), lhsT_scale=r_scales[:, t, :],
+                                    rhs=dy_codes[:, group(g)].bitcast(E5M2), rhs_scale=dy_scales[:, group(g)], start=True, stop=True)
+
+        first_product(0)
+        ck_sb = keep.tile([P, LANES], F32, name="ck_sb", tag="r_grouped0", align_bytes=64)
         nc.scalar.copy(out=ck_sb[:], in_=ck_bank[:, :, 0])
+        ck_spread = ck_sb[:].rearrange("p (o t) -> p o t", o=1).to_broadcast([P, GROUP, LANES])
 
-        w_sorted = [keep.tile([P, K], BF16, name="w_sorted%d" % n, tag="r_then_w" if n == 0 else "w_sorted%d" % n, align_bytes=64)
-                    for n in range(LANES)]
-        for n, t in enumerate(order):
-            nc.vector.tensor_copy(out=w_sorted[n][:].rearrange("m (u b i e) -> m u b i e", u=2, i=RUN, e=2),
-                                  in_=w_raw[t][:].rearrange("m (b u e i) -> m u b i e", u=2, i=RUN, e=2))
+        w_codes = keep.tile([P, LANES, P], U32, name="w_codes", align_bytes=64)
+        w_scales = keep.tile([P, LANES, P], U8, name="w_scales", align_bytes=64)
 
-        w_codes = keep.tile([P, LANES * P], U32, name="w_codes", align_bytes=64)
-        w_scales = keep.tile([P, LANES * P], U8, name="w_scales", align_bytes=64)
+        w_sorted = [keep.tile([P, K], BF16, name="w_sorted%d" % t, align_bytes=64) for t in range(LANES)]
+        for t in range(LANES):
+            nc.scalar.copy(out=w_sorted[t][:].rearrange("m (u b i e) -> m u b e i", u=2, i=RUN, e=2),
+                           in_=w_raw[t][:, 0, :].rearrange("m (b u e i) -> m u b e i", u=2, i=RUN, e=2))
 
-        def turn_w(first, count, bank, grouped):
-            turned = psum.tile([P, count, 2, P], F32, name="turned%d" % first, tag=bank)
+        def turn_w(t, count, bank):
+            turned = psum.tile([P, count, 2, P], F32, name="turned%d" % t, tag=bank)
             for n in range(count):
-                words = w_sorted[first + n][:].bitcast(F32)
+                words = w_sorted[t + n][:].bitcast(F32)
                 for u in range(2):
                     nc.tensor.transpose(turned[:, n, u, :], words[:, u * P:(u + 1) * P], ident[:])
-            nc.scalar.copy(out=grouped.rearrange("p m t -> p (m t)").bitcast(F32).rearrange("p (n m u) -> p n m u", n=count, u=2),
-                           in_=turned[:].rearrange("p n u m -> p n m u"))
+            w_grouped = keep.tile([P, count * P, LANES], BF16, name="w_grouped%d" % t, align_bytes=64)
+            copy = nc.scalar.copy if t < 2 else nc.vector.tensor_copy
+            copy(out=w_grouped[:].rearrange("p m t -> p (m t)").bitcast(F32).rearrange("p (n m u) -> p n m u", n=count, u=2),
+                 in_=turned[:].rearrange("p n u m -> p n m u"))
+            return w_grouped
 
-        s_planes = keep.tile([P, LANES, SLOTS], BF16, name="s_planes", align_bytes=64)
-        s_grouped = keep.tile([P, HALF + GROUP, LANES], BF16, name="s_grouped", tag="s_turns", align_bytes=64)
-        s_first = s_grouped[:, 0:GROUP, :]
-        s_second = s_grouped[:, HALF:HALF + GROUP, :]
-        s_rest = s_grouped[:, 0:HALF, :]
-        w_head = s_grouped[:, GROUP:HALF, :]
+        def quantize_w(t, count, grouped):
+            quantize(w_codes[:, t:t + count, :].rearrange("p n m -> p (n m)"), w_scales[:, t:t + count, :].rearrange("p n m -> p (n m)"),
+                     grouped[:], E4M3)
 
-        def scale_u(t, a, b):
-            if t == 2:
-                nc.vector.tensor_scalar(s_planes[:, t, a:b], u_bank[t][:, a:b], ck_sb[:, t:t + 1], None, MULT)
-            else:
-                nc.scalar.activation(out=s_planes[:, t, a:b], in_=u_bank[t][:, a:b], func=COPY, scale=ck_sb[:, t:t + 1])
+        s_grouped = keep.tile([P, SLOTS, LANES], BF16, name="s_grouped", align_bytes=64)
+        s_codes = keep.tile([P, SLOTS], U32, name="s_codes", align_bytes=64)
+        s_scales = keep.tile([P, SLOTS], U8, name="s_scales", align_bytes=64)
 
-        def quantize_s(a, b, grouped):
-            quantize(codes[:, S_FIRST + a:S_FIRST + b], scales[:, S_FIRST + a:S_FIRST + b], grouped, E5M2)
+        def scale_u(g):
+            nc.vector.tensor_tensor(s_grouped[:, group(g), :], u_bank[g][:].rearrange("p t n -> p n t"), ck_spread, MULT)
 
-        def second_product(bank, n, a):
-            nc.tensor.matmul_mx(out=bank[:], lhsT=w_codes[:, n * P:(n + 1) * P].bitcast(E4M3),
-                                lhsT_scale=w_scales[:, n * P:(n + 1) * P],
-                                rhs=codes[:, a:a + SLOTS].bitcast(E5M2), rhs_scale=scales[:, a:a + SLOTS], start=True, stop=True)
+        def quantize_s(g):
+            quantize(s_codes[:, group(g)], s_scales[:, group(g)], s_grouped[:, group(g), :], E5M2)
 
+        def second_product(out, t, slots):
+            nc.tensor.matmul_mx(out=out, lhsT=w_codes[:, t, :].bitcast(E4M3), lhsT_scale=w_scales[:, t, :],
+                                rhs=s_codes[:, slots].bitcast(E5M2), rhs_scale=s_scales[:, slots], start=True, stop=True)
+
+        def scatter_on_scalar(t, a, b, values):
+            nc.scalar.activation(out=window[t][:].indirect(slot_offsets(a, b)), in_=values, func=COPY)
+
+        new_early = keep.tile([P, GROUPS, 2, GROUP], F32, name="new_early")
+
+        def early_planes(g, first, count, bank):
+            bank = psum.tile([P, count, GROUP], F32, name="v_early%d_%d" % (g, first), tag=bank)
+            for n in range(count):
+                second_product(bank[:, n, :], first + n, group(g))
+            nc.vector.tensor_tensor(new_early[:, g, first:first + count, :], bank[:], picked[:, first:first + count, group(g)], ADD)
+            for t in range(first, first + count):
+                scatter_on_scalar(t, g * GROUP, (g + 1) * GROUP, new_early[:, g, t, :])
+
+        scale_u(0)
+        quantize_w(0, 1, turn_w(0, 1, "bank7"))
+        quantize_s(0)
+        early_planes(0, 0, 1, "bank6")
+        quantize_w(1, 1, turn_w(1, 1, "bank7"))
+        early_planes(0, 1, 1, "bank5")
+        first_product(1)
+        for g in range(1, GROUPS):
+            if g + 1 < GROUPS:
+                first_product(g + 1)
+            scale_u(g)
+            quantize_s(g)
+            early_planes(g, 0, 2, "bank%d" % (3 + g % 2))
+            if g == 1:
+                quantize_w(2, 2, turn_w(2, 2, "bank6"))
+        for t in range(2):
+            nc.sync.dma_start(out_planes[:, t, :], window[t][:])
+
+        new_late = {}
+        for t in (2, 3):
+            bank = psum.tile([P, SLOTS], F32, name="v_late%d" % t, tag="bank%d" % (0 if t == 2 else 2))
+            second_product(bank[:], t, slice(0, SLOTS))
+            new_late[t] = keep.tile([P, SLOTS], F32, name="new_late%d" % t, tag="new_then_pairs" if t == 2 else "new_late3", align_bytes=64)
+            nc.vector.tensor_tensor(new_late[t][:], bank[:], picked[:, t, :], ADD)
+        nc.vector.tensor_copy(window[2][:].indirect(offsets[:]), new_late[2][:])
+        nc.sync.dma_start(out_planes[:, 2, :], window[2][:])
+        for a in (0, HALF):
+            scatter_on_scalar(last, a, a + HALF, new_late[last][:, a:a + HALF])
+        nc.sync.dma_start(out_planes[:, last, :], window[last][:])
+
+        pairs = keep.tile([P, PIECES, 2, PIECE, 2], BF16, name="pairs", tag="new_then_pairs", align_bytes=64)
         for t in range(last):
-            scale_u(t, 0, SLOTS)
-        scale_u(last, 0, GROUP)
-        turn_w(0, 1, "bank4", w_head)
-        scale_u(last, GROUP, HALF)
-        scale_u(last, HALF, SLOTS)
-        weave(nc.vector.tensor_copy, s_first, s_planes[:, :, 0:GROUP])
-        weave(nc.vector.tensor_copy, s_second, s_planes[:, :, GROUP:HALF])
-        quantize(w_codes[:, 0:P], w_scales[:, 0:P], w_head, E4M3)
-        quantize_s(0, GROUP, s_first)
-        v_sb = keep.tile([P, LANES, SLOTS], F32, name="v_sb")
-        early_bank = psum.tile([P, SLOTS], F32, name="early_bank", tag="bank7")
-        second_product(early_bank, 0, 0)
-        weave(nc.vector.tensor_copy, s_rest[:, 0:S_SPLIT - HALF, :], s_planes[:, :, HALF:S_SPLIT])
-        weave(nc.scalar.copy, s_rest[:, S_SPLIT - HALF:HALF, :], s_planes[:, :, S_SPLIT:SLOTS])
-        quantize_s(GROUP, HALF, s_second)
-        quantize_s(HALF, SLOTS, s_rest)
-        w_late = keep.tile([P, 3 * P, LANES], BF16, name="w_late", tag="s_planes", align_bytes=64)
-        turn_w(1, 2, "bank1", w_late[:, 0:2 * P, :])
-        nc.scalar.copy(out=v_sb[:, order[0], 0:GROUP], in_=early_bank[:, S_FIRST:SLOTS])
-        turn_w(3, 1, "bank0", w_late[:, 2 * P:3 * P, :])
-        quantize(w_codes[:, P:3 * P], w_scales[:, P:3 * P], w_late[:, 0:2 * P, :], E4M3)
-        nc.vector.tensor_tensor(window[order[0]][:].indirect(slot_offsets(0, GROUP)), picked[:, order[0], 0:GROUP], v_sb[:, order[0], 0:GROUP], ADD)
-        quantize(w_codes[:, 3 * P:4 * P], w_scales[:, 3 * P:4 * P], w_late[:, 2 * P:3 * P, :], E4M3)
+            nc.vector.tensor_copy(out=pairs[:, :, t // 2, :, t % 2], in_=window[t][:].rearrange("p (k c) -> p k c", k=PIECES))
+        for k in (0, 3, 1, 2):
+            nc.vector.tensor_copy(out=pairs[:, k, 1, :, 1], in_=window[last][:, k * PIECE:(k + 1) * PIECE])
 
-        first_pieces = ((GROUP, SLOTS),)
-        for n, t in enumerate(order):
-            v_bank = psum.tile([P, SLOTS], F32, name="v_bank%d" % n, tag="bank%d" % (5, 6, 2, 3)[n])
-            second_product(v_bank, n, S_FIRST)
-            for a, b in (first_pieces if n == 0 else ((0, SLOTS),)):
-                nc.scalar.copy(out=v_sb[:, t, a:b], in_=v_bank[:, a:b])
-
-        y_grouped = keep.tile([P, TOKENS, LANES], BF16, name="y_grouped", tag="codes_then_y", align_bytes=64)
         y_codes = keep.tile([P, TOKENS], U32, name="y_codes", align_bytes=64)
         y_scales = keep.tile([P, TOKENS], U8, name="y_scales", align_bytes=64)
-        for n, t in enumerate(order):
-            for a, b in (first_pieces if n == 0 else ((0, SLOTS),)):
-                nc.vector.tensor_tensor(window[t][:].indirect(slot_offsets(a, b)), picked[:, t, a:b], v_sb[:, t, a:b], ADD)
-            nc.sync.dma_start(out_planes[:, t, :], window[t][:])
-            if n == 0:
-                nc.scalar.copy(out=y_grouped[:, :, t], in_=window[t][:])
-                a, b = Y_PIECE - 4, Y_PIECE + 4
-                nc.scalar.copy(out=y_grouped[:, a:b, 0:2],
-                               in_=window[t][:, a:b].rearrange("p (c o) -> p c o", o=1).to_broadcast([P, b - a, 2]))
-            elif n < last:
-                nc.scalar.copy(out=y_grouped[:, :, t], in_=window[t][:])
-            else:
-                for a, b in ((Y_SPLIT, TOKENS - Y_PIECE), (TOKENS - Y_PIECE, TOKENS)):
-                    nc.scalar.copy(out=y_grouped[:, a:b, t], in_=window[t][:, a:b])
-                for a, b in ((0, Y_PIECE), (Y_PIECE, Y_SPLIT)):
-                    nc.vector.tensor_copy(out=y_grouped[:, a:b, t], in_=window[t][:, a:b])
         words_out = out_1[0].rearrange("p c l -> p (c l)").bitcast(I32)
-        for a in range(0, TOKENS, Y_PIECE):
-            quantize(y_codes[:, a:a + Y_PIECE], y_scales[:, a:a + Y_PIECE], y_grouped[:, a:a + Y_PIECE, :], E4M3)
-            nc.sync.dma_start(words_out[:, a:a + Y_PIECE], y_codes[:, a:a + Y_PIECE].bitcast(I32))
+        y_grouped = {}
+        for k in (0, 3, 1, 2):
+            y_grouped[k] = keep.tile([P, PIECE, LANES], BF16, name="y_grouped%d" % k, align_bytes=64)
+            copy = nc.vector.tensor_copy if k == 3 else nc.scalar.copy
+            copy(out=y_grouped[k][:].rearrange("p c t -> p (c t)").bitcast(F32).rearrange("p (c i u) -> p c u i", i=4, u=2),
+                 in_=pairs[:, k].rearrange("p u c e -> p (u c e)").bitcast(F32).rearrange("p (u c i) -> p c u i", u=2, i=4))
+        for k in (0, 3, 1, 2):
+            a = k * PIECE
+            quantize(y_codes[:, a:a + PIECE], y_scales[:, a:a + PIECE], y_grouped[k][:], E4M3)
+            nc.sync.dma_start(words_out[:, a:a + PIECE], y_codes[:, a:a + PIECE].bitcast(I32))
         for q in range(4):
             queue = nc.sync if q < 2 else nc.scalar
             queue.dma_start(out_2[0, 4 * q:4 * q + 4, :].bitcast(I32), y_scales[32 * q:32 * q + 4, :].bitcast(I32))

@@ -109,7 +109,7 @@ def tile_attend_greft_pl_kernel(tc, dyT, R, W, ck, offs, out_0, out_1, out_2):
         u_bank = {}
 
         def first_product(g):
-            u_bank[g] = psum.tile([P, LANES, GROUP], F32, name="u_bank%d" % g, tag="bank%d" % (g % 2))
+            u_bank[g] = psum.tile([P, LANES, GROUP], F32, name="u_bank%d" % g, tag="bank%d" % g)
             for t in range(LANES):
                 if g == 0:
                     quantize(r_codes[:, t, :], r_scales[:, t, :], r_grouped[t][:], E4M3)
@@ -159,54 +159,70 @@ def tile_attend_greft_pl_kernel(tc, dyT, R, W, ck, offs, out_0, out_1, out_2):
             nc.tensor.matmul_mx(out=out, lhsT=w_codes[:, t, :].bitcast(E4M3), lhsT_scale=w_scales[:, t, :],
                                 rhs=s_codes[:, slots].bitcast(E5M2), rhs_scale=s_scales[:, slots], start=True, stop=True)
 
-        def scatter_on_scalar(t, a, b, values):
-            nc.scalar.activation(out=window[t][:].indirect(slot_offsets(a, b)), in_=values, func=COPY)
+        new_early = keep.tile([P, 2, SLOTS], F32, name="new_early")
+        new_third = keep.tile([P, 1, SLOTS], F32, name="new_third", tag="third_then_pairs", align_bytes=64)
+        new_last = keep.tile([P, 1, SLOTS], F32, name="new_last")
+        new = (new_early[:, 0:2], new_early[:, 1:2], new_third[:], new_last[:])
 
-        new_early = keep.tile([P, GROUPS, 2, GROUP], F32, name="new_early")
-
-        def early_planes(g, first, count, bank):
-            bank = psum.tile([P, count, GROUP], F32, name="v_early%d_%d" % (g, first), tag=bank)
+        def add_planes(first, count, a, b, bank):
+            v_bank = psum.tile([P, count, b - a], F32, name="v_bank%d_%d" % (first, a), tag=bank)
             for n in range(count):
-                second_product(bank[:, n, :], first + n, group(g))
-            nc.vector.tensor_tensor(new_early[:, g, first:first + count, :], bank[:], picked[:, first:first + count, group(g)], ADD)
-            for t in range(first, first + count):
-                scatter_on_scalar(t, g * GROUP, (g + 1) * GROUP, new_early[:, g, t, :])
+                second_product(v_bank[:, n, :], first + n, slice(a, b))
+            nc.vector.tensor_tensor(new[first][:, 0:count, a:b], v_bank[:], picked[:, first:first + count, a:b], ADD)
+
+        def scatter(t, a, b, on_vector=False):
+            if on_vector:
+                nc.vector.tensor_copy(window[t][:].indirect(slot_offsets(a, b)), new[t][:, 0, a:b])
+            else:
+                nc.scalar.activation(out=window[t][:].indirect(slot_offsets(a, b)), in_=new[t][:, 0, a:b], func=COPY)
 
         scale_u(0)
         quantize_w(0, 1, turn_w(0, 1, "bank7"))
         quantize_s(0)
-        early_planes(0, 0, 1, "bank6")
+        add_planes(0, 1, 0, GROUP, "bank6")
+        scatter(0, 0, GROUP)
         quantize_w(1, 1, turn_w(1, 1, "bank7"))
-        early_planes(0, 1, 1, "bank5")
+        add_planes(1, 1, 0, GROUP, "bank5")
+        scatter(1, 0, GROUP)
         first_product(1)
-        for g in range(1, GROUPS):
-            if g + 1 < GROUPS:
-                first_product(g + 1)
-            scale_u(g)
-            quantize_s(g)
-            early_planes(g, 0, 2, "bank%d" % (3 + g % 2))
-            if g == 1:
-                quantize_w(2, 2, turn_w(2, 2, "bank6"))
+        scale_u(1)
+        quantize_s(1)
+        add_planes(0, 2, GROUP, HALF, "bank4")
+        for t in range(2):
+            scatter(t, GROUP, HALF)
+        first_product(2)
+        first_product(3)
+        scale_u(2)
+        quantize_s(2)
+        quantize_w(2, 2, turn_w(2, 2, "bank6"))
+        for g in range(2, GROUPS):
+            if g == 3:
+                scale_u(g)
+                quantize_s(g)
+                add_planes(2, 1, 0, HALF, "bank5")
+            add_planes(0, 2, g * GROUP, (g + 1) * GROUP, "bank%d" % (g - 2))
+            for t in range(2):
+                scatter(t, g * GROUP, (g + 1) * GROUP)
         for t in range(2):
             nc.sync.dma_start(out_planes[:, t, :], window[t][:])
-
-        new_late = {}
-        for t in (2, 3):
-            bank = psum.tile([P, SLOTS], F32, name="v_late%d" % t, tag="bank%d" % (0 if t == 2 else 2))
-            second_product(bank[:], t, slice(0, SLOTS))
-            new_late[t] = keep.tile([P, SLOTS], F32, name="new_late%d" % t, tag="new_then_pairs" if t == 2 else "new_late3", align_bytes=64)
-            nc.vector.tensor_tensor(new_late[t][:], bank[:], picked[:, t, :], ADD)
-        nc.vector.tensor_copy(window[2][:].indirect(offsets[:]), new_late[2][:])
+        add_planes(last, 1, 0, SLOTS, "bank2")
+        add_planes(2, 1, HALF, SLOTS, "bank4")
+        scatter(last, 0, GROUP, on_vector=True)
+        scatter(2, 0, SLOTS, on_vector=True)
         nc.sync.dma_start(out_planes[:, 2, :], window[2][:])
-        for a in (0, HALF):
-            scatter_on_scalar(last, a, a + HALF, new_late[last][:, a:a + HALF])
+        scatter(last, GROUP, SLOTS)
         nc.sync.dma_start(out_planes[:, last, :], window[last][:])
 
-        pairs = keep.tile([P, PIECES, 2, PIECE, 2], BF16, name="pairs", tag="new_then_pairs", align_bytes=64)
-        for t in range(last):
-            nc.vector.tensor_copy(out=pairs[:, :, t // 2, :, t % 2], in_=window[t][:].rearrange("p (k c) -> p k c", k=PIECES))
+        pairs = [keep.tile([P, 2, 2, PIECE, 2], BF16, name="pairs%d" % h, tag="third_then_pairs" if h == 1 else "pairs0", align_bytes=64)
+                 for h in range(2)]
+        pieces = [window[t][:].rearrange("p (h k c) -> p h k c", h=2, k=2) for t in range(LANES)]
+        for h in range(2):
+            nc.vector.tensor_copy(out=pairs[h][:, :, 1, :, 0], in_=pieces[2][:, h])
+        for t in range(2):
+            nc.gpsimd.tensor_scalar(pairs[0][:, :, 0, :, t], pieces[t][:, 0], 1.0, 0.0, MULT, ADD)
+            nc.vector.tensor_copy(out=pairs[1][:, :, 0, :, t], in_=pieces[t][:, 1])
         for k in (0, 3, 1, 2):
-            nc.vector.tensor_copy(out=pairs[:, k, 1, :, 1], in_=window[last][:, k * PIECE:(k + 1) * PIECE])
+            nc.vector.tensor_copy(out=pairs[k // 2][:, k % 2, 1, :, 1], in_=window[last][:, k * PIECE:(k + 1) * PIECE])
 
         y_codes = keep.tile([P, TOKENS], U32, name="y_codes", align_bytes=64)
         y_scales = keep.tile([P, TOKENS], U8, name="y_scales", align_bytes=64)
@@ -216,7 +232,7 @@ def tile_attend_greft_pl_kernel(tc, dyT, R, W, ck, offs, out_0, out_1, out_2):
             y_grouped[k] = keep.tile([P, PIECE, LANES], BF16, name="y_grouped%d" % k, align_bytes=64)
             copy = nc.vector.tensor_copy if k == 3 else nc.scalar.copy
             copy(out=y_grouped[k][:].rearrange("p c t -> p (c t)").bitcast(F32).rearrange("p (c i u) -> p c u i", i=4, u=2),
-                 in_=pairs[:, k].rearrange("p u c e -> p (u c e)").bitcast(F32).rearrange("p (u c i) -> p c u i", u=2, i=4))
+                 in_=pairs[k // 2][:, k % 2].rearrange("p u c e -> p (u c e)").bitcast(F32).rearrange("p (u c i) -> p c u i", u=2, i=4))
         for k in (0, 3, 1, 2):
             a = k * PIECE
             quantize(y_codes[:, a:a + PIECE], y_scales[:, a:a + PIECE], y_grouped[k][:], E4M3)

@@ -27,6 +27,7 @@ RUN = 8
 GROUP = 128
 GROUPS = SLOTS // GROUP
 PIECE = 256
+LAST_SPLIT = 256
 PIECES = TOKENS // PIECE
 
 FLOPS = 2 * 2 * D * K * SLOTS
@@ -52,11 +53,9 @@ def tile_attend_greft_pl_kernel(tc, dyT, R, W, ck, offs, out_0, out_1, out_2):
         nc.sync.dma_start(r_raw[:], R.rearrange("(p j) k -> p j k", j=LANES))
         ck_line = keep.tile([1, K], F32, name="ck_line")
         nc.scalar.dma_start(ck_line[:], ck.rearrange("k o -> o k"))
-        w_sets = ((0, 1), (1, 1), (2, 1), (3, 1))
-        w_raw = {}
-        for t, count in w_sets:
-            w_raw[t] = keep.tile([P, count, K], F32, name="w_raw%d" % t)
-            nc.sync.dma_start(w_raw[t][:], w_planes[:, t:t + count, :])
+        w_raw = [keep.tile([P, 2, K], F32, name="w_raw%d" % h) for h in range(2)]
+        for h in range(2):
+            nc.sync.dma_start(w_raw[h][:], w_planes[:, 2 * h:2 * h + 2, :])
         window = [keep.tile([P, TOKENS], F32, name="window%d" % t) for t in range(LANES)]
         nc.sync.dma_start(window[last][:], dy_planes[:, last, :])
 
@@ -124,21 +123,20 @@ def tile_attend_greft_pl_kernel(tc, dyT, R, W, ck, offs, out_0, out_1, out_2):
         w_codes = keep.tile([P, LANES, P], U32, name="w_codes", align_bytes=64)
         w_scales = keep.tile([P, LANES, P], U8, name="w_scales", align_bytes=64)
 
-        w_sorted = [keep.tile([P, K], BF16, name="w_sorted%d" % t, align_bytes=64) for t in range(LANES)]
-        for t in range(LANES):
-            nc.scalar.copy(out=w_sorted[t][:].rearrange("m (u b i e) -> m u b e i", u=2, i=RUN, e=2),
-                           in_=w_raw[t][:, 0, :].rearrange("m (b u e i) -> m u b e i", u=2, i=RUN, e=2))
+        w_sorted = [keep.tile([P, 2 * K], BF16, name="w_sorted%d" % h, align_bytes=64) for h in range(2)]
+        for h in range(2):
+            nc.scalar.copy(out=w_sorted[h][:].rearrange("m (u b i e) -> m u b e i", u=2, i=RUN, e=2),
+                           in_=w_raw[h][:].rearrange("m n (b u e i) -> m u (n b) e i", u=2, i=RUN, e=2))
 
         def turn_w(t, count, bank):
             turned = psum.tile([P, count, 2, P], F32, name="turned%d" % t, tag=bank)
+            words = w_sorted[t // 2][:].bitcast(F32).rearrange("m (u n p) -> m u n p", u=2, n=2)
             for n in range(count):
-                words = w_sorted[t + n][:].bitcast(F32)
                 for u in range(2):
-                    nc.tensor.transpose(turned[:, n, u, :], words[:, u * P:(u + 1) * P], ident[:])
+                    nc.tensor.transpose(turned[:, n, u, :], words[:, u, t % 2 + n, :], ident[:])
             w_grouped = keep.tile([P, count * P, LANES], BF16, name="w_grouped%d" % t, align_bytes=64)
-            copy = nc.scalar.copy if t < 2 else nc.vector.tensor_copy
-            copy(out=w_grouped[:].rearrange("p m t -> p (m t)").bitcast(F32).rearrange("p (n m u) -> p n m u", n=count, u=2),
-                 in_=turned[:].rearrange("p n u m -> p n m u"))
+            nc.scalar.copy(out=w_grouped[:].rearrange("p m t -> p (m t)").bitcast(F32).rearrange("p (n m u) -> p n m u", n=count, u=2),
+                           in_=turned[:].rearrange("p n u m -> p n m u"))
             return w_grouped
 
         def quantize_w(t, count, grouped):
@@ -161,7 +159,7 @@ def tile_attend_greft_pl_kernel(tc, dyT, R, W, ck, offs, out_0, out_1, out_2):
 
         new_early = keep.tile([P, 2, SLOTS], F32, name="new_early")
         new_third = keep.tile([P, 1, SLOTS], F32, name="new_third", tag="third_then_pairs", align_bytes=64)
-        new_last = keep.tile([P, 1, SLOTS], F32, name="new_last")
+        new_last = keep.tile([P, 1, SLOTS], F32, name="new_last", tag="last_then_pairs", align_bytes=64)
         new = (new_early[:, 0:2], new_early[:, 1:2], new_third[:], new_last[:])
 
         def add_planes(first, count, a, b, bank):
@@ -176,64 +174,74 @@ def tile_attend_greft_pl_kernel(tc, dyT, R, W, ck, offs, out_0, out_1, out_2):
             else:
                 nc.scalar.activation(out=window[t][:].indirect(slot_offsets(a, b)), in_=new[t][:, 0, a:b], func=COPY)
 
-        scale_u(0)
-        quantize_w(0, 1, turn_w(0, 1, "bank7"))
-        quantize_s(0)
-        add_planes(0, 1, 0, GROUP, "bank6")
-        scatter(0, 0, GROUP)
-        quantize_w(1, 1, turn_w(1, 1, "bank7"))
-        add_planes(1, 1, 0, GROUP, "bank5")
-        scatter(1, 0, GROUP)
         first_product(1)
+        scale_u(0)
+        w_grouped = [turn_w(0, 1, "bank7"), turn_w(1, 1, "bank6"), turn_w(2, 2, "bank5")]
+        quantize_w(0, 1, w_grouped[0])
+        quantize_s(0)
+        add_planes(0, 1, 0, GROUP, "bank4")
+        scatter(0, 0, GROUP)
+        quantize_w(1, 1, w_grouped[1])
+        add_planes(1, 1, 0, GROUP, "bank7")
+        scatter(1, 0, GROUP)
         scale_u(1)
         quantize_s(1)
-        add_planes(0, 2, GROUP, HALF, "bank4")
+        add_planes(0, 2, GROUP, HALF, "bank6")
         for t in range(2):
             scatter(t, GROUP, HALF)
         first_product(2)
         first_product(3)
         scale_u(2)
         quantize_s(2)
-        quantize_w(2, 2, turn_w(2, 2, "bank6"))
+        quantize_w(2, 2, w_grouped[2])
         for g in range(2, GROUPS):
             if g == 3:
                 scale_u(g)
                 quantize_s(g)
                 add_planes(2, 1, 0, HALF, "bank5")
             add_planes(0, 2, g * GROUP, (g + 1) * GROUP, "bank%d" % (g - 2))
-            for t in range(2):
-                scatter(t, g * GROUP, (g + 1) * GROUP)
         for t in range(2):
+            scatter(t, HALF, SLOTS)
             nc.sync.dma_start(out_planes[:, t, :], window[t][:])
         add_planes(last, 1, 0, SLOTS, "bank2")
         add_planes(2, 1, HALF, SLOTS, "bank4")
-        scatter(last, 0, GROUP, on_vector=True)
+        scatter(last, 0, LAST_SPLIT, on_vector=True)
         scatter(2, 0, SLOTS, on_vector=True)
         nc.sync.dma_start(out_planes[:, 2, :], window[2][:])
-        scatter(last, GROUP, SLOTS)
+        scatter(last, LAST_SPLIT, SLOTS)
         nc.sync.dma_start(out_planes[:, last, :], window[last][:])
 
-        pairs = [keep.tile([P, 2, 2, PIECE, 2], BF16, name="pairs%d" % h, tag="third_then_pairs" if h == 1 else "pairs0", align_bytes=64)
-                 for h in range(2)]
-        pieces = [window[t][:].rearrange("p (h k c) -> p h k c", h=2, k=2) for t in range(LANES)]
-        for h in range(2):
-            nc.vector.tensor_copy(out=pairs[h][:, :, 1, :, 0], in_=pieces[2][:, h])
+        pairs_early = keep.tile([P, 2, 2, PIECE, 2], BF16, name="pairs_early", align_bytes=64)
+        pairs_third = keep.tile([P, 2, PIECE, 2], BF16, name="pairs_third", tag="third_then_pairs", align_bytes=64)
+        pairs_last = keep.tile([P, 2, PIECE, 2], BF16, name="pairs_last", tag="last_then_pairs", align_bytes=64)
+        pairs = (pairs_early[:, 0], pairs_early[:, 1], pairs_third[:], pairs_last[:])
+        pieces = [window[t][:].rearrange("p (k c) -> p k c", k=PIECES) for t in range(LANES)]
+
+        def round_into_pairs(copy, t, k):
+            copy(out=pairs[k][:, t // 2, :, t % 2], in_=pieces[t][:, k])
+
         for t in range(2):
-            nc.gpsimd.tensor_scalar(pairs[0][:, :, 0, :, t], pieces[t][:, 0], 1.0, 0.0, MULT, ADD)
-            nc.vector.tensor_copy(out=pairs[1][:, :, 0, :, t], in_=pieces[t][:, 1])
-        for k in (0, 3, 1, 2):
-            nc.vector.tensor_copy(out=pairs[k // 2][:, k % 2, 1, :, 1], in_=window[last][:, k * PIECE:(k + 1) * PIECE])
+            nc.gpsimd.tensor_scalar(pairs_early[:, :, 0, :, t], pieces[t][:, 0:2], 1.0, 0.0, MULT, ADD)
+        nc.vector.tensor_copy(out=pairs_early[:, :, 1, :, 0], in_=pieces[2][:, 0:2])
+        for t in (0, 1, 2):
+            round_into_pairs(nc.vector.tensor_copy, t, 2)
+        for t in (2, 3):
+            round_into_pairs(nc.scalar.copy, t, 3)
+        for t in range(2):
+            round_into_pairs(nc.vector.tensor_copy, t, 3)
+        for k in range(3):
+            round_into_pairs(nc.vector.tensor_copy, last, k)
 
         y_codes = keep.tile([P, TOKENS], U32, name="y_codes", align_bytes=64)
         y_scales = keep.tile([P, TOKENS], U8, name="y_scales", align_bytes=64)
         words_out = out_1[0].rearrange("p c l -> p (c l)").bitcast(I32)
         y_grouped = {}
-        for k in (0, 3, 1, 2):
+        for k in (0, 1, 3, 2):
             y_grouped[k] = keep.tile([P, PIECE, LANES], BF16, name="y_grouped%d" % k, align_bytes=64)
-            copy = nc.vector.tensor_copy if k == 3 else nc.scalar.copy
+            copy = nc.vector.tensor_copy if k < 2 else nc.scalar.copy
             copy(out=y_grouped[k][:].rearrange("p c t -> p (c t)").bitcast(F32).rearrange("p (c i u) -> p c u i", i=4, u=2),
-                 in_=pairs[k // 2][:, k % 2].rearrange("p u c e -> p (u c e)").bitcast(F32).rearrange("p (u c i) -> p c u i", u=2, i=4))
-        for k in (0, 3, 1, 2):
+                 in_=pairs[k].rearrange("p u c e -> p (u c e)").bitcast(F32).rearrange("p (u c i) -> p c u i", u=2, i=4))
+        for k in (0, 1, 3, 2):
             a = k * PIECE
             quantize(y_codes[:, a:a + PIECE], y_scales[:, a:a + PIECE], y_grouped[k][:], E4M3)
             nc.sync.dma_start(words_out[:, a:a + PIECE], y_codes[:, a:a + PIECE].bitcast(I32))

@@ -27,7 +27,7 @@ RUN = 8
 GROUP = 128
 GROUPS = SLOTS // GROUP
 PIECE = 256
-LAST_SPLIT = 256
+LAST_SPLIT = 320
 PIECES = TOKENS // PIECE
 
 FLOPS = 2 * 2 * D * K * SLOTS
@@ -46,7 +46,7 @@ def tile_attend_greft_pl_kernel(tc, dyT, R, W, ck, offs, out_0, out_1, out_2):
 
         offsets = keep.tile([P, SLOTS // PER_COL], U16, name="offsets")
         nc.sync.dma_start(offsets[:], offs)
-        source = [keep.tile([P, TOKENS], F32, name="source%d" % t) for t in range(LANES)]
+        source = [keep.tile([P, TOKENS], F32, name="source%d" % t, tag="source%d" % t) for t in range(LANES)]
         for t in range(LANES):
             nc.sync.dma_start(source[t][:], dy_planes[:, t, :])
         r_raw = keep.tile([P, LANES, K], F32, name="r_raw")
@@ -93,6 +93,10 @@ def tile_attend_greft_pl_kernel(tc, dyT, R, W, ck, offs, out_0, out_1, out_2):
         for a in (0, GROUP):
             nc.vector.tensor_copy(picked[:, last, a:a + GROUP], source[last][:].indirect(slot_offsets(a, a + GROUP)))
         nc.scalar.activation(out=picked[:, last, HALF:SLOTS], in_=source[last][:].indirect(slot_offsets(HALF, SLOTS)), func=COPY)
+        ck_sb = keep.tile([P, LANES], F32, name="ck_sb", tag="source%d" % last)
+        nc.scalar.copy(out=ck_sb[:], in_=ck_bank[:, :, 0])
+        ck_spread = ck_sb[:].rearrange("p (o t) -> p o t", o=1).to_broadcast([P, GROUP, LANES])
+
         for g in range(GROUPS):
             weave(nc.vector.tensor_copy if g < 2 else nc.scalar.copy, dy_grouped[:, group(g), :], picked[:, :, group(g)])
         for g in range(GROUPS):
@@ -114,11 +118,6 @@ def tile_attend_greft_pl_kernel(tc, dyT, R, W, ck, offs, out_0, out_1, out_2):
                     quantize(r_codes[:, t, :], r_scales[:, t, :], r_grouped[t][:], E4M3)
                 nc.tensor.matmul_mx(out=u_bank[g][:, t, :], lhsT=r_codes[:, t, :].bitcast(E4M3), lhsT_scale=r_scales[:, t, :],
                                     rhs=dy_codes[:, group(g)].bitcast(E5M2), rhs_scale=dy_scales[:, group(g)], start=True, stop=True)
-
-        first_product(0)
-        ck_sb = keep.tile([P, LANES], F32, name="ck_sb", tag="r_grouped0", align_bytes=64)
-        nc.scalar.copy(out=ck_sb[:], in_=ck_bank[:, :, 0])
-        ck_spread = ck_sb[:].rearrange("p (o t) -> p o t", o=1).to_broadcast([P, GROUP, LANES])
 
         w_codes = keep.tile([P, LANES, P], U32, name="w_codes", align_bytes=64)
         w_scales = keep.tile([P, LANES, P], U8, name="w_scales", align_bytes=64)
@@ -143,6 +142,7 @@ def tile_attend_greft_pl_kernel(tc, dyT, R, W, ck, offs, out_0, out_1, out_2):
             quantize(w_codes[:, t:t + count, :].rearrange("p n m -> p (n m)"), w_scales[:, t:t + count, :].rearrange("p n m -> p (n m)"),
                      grouped[:], E4M3)
 
+        first_product(0)
         s_grouped = keep.tile([P, SLOTS, LANES], BF16, name="s_grouped", align_bytes=64)
         s_codes = keep.tile([P, SLOTS], U32, name="s_codes", align_bytes=64)
         s_scales = keep.tile([P, SLOTS], U8, name="s_scales", align_bytes=64)
@@ -244,7 +244,9 @@ def tile_attend_greft_pl_kernel(tc, dyT, R, W, ck, offs, out_0, out_1, out_2):
         for k in (0, 1, 3, 2):
             a = k * PIECE
             quantize(y_codes[:, a:a + PIECE], y_scales[:, a:a + PIECE], y_grouped[k][:], E4M3)
-            nc.sync.dma_start(words_out[:, a:a + PIECE], y_codes[:, a:a + PIECE].bitcast(I32))
+            if k > 0:
+                first = 0 if k == 1 else a
+                nc.sync.dma_start(words_out[:, first:a + PIECE], y_codes[:, first:a + PIECE].bitcast(I32))
         for q in range(4):
             queue = nc.sync if q < 2 else nc.scalar
             queue.dma_start(out_2[0, 4 * q:4 * q + 4, :].bitcast(I32), y_scales[32 * q:32 * q + 4, :].bitcast(I32))

@@ -159,7 +159,7 @@ def tile_attend_greft_pl_kernel(tc, dyT, R, W, ck, offs, out_0, out_1, out_2):
 
         new_early = keep.tile([P, 2, SLOTS], F32, name="new_early")
         new_third = keep.tile([P, 1, SLOTS], F32, name="new_third", tag="third_then_pairs", align_bytes=64)
-        new_last = keep.tile([P, 1, SLOTS], F32, name="new_last", tag="last_then_pairs", align_bytes=64)
+        new_last = keep.tile([P, 1, SLOTS], F32, name="new_last")
         new = (new_early[:, 0:2], new_early[:, 1:2], new_third[:], new_last[:])
 
         def add_planes(first, count, a, b, bank):
@@ -211,25 +211,23 @@ def tile_attend_greft_pl_kernel(tc, dyT, R, W, ck, offs, out_0, out_1, out_2):
         scatter(last, LAST_SPLIT, SLOTS)
         nc.sync.dma_start(out_planes[:, last, :], window[last][:])
 
-        pairs_early = keep.tile([P, 2, 2, PIECE, 2], BF16, name="pairs_early", align_bytes=64)
-        pairs_third = keep.tile([P, 2, PIECE, 2], BF16, name="pairs_third", tag="third_then_pairs", align_bytes=64)
-        pairs_last = keep.tile([P, 2, PIECE, 2], BF16, name="pairs_last", tag="last_then_pairs", align_bytes=64)
-        pairs = (pairs_early[:, 0], pairs_early[:, 1], pairs_third[:], pairs_last[:])
+        pairs_early = keep.tile([P, last, 2, PIECE, 2], BF16, name="pairs_early", align_bytes=64)
+        pairs_last = keep.tile([P, 2, PIECE, 2], BF16, name="pairs_last", tag="third_then_pairs", align_bytes=64)
+        pairs = (pairs_early[:, 0], pairs_early[:, 1], pairs_early[:, 2], pairs_last[:])
         pieces = [window[t][:].rearrange("p (k c) -> p k c", k=PIECES) for t in range(LANES)]
 
         def round_into_pairs(copy, t, k):
             copy(out=pairs[k][:, t // 2, :, t % 2], in_=pieces[t][:, k])
 
         for t in range(2):
-            nc.gpsimd.tensor_scalar(pairs_early[:, :, 0, :, t], pieces[t][:, 0:2], 1.0, 0.0, MULT, ADD)
-        nc.vector.tensor_copy(out=pairs_early[:, :, 1, :, 0], in_=pieces[2][:, 0:2])
-        for t in (0, 1, 2):
-            round_into_pairs(nc.vector.tensor_copy, t, 2)
-        for t in (2, 3):
-            round_into_pairs(nc.scalar.copy, t, 3)
+            nc.gpsimd.tensor_scalar(pairs_early[:, :, 0, :, t], pieces[t][:, 0:last], 1.0, 0.0, MULT, ADD)
         for t in range(2):
-            round_into_pairs(nc.vector.tensor_copy, t, 3)
-        for k in range(3):
+            round_into_pairs(nc.vector.tensor_copy, t, last)
+        nc.vector.tensor_copy(out=pairs_early[:, 0:2, 1, :, 0], in_=pieces[2][:, 0:2])
+        for t in (3, 2):
+            for k in (3, 2):
+                round_into_pairs(nc.scalar.copy, t, k)
+        for k in range(2):
             round_into_pairs(nc.vector.tensor_copy, last, k)
 
         y_codes = keep.tile([P, TOKENS], U32, name="y_codes", align_bytes=64)

@@ -24,11 +24,12 @@ TOKENS = 1024
 PER_COL = 16
 HALF = SLOTS // 2
 RUN = 8
+LINE = 4
 GROUP = 128
 GROUPS = SLOTS // GROUP
 PIECE = 256
-LAST_SPLIT = 320
 PIECES = TOKENS // PIECE
+LAST_SPLIT = 320
 
 FLOPS = 2 * 2 * D * K * SLOTS
 
@@ -74,7 +75,7 @@ def tile_attend_greft_pl_kernel(tc, dyT, R, W, ck, offs, out_0, out_1, out_2):
             return offsets[:, a // PER_COL:b // PER_COL]
 
         def weave(copy, lanes, planes):
-            copy(out=lanes.rearrange("p (c i) t -> p c t i", i=4), in_=planes.rearrange("p t (c i) -> p c t i", i=4))
+            copy(out=lanes.rearrange("p (c i) t -> p c t i", i=LINE), in_=planes.rearrange("p t (c i) -> p c t i", i=LINE))
 
         def quantize(codes, scales, grouped, fmt):
             nc.vector.quantize_mx(out=codes.bitcast(fmt), scales=scales, in_=grouped.rearrange("p c t -> p (c t)"))
@@ -98,17 +99,17 @@ def tile_attend_greft_pl_kernel(tc, dyT, R, W, ck, offs, out_0, out_1, out_2):
         ck_spread = ck_sb[:].rearrange("p (o t) -> p o t", o=1).to_broadcast([P, GROUP, LANES])
 
         for g in range(GROUPS):
-            weave(nc.vector.tensor_copy if g < 2 else nc.scalar.copy, dy_grouped[:, group(g), :], picked[:, :, group(g)])
+            weave(nc.vector.tensor_copy if g < GROUPS // 2 else nc.scalar.copy, dy_grouped[:, group(g), :], picked[:, :, group(g)])
         for g in range(GROUPS):
             quantize(dy_codes[:, group(g)], dy_scales[:, group(g)], dy_grouped[:, group(g), :], E5M2)
 
         r_codes = keep.tile([P, LANES, P], U32, name="r_codes", align_bytes=64)
         r_scales = keep.tile([P, LANES, P], U8, name="r_scales", align_bytes=64)
-        r_columns = r_raw[:].rearrange("p j (b t h i) -> p t b h j i", t=LANES, h=2, i=4)
-        r_grouped = [keep.tile([P, P, LANES], BF16, name="r_grouped%d" % t, tag="r_grouped%d" % t, align_bytes=64) for t in range(LANES)]
+        r_columns = r_raw[:].rearrange("p j (b t h i) -> p t b h j i", t=LANES, h=RUN // LINE, i=LINE)
+        r_grouped = [keep.tile([P, P, LANES], BF16, name="r_grouped%d" % t, align_bytes=64) for t in range(LANES)]
         for t in range(LANES):
             copy = nc.vector.tensor_copy if t < last else nc.scalar.copy
-            copy(out=r_grouped[t][:].rearrange("p (b h i) j -> p b h j i", h=2, i=4), in_=r_columns[:, t])
+            copy(out=r_grouped[t][:].rearrange("p (b h i) j -> p b h j i", h=RUN // LINE, i=LINE), in_=r_columns[:, t])
         u_bank = {}
 
         def first_product(g):
@@ -194,12 +195,11 @@ def tile_attend_greft_pl_kernel(tc, dyT, R, W, ck, offs, out_0, out_1, out_2):
         scale_u(2)
         quantize_s(2)
         quantize_w(2, 2, w_grouped[2])
-        for g in range(2, GROUPS):
-            if g == 3:
-                scale_u(g)
-                quantize_s(g)
-                add_planes(2, 1, 0, HALF, "bank5")
-            add_planes(0, 2, g * GROUP, (g + 1) * GROUP, "bank%d" % (g - 2))
+        add_planes(0, 2, HALF, HALF + GROUP, "bank0")
+        scale_u(3)
+        quantize_s(3)
+        add_planes(2, 1, 0, HALF, "bank5")
+        add_planes(0, 2, HALF + GROUP, SLOTS, "bank1")
         for t in range(2):
             scatter(t, HALF, SLOTS)
             nc.sync.dma_start(out_planes[:, t, :], window[t][:])
@@ -211,7 +211,7 @@ def tile_attend_greft_pl_kernel(tc, dyT, R, W, ck, offs, out_0, out_1, out_2):
         scatter(last, LAST_SPLIT, SLOTS)
         nc.sync.dma_start(out_planes[:, last, :], window[last][:])
 
-        pairs_early = keep.tile([P, last, 2, PIECE, 2], BF16, name="pairs_early", align_bytes=64)
+        pairs_early = keep.tile([P, PIECES - 1, 2, PIECE, 2], BF16, name="pairs_early", align_bytes=64)
         pairs_last = keep.tile([P, 2, PIECE, 2], BF16, name="pairs_last", tag="third_then_pairs", align_bytes=64)
         pairs = (pairs_early[:, 0], pairs_early[:, 1], pairs_early[:, 2], pairs_last[:])
         pieces = [window[t][:].rearrange("p (k c) -> p k c", k=PIECES) for t in range(LANES)]
@@ -220,9 +220,9 @@ def tile_attend_greft_pl_kernel(tc, dyT, R, W, ck, offs, out_0, out_1, out_2):
             copy(out=pairs[k][:, t // 2, :, t % 2], in_=pieces[t][:, k])
 
         for t in range(2):
-            nc.gpsimd.tensor_scalar(pairs_early[:, :, 0, :, t], pieces[t][:, 0:last], 1.0, 0.0, MULT, ADD)
+            nc.gpsimd.tensor_scalar(pairs_early[:, :, 0, :, t], pieces[t][:, 0:PIECES - 1], 1.0, -0.0, MULT, ADD)
         for t in range(2):
-            round_into_pairs(nc.vector.tensor_copy, t, last)
+            round_into_pairs(nc.vector.tensor_copy, t, PIECES - 1)
         nc.vector.tensor_copy(out=pairs_early[:, 0:2, 1, :, 0], in_=pieces[2][:, 0:2])
         for t in (3, 2):
             for k in (3, 2):
@@ -233,18 +233,17 @@ def tile_attend_greft_pl_kernel(tc, dyT, R, W, ck, offs, out_0, out_1, out_2):
         y_codes = keep.tile([P, TOKENS], U32, name="y_codes", align_bytes=64)
         y_scales = keep.tile([P, TOKENS], U8, name="y_scales", align_bytes=64)
         words_out = out_1[0].rearrange("p c l -> p (c l)").bitcast(I32)
+        piece_order = (0, 1, 3, 2)
         y_grouped = {}
-        for k in (0, 1, 3, 2):
+        for k in piece_order:
             y_grouped[k] = keep.tile([P, PIECE, LANES], BF16, name="y_grouped%d" % k, align_bytes=64)
             copy = nc.vector.tensor_copy if k < 2 else nc.scalar.copy
-            copy(out=y_grouped[k][:].rearrange("p c t -> p (c t)").bitcast(F32).rearrange("p (c i u) -> p c u i", i=4, u=2),
-                 in_=pairs[k].rearrange("p u c e -> p (u c e)").bitcast(F32).rearrange("p (u c i) -> p c u i", u=2, i=4))
-        for k in (0, 1, 3, 2):
+            copy(out=y_grouped[k][:].rearrange("p c t -> p (c t)").bitcast(F32).rearrange("p (c i u) -> p c u i", i=LINE, u=2),
+                 in_=pairs[k].rearrange("p u c e -> p (u c e)").bitcast(F32).rearrange("p (u c i) -> p c u i", u=2, i=LINE))
+        for k in piece_order:
             a = k * PIECE
             quantize(y_codes[:, a:a + PIECE], y_scales[:, a:a + PIECE], y_grouped[k][:], E4M3)
-            if k > 0:
-                first = 0 if k == 1 else a
-                nc.sync.dma_start(words_out[:, first:a + PIECE], y_codes[:, first:a + PIECE].bitcast(I32))
+            nc.sync.dma_start(words_out[:, a:a + PIECE], y_codes[:, a:a + PIECE].bitcast(I32))
         for q in range(4):
             queue = nc.sync if q < 2 else nc.scalar
             queue.dma_start(out_2[0, 4 * q:4 * q + 4, :].bitcast(I32), y_scales[32 * q:32 * q + 4, :].bitcast(I32))

@@ -54,9 +54,9 @@ def tile_attend_greft_pl_kernel(tc, dyT, R, W, ck, offs, out_0, out_1, out_2):
         nc.sync.dma_start(r_raw[:], R.rearrange("(p j) k -> p j k", j=LANES))
         ck_line = keep.tile([1, K], F32, name="ck_line")
         nc.scalar.dma_start(ck_line[:], ck.rearrange("k o -> o k"))
-        w_raw = [keep.tile([P, 2, K], F32, name="w_raw%d" % h) for h in range(2)]
-        for h in range(2):
-            nc.sync.dma_start(w_raw[h][:], w_planes[:, 2 * h:2 * h + 2, :])
+        w_raw = [keep.tile([P, 2, K], F32, name="w_raw%d" % load) for load in range(2)]
+        for load in range(2):
+            nc.sync.dma_start(w_raw[load][:], w_planes[:, 2 * load:2 * load + 2, :])
         window = [keep.tile([P, TOKENS], F32, name="window%d" % t) for t in range(LANES)]
         nc.sync.dma_start(window[last][:], dy_planes[:, last, :])
 
@@ -123,21 +123,21 @@ def tile_attend_greft_pl_kernel(tc, dyT, R, W, ck, offs, out_0, out_1, out_2):
         w_codes = keep.tile([P, LANES, P], U32, name="w_codes", align_bytes=64)
         w_scales = keep.tile([P, LANES, P], U8, name="w_scales", align_bytes=64)
 
-        w_sorted = [keep.tile([P, 2 * K], BF16, name="w_sorted%d" % h, align_bytes=64) for h in range(2)]
-        for h in range(2):
-            nc.scalar.copy(out=w_sorted[h][:].rearrange("m (u b i e) -> m u b e i", u=2, i=RUN, e=2),
-                           in_=w_raw[h][:].rearrange("m n (b u e i) -> m u (n b) e i", u=2, i=RUN, e=2))
+        w_sorted = [keep.tile([P, 2 * K], BF16, name="w_sorted%d" % load, align_bytes=64) for load in range(2)]
+        for load in range(2):
+            nc.scalar.copy(out=w_sorted[load][:].rearrange("m (pair b i e) -> m pair b e i", pair=2, i=RUN, e=2),
+                           in_=w_raw[load][:].rearrange("m n (b pair e i) -> m pair (n b) e i", pair=2, i=RUN, e=2))
 
         def turn_w(t, count, bank):
             turned = psum.tile([P, count, 2, P], F32, name="turned%d" % t, tag=bank)
-            words = w_sorted[t // 2][:].bitcast(F32).rearrange("m (u n p) -> m u n p", u=2, n=2)
+            words = w_sorted[t // 2][:].bitcast(F32).rearrange("m (pair n p) -> m pair n p", pair=2, n=2)
             for n in range(count):
-                for u in range(2):
-                    nc.tensor.transpose(turned[:, n, u, :], words[:, u, t % 2 + n, :], ident[:])
-            w_grouped = keep.tile([P, count * P, LANES], BF16, name="w_grouped%d" % t, align_bytes=64)
-            nc.scalar.copy(out=w_grouped[:].rearrange("p m t -> p (m t)").bitcast(F32).rearrange("p (n m u) -> p n m u", n=count, u=2),
-                           in_=turned[:].rearrange("p n u m -> p n m u"))
-            return w_grouped
+                for pair in range(2):
+                    nc.tensor.transpose(turned[:, n, pair, :], words[:, pair, t % 2 + n, :], ident[:])
+            grouped = keep.tile([P, count * P, LANES], BF16, name="w_grouped%d" % t, align_bytes=64)
+            nc.scalar.copy(out=grouped[:].rearrange("p m t -> p (m t)").bitcast(F32).rearrange("p (n m pair) -> p n m pair", n=count, pair=2),
+                           in_=turned[:].rearrange("p n pair m -> p n m pair"))
+            return grouped
 
         def quantize_w(t, count, grouped):
             quantize(w_codes[:, t:t + count, :].rearrange("p n m -> p (n m)"), w_scales[:, t:t + count, :].rearrange("p n m -> p (n m)"),
@@ -214,10 +214,10 @@ def tile_attend_greft_pl_kernel(tc, dyT, R, W, ck, offs, out_0, out_1, out_2):
         pairs_early = keep.tile([P, PIECES - 1, 2, PIECE, 2], BF16, name="pairs_early", align_bytes=64)
         pairs_last = keep.tile([P, 2, PIECE, 2], BF16, name="pairs_last", tag="third_then_pairs", align_bytes=64)
         pairs = (pairs_early[:, 0], pairs_early[:, 1], pairs_early[:, 2], pairs_last[:])
-        pieces = [window[t][:].rearrange("p (k c) -> p k c", k=PIECES) for t in range(LANES)]
+        pieces = [window[t][:].rearrange("p (piece c) -> p piece c", piece=PIECES) for t in range(LANES)]
 
-        def round_into_pairs(copy, t, k):
-            copy(out=pairs[k][:, t // 2, :, t % 2], in_=pieces[t][:, k])
+        def round_into_pairs(copy, t, piece):
+            copy(out=pairs[piece][:, t // 2, :, t % 2], in_=pieces[t][:, piece])
 
         for t in range(2):
             nc.gpsimd.tensor_scalar(pairs_early[:, :, 0, :, t], pieces[t][:, 0:PIECES - 1], 1.0, -0.0, MULT, ADD)
@@ -225,25 +225,29 @@ def tile_attend_greft_pl_kernel(tc, dyT, R, W, ck, offs, out_0, out_1, out_2):
             round_into_pairs(nc.vector.tensor_copy, t, PIECES - 1)
         nc.vector.tensor_copy(out=pairs_early[:, 0:2, 1, :, 0], in_=pieces[2][:, 0:2])
         for t in (3, 2):
-            for k in (3, 2):
-                round_into_pairs(nc.scalar.copy, t, k)
-        for k in range(2):
-            round_into_pairs(nc.vector.tensor_copy, last, k)
+            for piece in (3, 2):
+                round_into_pairs(nc.scalar.copy, t, piece)
+        for piece in range(2):
+            round_into_pairs(nc.vector.tensor_copy, last, piece)
 
         y_codes = keep.tile([P, TOKENS], U32, name="y_codes", align_bytes=64)
         y_scales = keep.tile([P, TOKENS], U8, name="y_scales", align_bytes=64)
         words_out = out_1[0].rearrange("p c l -> p (c l)").bitcast(I32)
         piece_order = (0, 1, 3, 2)
         y_grouped = {}
-        for k in piece_order:
-            y_grouped[k] = keep.tile([P, PIECE, LANES], BF16, name="y_grouped%d" % k, align_bytes=64)
-            copy = nc.vector.tensor_copy if k < 2 else nc.scalar.copy
-            copy(out=y_grouped[k][:].rearrange("p c t -> p (c t)").bitcast(F32).rearrange("p (c i u) -> p c u i", i=LINE, u=2),
-                 in_=pairs[k].rearrange("p u c e -> p (u c e)").bitcast(F32).rearrange("p (u c i) -> p c u i", u=2, i=LINE))
-        for k in piece_order:
-            a = k * PIECE
-            quantize(y_codes[:, a:a + PIECE], y_scales[:, a:a + PIECE], y_grouped[k][:], E4M3)
-            nc.sync.dma_start(words_out[:, a:a + PIECE], y_codes[:, a:a + PIECE].bitcast(I32))
+        for piece in piece_order:
+            y_grouped[piece] = keep.tile([P, PIECE, LANES], BF16, name="y_grouped%d" % piece, align_bytes=64)
+            joined = y_grouped[piece][:].rearrange("p c t -> p (c t)").bitcast(F32)
+            apart = pairs[piece].rearrange("p pair c e -> p (pair c e)").bitcast(F32)
+            copy = nc.vector.tensor_copy if piece < 2 else nc.scalar.copy
+            copy(out=joined.rearrange("p (c i pair) -> p c pair i", i=LINE, pair=2),
+                 in_=apart.rearrange("p (pair c i) -> p c pair i", pair=2, i=LINE))
+        for piece in piece_order:
+            columns = slice(piece * PIECE, (piece + 1) * PIECE)
+            quantize(y_codes[:, columns], y_scales[:, columns], y_grouped[piece][:], E4M3)
+            if piece > 0:
+                stored = slice(0, 2 * PIECE) if piece == 1 else columns
+                nc.sync.dma_start(words_out[:, stored], y_codes[:, stored].bitcast(I32))
         for q in range(4):
             queue = nc.sync if q < 2 else nc.scalar
             queue.dma_start(out_2[0, 4 * q:4 * q + 4, :].bitcast(I32), y_scales[32 * q:32 * q + 4, :].bitcast(I32))

@@ -85,7 +85,6 @@ def tile_attend_greft_pl_kernel(tc, dyT, R, W, ck, offs, out_0, out_1, out_2):
 
         picked = keep.tile([P, LANES, SLOTS], F32, name="picked")
         dy_grouped = keep.tile([P, SLOTS, LANES], BF16, name="dy_grouped", align_bytes=64)
-        dy_codes = keep.tile([P, SLOTS], U32, name="dy_codes", align_bytes=64)
         dy_scales = keep.tile([P, SLOTS], U8, name="dy_scales", align_bytes=64)
 
         for t in range(last):
@@ -100,13 +99,14 @@ def tile_attend_greft_pl_kernel(tc, dyT, R, W, ck, offs, out_0, out_1, out_2):
 
         for g in range(GROUPS):
             weave(nc.vector.tensor_copy if g < GROUPS // 2 else nc.scalar.copy, dy_grouped[:, group(g), :], picked[:, :, group(g)])
-        for g in range(GROUPS):
-            quantize(dy_codes[:, group(g)], dy_scales[:, group(g)], dy_grouped[:, group(g), :], E5M2)
+        dy_codes = [keep.tile([P, HALF], U32, name="dy_codes0", align_bytes=64)]
+        for g in range(2):
+            quantize(dy_codes[0][:, group(g)], dy_scales[:, group(g)], dy_grouped[:, group(g), :], E5M2)
 
         r_codes = keep.tile([P, LANES, P], U32, name="r_codes", align_bytes=64)
         r_scales = keep.tile([P, LANES, P], U8, name="r_scales", align_bytes=64)
         r_columns = r_raw[:].rearrange("p j (b t h i) -> p t b h j i", t=LANES, h=RUN // LINE, i=LINE)
-        r_grouped = [keep.tile([P, P, LANES], BF16, name="r_grouped%d" % t, align_bytes=64) for t in range(LANES)]
+        r_grouped = [keep.tile([P, P, LANES], BF16, name="r_grouped%d" % t, tag="r_grouped%d" % t, align_bytes=64) for t in range(LANES)]
         for t in range(LANES):
             copy = nc.vector.tensor_copy if t < last else nc.scalar.copy
             copy(out=r_grouped[t][:].rearrange("p (b h i) j -> p b h j i", h=RUN // LINE, i=LINE), in_=r_columns[:, t])
@@ -118,7 +118,7 @@ def tile_attend_greft_pl_kernel(tc, dyT, R, W, ck, offs, out_0, out_1, out_2):
                 if g == 0:
                     quantize(r_codes[:, t, :], r_scales[:, t, :], r_grouped[t][:], E4M3)
                 nc.tensor.matmul_mx(out=u_bank[g][:, t, :], lhsT=r_codes[:, t, :].bitcast(E4M3), lhsT_scale=r_scales[:, t, :],
-                                    rhs=dy_codes[:, group(g)].bitcast(E5M2), rhs_scale=dy_scales[:, group(g)], start=True, stop=True)
+                                    rhs=dy_codes[g // 2][:, group(g % 2)].bitcast(E5M2), rhs_scale=dy_scales[:, group(g)], start=True, stop=True)
 
         w_codes = keep.tile([P, LANES, P], U32, name="w_codes", align_bytes=64)
         w_scales = keep.tile([P, LANES, P], U8, name="w_scales", align_bytes=64)
@@ -144,6 +144,8 @@ def tile_attend_greft_pl_kernel(tc, dyT, R, W, ck, offs, out_0, out_1, out_2):
                      grouped[:], E4M3)
 
         first_product(0)
+        dy_codes.append(keep.tile([P, HALF], U32, name="dy_codes1", tag="r_grouped2", align_bytes=64))
+        quantize(dy_codes[1][:], dy_scales[:, HALF:SLOTS], dy_grouped[:, HALF:SLOTS, :], E5M2)
         s_grouped = keep.tile([P, SLOTS, LANES], BF16, name="s_grouped", align_bytes=64)
         s_codes = keep.tile([P, SLOTS], U32, name="s_codes", align_bytes=64)
         s_scales = keep.tile([P, SLOTS], U8, name="s_scales", align_bytes=64)

@@ -223,14 +223,13 @@ def tile_attend_greft_pl_kernel(tc, dyT, R, W, ck, offs, out_0, out_1, out_2):
 
         for t in range(2):
             nc.gpsimd.tensor_scalar(pairs_early[:, :, 0, :, t], pieces[t][:, 0:PIECES - 1], 1.0, -0.0, MULT, ADD)
+        nc.vector.tensor_copy(out=pairs_early[:, 0:2, 1, :, 1], in_=pieces[last][:, 0:2])
+        nc.vector.tensor_copy(out=pairs_early[:, 0:2, 1, :, 0], in_=pieces[2][:, 0:2])
         for t in range(2):
             round_into_pairs(nc.vector.tensor_copy, t, PIECES - 1)
-        nc.vector.tensor_copy(out=pairs_early[:, 0:2, 1, :, 0], in_=pieces[2][:, 0:2])
         for t in (3, 2):
             for piece in (3, 2):
                 round_into_pairs(nc.scalar.copy, t, piece)
-        for piece in range(2):
-            round_into_pairs(nc.vector.tensor_copy, last, piece)
 
         y_codes = keep.tile([P, TOKENS], U32, name="y_codes", align_bytes=64)
         y_scales = keep.tile([P, TOKENS], U8, name="y_scales", align_bytes=64)

@@ -29,7 +29,6 @@ GROUP = 128
 GROUPS = SLOTS // GROUP
 PIECE = 256
 PIECES = TOKENS // PIECE
-LAST_SPLIT = 320
 
 FLOPS = 2 * 2 * D * K * SLOTS
 
@@ -63,6 +62,8 @@ def tile_attend_greft_pl_kernel(tc, dyT, R, W, ck, offs, out_0, out_1, out_2):
         ident = keep.tile([P, P], F32, name="ident")
         make_identity(nc, ident[:])
 
+        one = keep.tile([P, 1], F32, name="one")
+        nc.vector.memset(one[:], 1.0)
         ck_dealt = keep.tile([P, K], F32, name="ck_dealt")
         nc.vector.memset(ck_dealt[:], 0.0)
         nc.gpsimd.tensor_scalar(ck_dealt[0:1, :].rearrange("o (t b i) -> o t b i", t=LANES, i=RUN),
@@ -82,6 +83,34 @@ def tile_attend_greft_pl_kernel(tc, dyT, R, W, ck, offs, out_0, out_1, out_2):
 
         def group(g):
             return slice(g * GROUP, (g + 1) * GROUP)
+
+        w_codes = keep.tile([P, LANES, P], U32, name="w_codes", align_bytes=64)
+        w_scales = keep.tile([P, LANES, P], U8, name="w_scales", align_bytes=64)
+
+        def sort_w(t):
+            words = keep.tile([P, K], BF16, name="w_sorted%d" % t, align_bytes=64)
+            out = words[:].rearrange("m (pair b i e) -> m pair b e i", pair=2, i=RUN, e=2)
+            raw = w_raw[t // 2][:, t % 2, :].rearrange("m (b pair e i) -> m pair b e i", pair=2, i=RUN, e=2)
+            if t < last:
+                nc.scalar.copy(out=out, in_=raw)
+            else:
+                for pair in range(2):
+                    nc.gpsimd.tensor_scalar(out[:, pair], raw[:, pair], 1.0, -0.0, MULT, ADD)
+            return words[:].bitcast(F32).rearrange("m (pair p) -> m pair p", pair=2)
+
+        def turn_w(t, count, bank):
+            turned = psum.tile([P, count, 2, P], F32, name="turned%d" % t, tag=bank)
+            for n in range(count):
+                for pair in range(2):
+                    nc.tensor.transpose(turned[:, n, pair, :], w_words[t + n][:, pair, :], ident[:])
+            grouped = keep.tile([P, count * P, LANES], BF16, name="w_grouped%d" % t, align_bytes=64)
+            nc.scalar.copy(out=grouped[:].rearrange("p m t -> p (m t)").bitcast(F32).rearrange("p (n m pair) -> p n m pair", n=count, pair=2),
+                           in_=turned[:].rearrange("p n pair m -> p n m pair"))
+            return grouped
+
+        def quantize_w(t, count, grouped):
+            quantize(w_codes[:, t:t + count, :].rearrange("p n m -> p (n m)"), w_scales[:, t:t + count, :].rearrange("p n m -> p (n m)"),
+                     grouped[:], E4M3)
 
         picked = keep.tile([P, LANES, SLOTS], F32, name="picked")
         dy_grouped = keep.tile([P, SLOTS, LANES], BF16, name="dy_grouped", align_bytes=64)
@@ -106,46 +135,32 @@ def tile_attend_greft_pl_kernel(tc, dyT, R, W, ck, offs, out_0, out_1, out_2):
         r_codes = keep.tile([P, LANES, P], U32, name="r_codes", align_bytes=64)
         r_scales = keep.tile([P, LANES, P], U8, name="r_scales", align_bytes=64)
         r_columns = r_raw[:].rearrange("p j (b t h i) -> p t b h j i", t=LANES, h=RUN // LINE, i=LINE)
-        r_grouped = [keep.tile([P, P, LANES], BF16, name="r_grouped%d" % t, tag="r_grouped%d" % t, align_bytes=64) for t in range(LANES)]
-        for t in range(LANES):
-            copy = nc.vector.tensor_copy if t < last else nc.scalar.copy
-            copy(out=r_grouped[t][:].rearrange("p (b h i) j -> p b h j i", h=RUN // LINE, i=LINE), in_=r_columns[:, t])
+        r_grouped = [keep.tile([P, 2, P, LANES], BF16, name="r_grouped%d" % n, tag="r_grouped%d" % n, align_bytes=64) for n in range(2)]
+        blocks = P // RUN
+
+        def deal_r(copy, t, a, b):
+            copy(out=r_grouped[t // 2][:, t % 2].rearrange("p (b h i) j -> p b h j i", h=RUN // LINE, i=LINE)[:, a:b], in_=r_columns[:, t, a:b])
+
+        deal_r(nc.vector.tensor_copy, 0, 0, blocks)
+        deal_r(nc.vector.tensor_copy, 1, 0, blocks)
+        deal_r(nc.vector.tensor_copy, 2, 0, blocks // 2)
+        deal_r(nc.scalar.copy, 3, 0, blocks)
+        deal_r(nc.scalar.copy, 2, blocks // 2, blocks)
         u_bank = {}
 
         def first_product(g):
-            u_bank[g] = psum.tile([P, LANES, GROUP], F32, name="u_bank%d" % g, tag="bank%d" % g)
+            u_bank[g] = psum.tile([P, LANES, GROUP], F32, name="u_bank%d" % g, tag="bank%d" % (g % 3))
             for t in range(LANES):
-                if g == 0:
-                    quantize(r_codes[:, t, :], r_scales[:, t, :], r_grouped[t][:], E4M3)
+                if g == 0 and t % 2 == 0:
+                    quantize(r_codes[:, t:t + 2, :].rearrange("p n m -> p (n m)"), r_scales[:, t:t + 2, :].rearrange("p n m -> p (n m)"),
+                             r_grouped[t // 2][:].rearrange("p n m j -> p (n m) j"), E4M3)
                 nc.tensor.matmul_mx(out=u_bank[g][:, t, :], lhsT=r_codes[:, t, :].bitcast(E4M3), lhsT_scale=r_scales[:, t, :],
                                     rhs=dy_codes[g // 2][:, group(g % 2)].bitcast(E5M2), rhs_scale=dy_scales[:, group(g)], start=True, stop=True)
 
-        w_codes = keep.tile([P, LANES, P], U32, name="w_codes", align_bytes=64)
-        w_scales = keep.tile([P, LANES, P], U8, name="w_scales", align_bytes=64)
-
-        w_sorted = [keep.tile([P, 2 * K], BF16, name="w_sorted%d" % load, align_bytes=64) for load in range(2)]
-        for load in range(2):
-            nc.scalar.copy(out=w_sorted[load][:].rearrange("m (pair b i e) -> m pair b e i", pair=2, i=RUN, e=2),
-                           in_=w_raw[load][:].rearrange("m n (b pair e i) -> m pair (n b) e i", pair=2, i=RUN, e=2))
-
-        def turn_w(t, count, bank):
-            turned = psum.tile([P, count, 2, P], F32, name="turned%d" % t, tag=bank)
-            words = w_sorted[t // 2][:].bitcast(F32).rearrange("m (pair n p) -> m pair n p", pair=2, n=2)
-            for n in range(count):
-                for pair in range(2):
-                    nc.tensor.transpose(turned[:, n, pair, :], words[:, pair, t % 2 + n, :], ident[:])
-            grouped = keep.tile([P, count * P, LANES], BF16, name="w_grouped%d" % t, align_bytes=64)
-            nc.scalar.copy(out=grouped[:].rearrange("p m t -> p (m t)").bitcast(F32).rearrange("p (n m pair) -> p n m pair", n=count, pair=2),
-                           in_=turned[:].rearrange("p n pair m -> p n m pair"))
-            return grouped
-
-        def quantize_w(t, count, grouped):
-            quantize(w_codes[:, t:t + count, :].rearrange("p n m -> p (n m)"), w_scales[:, t:t + count, :].rearrange("p n m -> p (n m)"),
-                     grouped[:], E4M3)
-
         first_product(0)
-        dy_codes.append(keep.tile([P, HALF], U32, name="dy_codes1", tag="r_grouped2", align_bytes=64))
+        dy_codes.append(keep.tile([P, HALF], U32, name="dy_codes1", tag="r_grouped1", align_bytes=64))
         quantize(dy_codes[1][:], dy_scales[:, HALF:SLOTS], dy_grouped[:, HALF:SLOTS, :], E5M2)
+        w_words = [sort_w(t) for t in range(LANES)]
         s_grouped = keep.tile([P, SLOTS, LANES], BF16, name="s_grouped", align_bytes=64)
         s_codes = keep.tile([P, SLOTS], U32, name="s_codes", align_bytes=64)
         s_scales = keep.tile([P, SLOTS], U8, name="s_scales", align_bytes=64)
@@ -156,94 +171,81 @@ def tile_attend_greft_pl_kernel(tc, dyT, R, W, ck, offs, out_0, out_1, out_2):
         def quantize_s(g):
             quantize(s_codes[:, group(g)], s_scales[:, group(g)], s_grouped[:, group(g), :], E5M2)
 
-        def second_product(out, t, slots):
-            nc.tensor.matmul_mx(out=out, lhsT=w_codes[:, t, :].bitcast(E4M3), lhsT_scale=w_scales[:, t, :],
-                                rhs=s_codes[:, slots].bitcast(E5M2), rhs_scale=s_scales[:, slots], start=True, stop=True)
+        new = keep.tile([P, LANES, SLOTS], F32, name="new")
 
-        new_early = keep.tile([P, 2, SLOTS], F32, name="new_early")
-        new_third = keep.tile([P, 1, SLOTS], F32, name="new_third", tag="third_then_pairs", align_bytes=64)
-        new_last = keep.tile([P, 1, SLOTS], F32, name="new_last")
-        new = (new_early[:, 0:2], new_early[:, 1:2], new_third[:], new_last[:])
-
-        def add_planes(first, count, a, b, bank):
+        def add_planes(first, count, bank, *cuts):
+            a, b = cuts[0], cuts[-1]
             v_bank = psum.tile([P, count, b - a], F32, name="v_bank%d_%d" % (first, a), tag=bank)
             for n in range(count):
-                second_product(v_bank[:, n, :], first + n, slice(a, b))
-            nc.vector.tensor_tensor(new[first][:, 0:count, a:b], v_bank[:], picked[:, first:first + count, a:b], ADD)
+                for lo, hi in zip(cuts, cuts[1:]):
+                    nc.tensor.matmul_mx(out=v_bank[:, n, lo - a:hi - a], lhsT=w_codes[:, first + n, :].bitcast(E4M3), lhsT_scale=w_scales[:, first + n, :],
+                                        rhs=s_codes[:, lo:hi].bitcast(E5M2), rhs_scale=s_scales[:, lo:hi], start=True, stop=True)
+            nc.vector.tensor_tensor(new[:, first:first + count, a:b], v_bank[:], picked[:, first:first + count, a:b], ADD)
 
         def scatter(t, a, b, on_vector=False):
             if on_vector:
-                nc.vector.tensor_copy(window[t][:].indirect(slot_offsets(a, b)), new[t][:, 0, a:b])
+                nc.vector.tensor_copy(window[t][:].indirect(slot_offsets(a, b)), new[:, t, a:b])
             else:
-                nc.scalar.activation(out=window[t][:].indirect(slot_offsets(a, b)), in_=new[t][:, 0, a:b], func=COPY)
+                nc.scalar.activation(out=window[t][:].indirect(slot_offsets(a, b)), in_=new[:, t, a:b], func=COPY)
+
+        def store_plane(t):
+            nc.sync.dma_start(out_planes[:, t, :], window[t][:])
 
         first_product(1)
+        w_grouped = {0: turn_w(0, 1, "bank6"), 1: turn_w(1, 1, "bank7")}
         scale_u(0)
-        w_grouped = [turn_w(0, 1, "bank7"), turn_w(1, 1, "bank6"), turn_w(2, 2, "bank5")]
         quantize_w(0, 1, w_grouped[0])
         quantize_s(0)
-        add_planes(0, 1, 0, GROUP, "bank4")
-        scatter(0, 0, GROUP)
-        quantize_w(1, 1, w_grouped[1])
-        add_planes(1, 1, 0, GROUP, "bank7")
-        scatter(1, 0, GROUP)
-        scale_u(1)
-        quantize_s(1)
-        add_planes(0, 2, GROUP, HALF, "bank6")
-        for t in range(2):
-            scatter(t, GROUP, HALF)
+        add_planes(0, 1, "bank4", 0, GROUP)
         first_product(2)
+        w_grouped[2] = turn_w(2, 2, "bank5")
         first_product(3)
-        scale_u(2)
-        quantize_s(2)
+        scatter(0, 0, GROUP)
+        scale_u(1)
+        quantize_w(1, 1, w_grouped[1])
+        quantize_s(1)
         quantize_w(2, 2, w_grouped[2])
-        add_planes(0, 2, HALF, HALF + GROUP, "bank0")
+        add_planes(1, 1, "bank3", 0, HALF)
+        scatter(1, 0, HALF)
+        scale_u(2)
         scale_u(3)
-        quantize_s(3)
-        add_planes(2, 1, 0, HALF, "bank5")
-        add_planes(0, 2, HALF + GROUP, SLOTS, "bank1")
-        for t in range(2):
-            scatter(t, HALF, SLOTS)
-            nc.sync.dma_start(out_planes[:, t, :], window[t][:])
-        add_planes(last, 1, 0, SLOTS, "bank2")
-        add_planes(2, 1, HALF, SLOTS, "bank4")
-        scatter(last, 0, LAST_SPLIT, on_vector=True)
-        scatter(2, 0, SLOTS, on_vector=True)
-        nc.sync.dma_start(out_planes[:, 2, :], window[2][:])
-        scatter(last, LAST_SPLIT, SLOTS)
-        nc.sync.dma_start(out_planes[:, last, :], window[last][:])
+        quantize(s_codes[:, HALF:SLOTS], s_scales[:, HALF:SLOTS], s_grouped[:, HALF:SLOTS, :], E5M2)
+        add_planes(2, 2, "bank1", 0, HALF)
+        add_planes(0, 1, "bank6", GROUP, HALF, SLOTS)
+        add_planes(last, 1, "bank7", HALF, SLOTS)
+        add_planes(1, 2, "bank4", HALF, SLOTS)
 
-        pairs_early = keep.tile([P, PIECES - 1, 2, PIECE, 2], BF16, name="pairs_early", align_bytes=64)
-        pairs_last = keep.tile([P, 2, PIECE, 2], BF16, name="pairs_last", tag="third_then_pairs", align_bytes=64)
-        pairs = (pairs_early[:, 0], pairs_early[:, 1], pairs_early[:, 2], pairs_last[:])
+        pairs = keep.tile([P, PIECES, 2, PIECE, 2], BF16, name="pairs", align_bytes=64)
         pieces = [window[t][:].rearrange("p (piece c) -> p piece c", piece=PIECES) for t in range(LANES)]
 
-        def round_into_pairs(copy, t, piece):
-            copy(out=pairs[piece][:, t // 2, :, t % 2], in_=pieces[t][:, piece])
-
-        for t in range(2):
-            nc.gpsimd.tensor_scalar(pairs_early[:, :, 0, :, t], pieces[t][:, 0:PIECES - 1], 1.0, -0.0, MULT, ADD)
-        nc.vector.tensor_copy(out=pairs_early[:, 0:2, 1, :, 1], in_=pieces[last][:, 0:2])
-        nc.vector.tensor_copy(out=pairs_early[:, 0:2, 1, :, 0], in_=pieces[2][:, 0:2])
-        for t in range(2):
-            round_into_pairs(nc.vector.tensor_copy, t, PIECES - 1)
-        for t in (3, 2):
-            for piece in (3, 2):
-                round_into_pairs(nc.scalar.copy, t, piece)
+        scatter(0, GROUP, SLOTS)
+        store_plane(0)
+        nc.gpsimd.tensor_scalar(pairs[:, :, 0, :, 0], pieces[0], 1.0, -0.0, MULT, ADD)
+        scatter(1, HALF, SLOTS, on_vector=True)
+        store_plane(1)
+        nc.gpsimd.tensor_scalar(pairs[:, :, 0, :, 1], pieces[1], 1.0, -0.0, MULT, ADD)
+        nc.scalar.activation(out=window[last][:].indirect(offsets[:]), in_=new[:, last, :], func=COPY, scale=one[:])
+        store_plane(last)
+        scatter(2, 0, SLOTS, on_vector=True)
+        store_plane(2)
+        for t in (last, 2):
+            nc.vector.tensor_copy(out=pairs[:, 0:2, 1, :, t % 2], in_=pieces[t][:, 0:2])
+        nc.scalar.copy(out=pairs[:, 2:4, 1, :, 1], in_=pieces[last][:, 2:4])
+        for piece in (3, 2):
+            nc.scalar.copy(out=pairs[:, piece, 1, :, 0], in_=pieces[2][:, piece])
 
         y_codes = keep.tile([P, TOKENS], U32, name="y_codes", align_bytes=64)
         y_scales = keep.tile([P, TOKENS], U8, name="y_scales", align_bytes=64)
         words_out = out_1[0].rearrange("p c l -> p (c l)").bitcast(I32)
-        piece_order = (0, 1, 3, 2)
         y_grouped = {}
-        for piece in piece_order:
+        for piece in (0, 1, 3, 2):
             y_grouped[piece] = keep.tile([P, PIECE, LANES], BF16, name="y_grouped%d" % piece, align_bytes=64)
             joined = y_grouped[piece][:].rearrange("p c t -> p (c t)").bitcast(F32)
-            apart = pairs[piece].rearrange("p pair c e -> p (pair c e)").bitcast(F32)
+            apart = pairs[:, piece].rearrange("p pair c e -> p (pair c e)").bitcast(F32)
             copy = nc.vector.tensor_copy if piece < 2 else nc.scalar.copy
             copy(out=joined.rearrange("p (c i pair) -> p c pair i", i=LINE, pair=2),
                  in_=apart.rearrange("p (pair c i) -> p c pair i", pair=2, i=LINE))
-        for piece in piece_order:
+        for piece in (0, 1, 3, 2):
             columns = slice(piece * PIECE, (piece + 1) * PIECE)
             quantize(y_codes[:, columns], y_scales[:, columns], y_grouped[piece][:], E4M3)
             if piece > 0:

@@ -149,11 +149,13 @@ def tile_attend_greft_pl_kernel(tc, dyT, R, W, ck, offs, out_0, out_1, out_2):
         u_bank = {}
 
         def first_product(g):
-            u_bank[g] = psum.tile([P, LANES, GROUP], F32, name="u_bank%d" % g, tag="bank%d" % (g % 3))
+            u_bank[g] = psum.tile([P, LANES, GROUP], F32, name="u_bank%d" % g, tag="bank%d" % (g if g < 3 else 1))
             for t in range(LANES):
-                if g == 0 and t % 2 == 0:
-                    quantize(r_codes[:, t:t + 2, :].rearrange("p n m -> p (n m)"), r_scales[:, t:t + 2, :].rearrange("p n m -> p (n m)"),
-                             r_grouped[t // 2][:].rearrange("p n m j -> p (n m) j"), E4M3)
+                if g == 0 and t < 2:
+                    quantize(r_codes[:, t, :], r_scales[:, t, :], r_grouped[0][:, t], E4M3)
+                if g == 0 and t == 2:
+                    quantize(r_codes[:, 2:4, :].rearrange("p n m -> p (n m)"), r_scales[:, 2:4, :].rearrange("p n m -> p (n m)"),
+                             r_grouped[1][:].rearrange("p n m j -> p (n m) j"), E4M3)
                 nc.tensor.matmul_mx(out=u_bank[g][:, t, :], lhsT=r_codes[:, t, :].bitcast(E4M3), lhsT_scale=r_scales[:, t, :],
                                     rhs=dy_codes[g // 2][:, group(g % 2)].bitcast(E5M2), rhs_scale=dy_scales[:, group(g)], start=True, stop=True)
 
@@ -204,14 +206,14 @@ def tile_attend_greft_pl_kernel(tc, dyT, R, W, ck, offs, out_0, out_1, out_2):
         scale_u(1)
         quantize_w(1, 1, w_grouped[1])
         quantize_s(1)
-        quantize_w(2, 2, w_grouped[2])
         add_planes(1, 1, "bank3", 0, HALF)
         scatter(1, 0, HALF)
+        quantize_w(2, 2, w_grouped[2])
         scale_u(2)
         scale_u(3)
         quantize(s_codes[:, HALF:SLOTS], s_scales[:, HALF:SLOTS], s_grouped[:, HALF:SLOTS, :], E5M2)
-        add_planes(2, 2, "bank1", 0, HALF)
         add_planes(0, 1, "bank6", GROUP, HALF, SLOTS)
+        add_planes(2, 2, "bank0", 0, HALF)
         add_planes(last, 1, "bank7", HALF, SLOTS)
         add_planes(1, 2, "bank4", HALF, SLOTS)
 
@@ -228,24 +230,25 @@ def tile_attend_greft_pl_kernel(tc, dyT, R, W, ck, offs, out_0, out_1, out_2):
         store_plane(last)
         scatter(2, 0, SLOTS, on_vector=True)
         store_plane(2)
-        for t in (last, 2):
-            nc.vector.tensor_copy(out=pairs[:, 0:2, 1, :, t % 2], in_=pieces[t][:, 0:2])
+        nc.vector.tensor_copy(out=pairs[:, 0:2, 1, :, 1], in_=pieces[last][:, 0:2])
+        for piece in range(2):
+            nc.vector.tensor_copy(out=pairs[:, piece, 1, :, 0], in_=pieces[2][:, piece])
         nc.scalar.copy(out=pairs[:, 2:4, 1, :, 1], in_=pieces[last][:, 2:4])
-        for piece in (3, 2):
+        for piece in (2, 3):
             nc.scalar.copy(out=pairs[:, piece, 1, :, 0], in_=pieces[2][:, piece])
 
         y_codes = keep.tile([P, TOKENS], U32, name="y_codes", align_bytes=64)
         y_scales = keep.tile([P, TOKENS], U8, name="y_scales", align_bytes=64)
         words_out = out_1[0].rearrange("p c l -> p (c l)").bitcast(I32)
         y_grouped = {}
-        for piece in (0, 1, 3, 2):
+        for piece in range(PIECES):
             y_grouped[piece] = keep.tile([P, PIECE, LANES], BF16, name="y_grouped%d" % piece, align_bytes=64)
             joined = y_grouped[piece][:].rearrange("p c t -> p (c t)").bitcast(F32)
             apart = pairs[:, piece].rearrange("p pair c e -> p (pair c e)").bitcast(F32)
-            copy = nc.vector.tensor_copy if piece < 2 else nc.scalar.copy
+            copy = nc.vector.tensor_copy if piece < 3 else nc.scalar.copy
             copy(out=joined.rearrange("p (c i pair) -> p c pair i", i=LINE, pair=2),
                  in_=apart.rearrange("p (pair c i) -> p c pair i", pair=2, i=LINE))
-        for piece in (0, 1, 3, 2):
+        for piece in range(PIECES):
             columns = slice(piece * PIECE, (piece + 1) * PIECE)
             quantize(y_codes[:, columns], y_scales[:, columns], y_grouped[piece][:], E4M3)
             if piece > 0:

@@ -234,21 +234,27 @@ def tile_attend_greft_pl_kernel(tc, dyT, R, W, ck, offs, out_0, out_1, out_2):
         for piece in range(2):
             nc.vector.tensor_copy(out=pairs[:, piece, 1, :, 0], in_=pieces[2][:, piece])
         nc.scalar.copy(out=pairs[:, 2:4, 1, :, 1], in_=pieces[last][:, 2:4])
-        for piece in (2, 3):
+        for piece in (3, 2):
             nc.scalar.copy(out=pairs[:, piece, 1, :, 0], in_=pieces[2][:, piece])
 
         y_codes = keep.tile([P, TOKENS], U32, name="y_codes", align_bytes=64)
         y_scales = keep.tile([P, TOKENS], U8, name="y_scales", align_bytes=64)
         words_out = out_1[0].rearrange("p c l -> p (c l)").bitcast(I32)
-        y_grouped = {}
-        for piece in range(PIECES):
-            y_grouped[piece] = keep.tile([P, PIECE, LANES], BF16, name="y_grouped%d" % piece, align_bytes=64)
+        y_grouped = [keep.tile([P, PIECE, LANES], BF16, name="y_grouped%d" % piece, align_bytes=64) for piece in range(PIECES)]
+
+        def join(copy, piece, a, b):
             joined = y_grouped[piece][:].rearrange("p c t -> p (c t)").bitcast(F32)
             apart = pairs[:, piece].rearrange("p pair c e -> p (pair c e)").bitcast(F32)
-            copy = nc.vector.tensor_copy if piece < 3 else nc.scalar.copy
-            copy(out=joined.rearrange("p (c i pair) -> p c pair i", i=LINE, pair=2),
-                 in_=apart.rearrange("p (pair c i) -> p c pair i", pair=2, i=LINE))
-        for piece in range(PIECES):
+            copy(out=joined.rearrange("p (c i pair) -> p c pair i", i=LINE, pair=2)[:, a // LINE:b // LINE],
+                 in_=apart.rearrange("p (pair c i) -> p c pair i", pair=2, i=LINE)[:, a // LINE:b // LINE])
+
+        join(nc.vector.tensor_copy, 0, 0, PIECE)
+        join(nc.vector.tensor_copy, 1, 0, PIECE)
+        join(nc.scalar.copy, 3, 0, PIECE)
+        join(nc.scalar.copy, 2, PIECE // 2, PIECE)
+        for piece in (0, 1, 3, 2):
+            if piece == 3:
+                join(nc.vector.tensor_copy, 2, 0, PIECE // 2)
             columns = slice(piece * PIECE, (piece + 1) * PIECE)
             quantize(y_codes[:, columns], y_scales[:, columns], y_grouped[piece][:], E4M3)
             if piece > 0:

@@ -251,10 +251,9 @@ def tile_attend_greft_pl_kernel(tc, dyT, R, W, ck, offs, out_0, out_1, out_2):
         join(nc.vector.tensor_copy, 0, 0, PIECE)
         join(nc.vector.tensor_copy, 1, 0, PIECE)
         join(nc.scalar.copy, 3, 0, PIECE)
-        join(nc.scalar.copy, 2, PIECE // 2, PIECE)
         for piece in (0, 1, 3, 2):
             if piece == 3:
-                join(nc.vector.tensor_copy, 2, 0, PIECE // 2)
+                join(nc.vector.tensor_copy, 2, 0, PIECE)
             columns = slice(piece * PIECE, (piece + 1) * PIECE)
             quantize(y_codes[:, columns], y_scales[:, columns], y_grouped[piece][:], E4M3)
             if piece > 0:

@@ -29,6 +29,7 @@ GROUP = 128
 GROUPS = SLOTS // GROUP
 PIECE = 256
 PIECES = TOKENS // PIECE
+SECOND_SPLIT = 224
 
 FLOPS = 2 * 2 * D * K * SLOTS
 
@@ -207,7 +208,7 @@ def tile_attend_greft_pl_kernel(tc, dyT, R, W, ck, offs, out_0, out_1, out_2):
         quantize_w(1, 1, w_grouped[1])
         quantize_s(1)
         add_planes(1, 1, "bank3", 0, HALF)
-        scatter(1, 0, HALF)
+        scatter(1, 0, SECOND_SPLIT)
         quantize_w(2, 2, w_grouped[2])
         scale_u(2)
         scale_u(3)
@@ -223,7 +224,7 @@ def tile_attend_greft_pl_kernel(tc, dyT, R, W, ck, offs, out_0, out_1, out_2):
         scatter(0, GROUP, SLOTS)
         store_plane(0)
         nc.gpsimd.tensor_scalar(pairs[:, :, 0, :, 0], pieces[0], 1.0, -0.0, MULT, ADD)
-        scatter(1, HALF, SLOTS, on_vector=True)
+        scatter(1, SECOND_SPLIT, SLOTS, on_vector=True)
         store_plane(1)
         nc.gpsimd.tensor_scalar(pairs[:, :, 0, :, 1], pieces[1], 1.0, -0.0, MULT, ADD)
         nc.scalar.activation(out=window[last][:].indirect(offsets[:]), in_=new[:, last, :], func=COPY, scale=one[:])

from contextlib import ExitStack

import concourse.mybir as mybir
from concourse.masks import make_identity

F32 = mybir.dt.float32
BF16 = mybir.dt.bfloat16
I32 = mybir.dt.int32
U32 = mybir.dt.uint32
U16 = mybir.dt.uint16
U8 = mybir.dt.uint8
E4M3 = mybir.dt.float8_e4m3fn_x4
E5M2 = mybir.dt.float8_e5m2_x4
COPY = mybir.ActivationFunctionType.Copy
ADD = mybir.AluOpType.add
MULT = mybir.AluOpType.mult

P = 128
LANES = 4
D = 512
K = 512
SLOTS = 512
TOKENS = 1024
PER_COL = 16
HALF = SLOTS // 2
RUN = 8
LINE = 4
GROUP = 128
GROUPS = SLOTS // GROUP
PIECE = 256
PIECES = TOKENS // PIECE
SECOND_SPLIT = 224

FLOPS = 2 * 2 * D * K * SLOTS


def tile_attend_greft_pl_kernel(tc, dyT, R, W, ck, offs, out_0, out_1, out_2):
    nc = tc.nc
    with ExitStack() as ctx:
        keep = ctx.enter_context(tc.tile_pool(name="keep", bufs=1))
        psum = ctx.enter_context(tc.psum_pool(name="psum", bufs=1))

        dy_planes = dyT.rearrange("(p t) c -> p t c", t=LANES)
        out_planes = out_0.rearrange("(p t) c -> p t c", t=LANES)
        w_planes = W.rearrange("(m t) k -> m t k", t=LANES)
        last = LANES - 1

        offsets = keep.tile([P, SLOTS // PER_COL], U16, name="offsets")
        nc.sync.dma_start(offsets[:], offs)
        source = [keep.tile([P, TOKENS], F32, name="source%d" % t, tag="source%d" % t) for t in range(LANES)]
        for t in range(LANES):
            nc.sync.dma_start(source[t][:], dy_planes[:, t, :])
        r_raw = keep.tile([P, LANES, K], F32, name="r_raw")
        nc.sync.dma_start(r_raw[:], R.rearrange("(p j) k -> p j k", j=LANES))
        ck_line = keep.tile([1, K], F32, name="ck_line")
        nc.scalar.dma_start(ck_line[:], ck.rearrange("k o -> o k"))
        w_raw = [keep.tile([P, 2, K], F32, name="w_raw%d" % load) for load in range(2)]
        for load in range(2):
            nc.sync.dma_start(w_raw[load][:], w_planes[:, 2 * load:2 * load + 2, :])
        window = [keep.tile([P, TOKENS], F32, name="window%d" % t) for t in range(LANES)]
        nc.sync.dma_start(window[last][:], dy_planes[:, last, :])

        ident = keep.tile([P, P], F32, name="ident")
        make_identity(nc, ident[:])

        one = keep.tile([P, 1], F32, name="one")
        nc.vector.memset(one[:], 1.0)
        ck_dealt = keep.tile([P, K], F32, name="ck_dealt")
        nc.vector.memset(ck_dealt[:], 0.0)
        nc.gpsimd.tensor_scalar(ck_dealt[0:1, :].rearrange("o (t b i) -> o t b i", t=LANES, i=RUN),
                                ck_line[:].rearrange("o (b t i) -> o t b i", t=LANES, i=RUN), 1.0, 0.0, MULT, ADD)
        ck_bank = psum.tile([P, LANES, P], F32, name="ck_bank", tag="bank7")
        for t in range(LANES):
            nc.tensor.transpose(ck_bank[:, t, :], ck_dealt[:, t * P:(t + 1) * P], ident[:])

        def slot_offsets(a, b):
            return offsets[:, a // PER_COL:b // PER_COL]

        def weave(copy, lanes, planes):
            copy(out=lanes.rearrange("p (c i) t -> p c t i", i=LINE), in_=planes.rearrange("p t (c i) -> p c t i", i=LINE))

        def quantize(codes, scales, grouped, fmt):
            nc.vector.quantize_mx(out=codes.bitcast(fmt), scales=scales, in_=grouped.rearrange("p c t -> p (c t)"))

        def group(g):
            return slice(g * GROUP, (g + 1) * GROUP)

        w_codes = keep.tile([P, LANES, P], U32, name="w_codes", align_bytes=64)
        w_scales = keep.tile([P, LANES, P], U8, name="w_scales", align_bytes=64)

        def sort_w(t):
            words = keep.tile([P, K], BF16, name="w_sorted%d" % t, align_bytes=64)
            out = words[:].rearrange("m (pair b i e) -> m pair b e i", pair=2, i=RUN, e=2)
            raw = w_raw[t // 2][:, t % 2, :].rearrange("m (b pair e i) -> m pair b e i", pair=2, i=RUN, e=2)
            if t < last:
                nc.scalar.copy(out=out, in_=raw)
            else:
                for pair in range(2):
                    nc.gpsimd.tensor_scalar(out[:, pair], raw[:, pair], 1.0, -0.0, MULT, ADD)
            return words[:].bitcast(F32).rearrange("m (pair p) -> m pair p", pair=2)

        def turn_w(t, count, bank):
            turned = psum.tile([P, count, 2, P], F32, name="turned%d" % t, tag=bank)
            for n in range(count):
                for pair in range(2):
                    nc.tensor.transpose(turned[:, n, pair, :], w_words[t + n][:, pair, :], ident[:])
            grouped = keep.tile([P, count * P, LANES], BF16, name="w_grouped%d" % t, align_bytes=64)
            nc.scalar.copy(out=grouped[:].rearrange("p m t -> p (m t)").bitcast(F32).rearrange("p (n m pair) -> p n m pair", n=count, pair=2),
                           in_=turned[:].rearrange("p n pair m -> p n m pair"))
            return grouped

        def quantize_w(t, count, grouped):
            quantize(w_codes[:, t:t + count, :].rearrange("p n m -> p (n m)"), w_scales[:, t:t + count, :].rearrange("p n m -> p (n m)"),
                     grouped[:], E4M3)

        picked = keep.tile([P, LANES, SLOTS], F32, name="picked")
        dy_grouped = keep.tile([P, SLOTS, LANES], BF16, name="dy_grouped", align_bytes=64)
        dy_scales = keep.tile([P, SLOTS], U8, name="dy_scales", align_bytes=64)

        for t in range(last):
            nc.vector.tensor_copy(picked[:, t, :], source[t][:].indirect(offsets[:]))
            nc.scalar.activation(out=window[t][:], in_=source[t][:], func=COPY)
        for a in (0, GROUP):
            nc.vector.tensor_copy(picked[:, last, a:a + GROUP], source[last][:].indirect(slot_offsets(a, a + GROUP)))
        nc.scalar.activation(out=picked[:, last, HALF:SLOTS], in_=source[last][:].indirect(slot_offsets(HALF, SLOTS)), func=COPY)
        ck_sb = keep.tile([P, LANES], F32, name="ck_sb", tag="source%d" % last)
        nc.scalar.copy(out=ck_sb[:], in_=ck_bank[:, :, 0])
        ck_spread = ck_sb[:].rearrange("p (o t) -> p o t", o=1).to_broadcast([P, GROUP, LANES])

        for g in range(GROUPS):
            weave(nc.vector.tensor_copy if g < GROUPS // 2 else nc.scalar.copy, dy_grouped[:, group(g), :], picked[:, :, group(g)])
        dy_codes = [keep.tile([P, HALF], U32, name="dy_codes0", align_bytes=64)]
        for g in range(2):
            quantize(dy_codes[0][:, group(g)], dy_scales[:, group(g)], dy_grouped[:, group(g), :], E5M2)

        r_codes = keep.tile([P, LANES, P], U32, name="r_codes", align_bytes=64)
        r_scales = keep.tile([P, LANES, P], U8, name="r_scales", align_bytes=64)
        r_columns = r_raw[:].rearrange("p j (b t h i) -> p t b h j i", t=LANES, h=RUN // LINE, i=LINE)
        r_grouped = [keep.tile([P, 2, P, LANES], BF16, name="r_grouped%d" % n, tag="r_grouped%d" % n, align_bytes=64) for n in range(2)]
        blocks = P // RUN

        def deal_r(copy, t, a, b):
            copy(out=r_grouped[t // 2][:, t % 2].rearrange("p (b h i) j -> p b h j i", h=RUN // LINE, i=LINE)[:, a:b], in_=r_columns[:, t, a:b])

        deal_r(nc.vector.tensor_copy, 0, 0, blocks)
        deal_r(nc.vector.tensor_copy, 1, 0, blocks)
        deal_r(nc.vector.tensor_copy, 2, 0, blocks // 2)
        deal_r(nc.scalar.copy, 3, 0, blocks)
        deal_r(nc.scalar.copy, 2, blocks // 2, blocks)
        u_bank = {}

        def first_product(g):
            u_bank[g] = psum.tile([P, LANES, GROUP], F32, name="u_bank%d" % g, tag="bank%d" % (g if g < 3 else 1))
            for t in range(LANES):
                if g == 0 and t < 2:
                    quantize(r_codes[:, t, :], r_scales[:, t, :], r_grouped[0][:, t], E4M3)
                if g == 0 and t == 2:
                    quantize(r_codes[:, 2:4, :].rearrange("p n m -> p (n m)"), r_scales[:, 2:4, :].rearrange("p n m -> p (n m)"),
                             r_grouped[1][:].rearrange("p n m j -> p (n m) j"), E4M3)
                nc.tensor.matmul_mx(out=u_bank[g][:, t, :], lhsT=r_codes[:, t, :].bitcast(E4M3), lhsT_scale=r_scales[:, t, :],
                                    rhs=dy_codes[g // 2][:, group(g % 2)].bitcast(E5M2), rhs_scale=dy_scales[:, group(g)], start=True, stop=True)

        first_product(0)
        dy_codes.append(keep.tile([P, HALF], U32, name="dy_codes1", tag="r_grouped1", align_bytes=64))
        quantize(dy_codes[1][:], dy_scales[:, HALF:SLOTS], dy_grouped[:, HALF:SLOTS, :], E5M2)
        w_words = [sort_w(t) for t in range(LANES)]
        s_grouped = keep.tile([P, SLOTS, LANES], BF16, name="s_grouped", align_bytes=64)
        s_codes = keep.tile([P, SLOTS], U32, name="s_codes", align_bytes=64)
        s_scales = keep.tile([P, SLOTS], U8, name="s_scales", align_bytes=64)

        def scale_u(g):
            nc.vector.tensor_tensor(s_grouped[:, group(g), :], u_bank[g][:].rearrange("p t n -> p n t"), ck_spread, MULT)

        def quantize_s(g):
            quantize(s_codes[:, group(g)], s_scales[:, group(g)], s_grouped[:, group(g), :], E5M2)

        new = keep.tile([P, LANES, SLOTS], F32, name="new")

        def add_planes(first, count, bank, *cuts):
            a, b = cuts[0], cuts[-1]
            v_bank = psum.tile([P, count, b - a], F32, name="v_bank%d_%d" % (first, a), tag=bank)
            for n in range(count):
                for lo, hi in zip(cuts, cuts[1:]):
                    nc.tensor.matmul_mx(out=v_bank[:, n, lo - a:hi - a], lhsT=w_codes[:, first + n, :].bitcast(E4M3), lhsT_scale=w_scales[:, first + n, :],
                                        rhs=s_codes[:, lo:hi].bitcast(E5M2), rhs_scale=s_scales[:, lo:hi], start=True, stop=True)
            nc.vector.tensor_tensor(new[:, first:first + count, a:b], v_bank[:], picked[:, first:first + count, a:b], ADD)

        def scatter(t, a, b, on_vector=False):
            if on_vector:
                nc.vector.tensor_copy(window[t][:].indirect(slot_offsets(a, b)), new[:, t, a:b])
            else:
                nc.scalar.activation(out=window[t][:].indirect(slot_offsets(a, b)), in_=new[:, t, a:b], func=COPY)

        def store_plane(t):
            nc.sync.dma_start(out_planes[:, t, :], window[t][:])

        first_product(1)
        w_grouped = {0: turn_w(0, 1, "bank6"), 1: turn_w(1, 1, "bank7")}
        scale_u(0)
        quantize_w(0, 1, w_grouped[0])
        quantize_s(0)
        add_planes(0, 1, "bank4", 0, GROUP)
        first_product(2)
        w_grouped[2] = turn_w(2, 2, "bank5")
        first_product(3)
        scatter(0, 0, GROUP)
        scale_u(1)
        quantize_w(1, 1, w_grouped[1])
        quantize_s(1)
        add_planes(1, 1, "bank3", 0, HALF)
        scatter(1, 0, SECOND_SPLIT)
        quantize_w(2, 2, w_grouped[2])
        scale_u(2)
        scale_u(3)
        quantize(s_codes[:, HALF:SLOTS], s_scales[:, HALF:SLOTS], s_grouped[:, HALF:SLOTS, :], E5M2)
        add_planes(0, 1, "bank6", GROUP, HALF, SLOTS)
        add_planes(2, 2, "bank0", 0, HALF)
        add_planes(last, 1, "bank7", HALF, SLOTS)
        add_planes(1, 2, "bank4", HALF, SLOTS)

        pairs = keep.tile([P, PIECES, 2, PIECE, 2], BF16, name="pairs", align_bytes=64)
        pieces = [window[t][:].rearrange("p (piece c) -> p piece c", piece=PIECES) for t in range(LANES)]

        scatter(0, GROUP, SLOTS)
        store_plane(0)
        nc.gpsimd.tensor_scalar(pairs[:, :, 0, :, 0], pieces[0], 1.0, -0.0, MULT, ADD)
        scatter(1, SECOND_SPLIT, SLOTS, on_vector=True)
        store_plane(1)
        nc.gpsimd.tensor_scalar(pairs[:, :, 0, :, 1], pieces[1], 1.0, -0.0, MULT, ADD)
        nc.scalar.activation(out=window[last][:].indirect(offsets[:]), in_=new[:, last, :], func=COPY, scale=one[:])
        store_plane(last)
        scatter(2, 0, SLOTS, on_vector=True)
        store_plane(2)
        nc.vector.tensor_copy(out=pairs[:, 0:2, 1, :, 1], in_=pieces[last][:, 0:2])
        for piece in range(2):
            nc.vector.tensor_copy(out=pairs[:, piece, 1, :, 0], in_=pieces[2][:, piece])
        nc.scalar.copy(out=pairs[:, 2:4, 1, :, 1], in_=pieces[last][:, 2:4])
        for piece in (3, 2):
            nc.scalar.copy(out=pairs[:, piece, 1, :, 0], in_=pieces[2][:, piece])

        y_codes = keep.tile([P, TOKENS], U32, name="y_codes", align_bytes=64)
        y_scales = keep.tile([P, TOKENS], U8, name="y_scales", align_bytes=64)
        words_out = out_1[0].rearrange("p c l -> p (c l)").bitcast(I32)
        y_grouped = [keep.tile([P, PIECE, LANES], BF16, name="y_grouped%d" % piece, align_bytes=64) for piece in range(PIECES)]

        def join(copy, piece, a, b):
            joined = y_grouped[piece][:].rearrange("p c t -> p (c t)").bitcast(F32)
            apart = pairs[:, piece].rearrange("p pair c e -> p (pair c e)").bitcast(F32)
            copy(out=joined.rearrange("p (c i pair) -> p c pair i", i=LINE, pair=2)[:, a // LINE:b // LINE],
                 in_=apart.rearrange("p (pair c i) -> p c pair i", pair=2, i=LINE)[:, a // LINE:b // LINE])

        join(nc.vector.tensor_copy, 0, 0, PIECE)
        join(nc.vector.tensor_copy, 1, 0, PIECE)
        join(nc.scalar.copy, 3, 0, PIECE)
        for piece in (0, 1, 3, 2):
            if piece == 3:
                join(nc.vector.tensor_copy, 2, 0, PIECE)
            columns = slice(piece * PIECE, (piece + 1) * PIECE)
            quantize(y_codes[:, columns], y_scales[:, columns], y_grouped[piece][:], E4M3)
            if piece > 0:
                stored = slice(0, 2 * PIECE) if piece == 1 else columns
                nc.sync.dma_start(words_out[:, stored], y_codes[:, stored].bitcast(I32))
        for q in range(4):
            queue = nc.sync if q < 2 else nc.scalar
            queue.dma_start(out_2[0, 4 * q:4 * q + 4, :].bitcast(I32), y_scales[32 * q:32 * q + 4, :].bitcast(I32))
